import numpy as np
import ml_dtypes


def mxq(x, axis, fmt="e4m3"):
    dtype, down = {"e4m3": (ml_dtypes.float8_e4m3fn, 7), "e5m2": (ml_dtypes.float8_e5m2, 14)}[fmt]
    v = np.moveaxis(np.asarray(x, np.float32).astype(ml_dtypes.bfloat16).astype(np.float64), axis, -1)
    blocks = v.reshape(v.shape[:-1] + (-1, 32))
    amax = np.abs(blocks).max(-1, keepdims=True)
    byte = np.maximum(np.where(amax > 0, np.frexp(amax)[1] - 1 + 127, 0) - down, 1)
    scale = np.exp2(byte - 127.0)
    codes = (blocks / scale).astype(np.float32).astype(dtype).astype(np.float64)
    return np.moveaxis((codes * scale).reshape(v.shape), -1, axis)


WIDE = False


def mx_kscale(k):
    if not WIDE:
        return np.ones(k)
    levels = np.array([10, -10, 5, -5, 0])
    if k % 512:
        return np.exp2(np.random.permutation(np.resize(levels, k // 32))).repeat(32)
    a = np.empty((k // 512, 16))
    for p in range(k // 512):
        a[p, :8] = np.random.permutation(np.resize(levels, 8))
        for g in range(8):
            far = levels[np.abs(levels - a[p, g]) >= 10]
            a[p, g + 8] = far[np.random.randint(len(far))]
    return np.exp2(a.ravel()).repeat(32)


def f64(x):
    return np.asarray(x).astype(np.float64)


def striped(idx):
    return np.tile(np.asarray(idx).reshape(-1, 16).T, (8, 1)).astype(np.uint16)


def unstriped(offs):
    return offs[:16].T.reshape(-1).astype(np.int64)


B, N, T, D, DV, NQ = 1, 512, 1024, 512, 256, 256
NEW = 128


def setup_inputs():
    n = np.random.standard_normal
    idx = np.random.permutation(T)[:B * N]
    s = mx_kscale(D)[:, None]
    u = np.ones(T)
    u[idx] = mx_kscale(B * N)
    r = np.random.uniform(0.5, 2.0, T)
    k = n((D, T)) / s
    v = n((DV, T)) / (u * r)
    new = np.random.permutation(idx.reshape(B, N)[:, -NEW // B:].reshape(-1))
    return {
        "qT": (n((B, D, NQ)) * s * (0.80 / np.sqrt(D))).astype(np.float32),
        "kT": np.where(np.isin(np.arange(T), new)[None, :], n((D, T)), k).astype(np.float32),
        "vT": np.where(np.isin(np.arange(T), new)[None, :], n((DV, T)), v).astype(np.float32),
        "new_kT": k[:, new].astype(np.float32),
        "new_vT": v[:, new].astype(np.float32),
        "vs": np.tile(u * r, (128, 1)).astype(np.float32),
        "og": n((B, NQ, DV)).astype(np.float32),
        "offs": striped(idx),
        "slots": striped(new),
    }


def reference(qT, kT, vT, new_kT, new_vT, vs, og, offs, slots):
    idx = unstriped(offs)
    k = f64(kT)
    k[:, unstriped(slots)] = f64(new_kT)
    v = f64(vT)
    v[:, unstriped(slots)] = f64(new_vT)
    pick = lambda x: x[:, idx].reshape(x.shape[0], B, N).transpose(1, 0, 2)
    q = f64(qT)
    score = mxq(q, 1, "e4m3").transpose(0, 2, 1) @ mxq(pick(k), 1, "e4m3")
    m = score.max(-1, keepdims=True)
    p = np.exp(score - m)
    total = p.sum(-1, keepdims=True)
    w = p * pick(f64(vs))[:, :1, :]
    y = mxq(w, 2, "e4m3") @ mxq(pick(v).transpose(0, 2, 1), 1, "e4m3")
    y = y / total
    y = y / (1.0 + np.exp(-f64(og)))
    return y

@@ -1,0 +1,154 @@
+from contextlib import ExitStack
+
+import concourse.mybir as mybir
+from concourse.masks import make_identity
+
+F32 = mybir.dt.float32
+BF16 = mybir.dt.bfloat16
+U32 = mybir.dt.uint32
+U16 = mybir.dt.uint16
+U8 = mybir.dt.uint8
+FP8X4 = mybir.dt.float8_e4m3fn_x4
+ACT = mybir.ActivationFunctionType
+ALU = mybir.AluOpType
+AXX = mybir.AxisListType.X
+
+D, DV, T, N, NQ, NEW = 512, 256, 1024, 512, 256, 128
+P = 128
+PACK = 4
+QT = NQ // P
+ET = DV // P
+
+FLOPS = 2 * NQ * N * (D + DV)
+
+
+def tile_attend_x_append128_gate_topk_kernel(tc, qT, kT, vT, new_kT, new_vT, vs, og, offs, slots, out):
+    nc = tc.nc
+    with ExitStack() as ctx:
+        keep = ctx.enter_context(tc.tile_pool(name="keep", bufs=1))
+        psum = ctx.enter_context(tc.psum_pool(name="psum", bufs=1))
+        slots_t = keep.tile([P, NEW // 16], U16, name="slots_t")
+        offs_t = keep.tile([P, N // 16], U16, name="offs_t")
+        kp = [keep.tile([P, T], F32, name=f"kp{t}") for t in range(PACK)]
+        kb = [keep.tile([P, T], BF16, name=f"kb{t}") for t in range(PACK)]
+        vp = [keep.tile([P, T], F32, name=f"vp{h}") for h in range(ET)]
+        vb = [keep.tile([P, T], BF16, name=f"vb{h}") for h in range(ET)]
+        newk = keep.tile([P, PACK, NEW], F32, name="newk")
+        newka = keep.tile([P, 1, NEW], F32, name="newka")
+        newkb = keep.tile([P, 3, NEW], F32, name="newkb")
+        newv = keep.tile([P, ET, NEW], F32, name="newv")
+        qf = keep.tile([P, PACK, NQ], F32, name="qf")
+        vs_t = keep.tile([P, T], F32, name="vs_t")
+        og_t = keep.tile([P, QT, DV], F32, name="og_t")
+        ki = keep.tile([P, N, PACK], BF16, name="ki", align_bytes=64)
+        g2t = keep.tile([P, 2, N], F32, name="g2t")
+        qi = keep.tile([P, NQ, PACK], BF16, name="qi", align_bytes=64)
+        qc = keep.tile([P, NQ], U32, name="qc", align_bytes=64)
+        qs = keep.tile([P, NQ], U8, name="qs", align_bytes=64)
+        kc = keep.tile([P, N], U32, name="kc", align_bytes=64)
+        ks = keep.tile([P, N], U8, name="ks", align_bytes=64)
+        vg = [keep.tile([P, PACK, P], BF16, name=f"vg{h}") for h in range(ET)]
+        vsg = keep.tile([P, N], F32, name="vsg")
+        vsc = keep.tile([P, PACK], F32, name="vsc")
+        vi = keep.tile([P, DV, PACK], BF16, name="vi", align_bytes=64)
+        vc = keep.tile([P, DV], U32, name="vc", align_bytes=64)
+        vsx = keep.tile([P, DV], U8, name="vsx", align_bytes=64)
+        th = keep.tile([P, QT, DV], F32, name="th")
+        gate = keep.tile([P, QT, DV], F32, name="gate")
+        nm = [keep.tile([P, 1], F32, name=f"nm{a}") for a in range(QT)]
+        lt = keep.tile([P, QT], F32, name="lt")
+        rl = keep.tile([P, QT], F32, name="rl")
+        pt = [keep.tile([P, PACK, P], F32, name=f"pt{a}") for a in range(QT)]
+        wi = [keep.tile([P, P, PACK], BF16, name=f"wi{a}", align_bytes=64) for a in range(QT)]
+        wc = [keep.tile([P, P], U32, name=f"wc{a}", align_bytes=64) for a in range(QT)]
+        ws = [keep.tile([P, P], U8, name=f"ws{a}", align_bytes=64) for a in range(QT)]
+        res = [keep.tile([P, DV], F32, name=f"res{a}") for a in range(QT)]
+        s_ps = [psum.tile([P, N], F32, name=f"s_ps{a}") for a in range(QT)]
+        w_ps = [psum.tile([P, PACK, P], F32, name=f"w_ps{a}") for a in range(QT)]
+        y_ps = [psum.tile([P, DV], F32, name=f"y_ps{a}") for a in range(QT)]
+        vs_ps = psum.tile([P, PACK, P], F32, name="vs_ps")
+        v_ps = psum.tile([P, PACK, DV], BF16, name="v_ps")
+        kview = kT.rearrange("(p t) n -> p t n", t=PACK)
+        nkview = new_kT.rearrange("(p t) n -> p t n", t=PACK)
+        vview = vT.rearrange("(h p) n -> p h n", p=P)
+        oview = out[0].rearrange("(a p) e -> a p e", p=P)
+        nc.sync.dma_start(slots_t[:], slots)
+        nc.sync.dma_start(newka[:], nkview[:, 0:1, :])
+        nc.sync.dma_start(kp[0][:], kview[:, 0, :])
+        nc.sync.dma_start(newkb[:], nkview[:, 1:4, :])
+        nc.sync.dma_start(kp[1][:], kview[:, 1, :])
+        nc.sync.dma_start(kp[2][:], kview[:, 2, :])
+        nc.sync.dma_start(kp[3][:], kview[:, 3, :])
+        nc.sync.dma_start(offs_t[:], offs)
+        nc.sync.dma_start(newv[:], new_vT.rearrange("(h p) n -> p h n", p=P))
+        nc.sync.dma_start(qf[:], qT[0].rearrange("(p t) n -> p t n", t=PACK))
+        nc.sync.dma_start(vp[0][:], vview[:, 0, :])
+        nc.sync.dma_start(og_t[:], og[0].rearrange("(a p) e -> p a e", p=P))
+        nc.sync.dma_start(vs_t[:], vs)
+        nc.sync.dma_start(vp[1][:], vview[:, 1, :])
+        warm = keep.tile([P, 1], F32, name="warm")
+        nc.gpsimd.memset(warm[:], 0.0)
+        warm_out = keep.tile([P, 1], F32, name="warm_out")
+        nc.scalar.activation(warm_out[:], warm[:], ACT.Exp)
+        ident_f = keep.tile([P, P], F32, name="ident_f")
+        make_identity(nc, ident_f[:])
+        ident_b = keep.tile([P, P], BF16, name="ident_b")
+        make_identity(nc, ident_b[:])
+        nc.vector.tensor_copy(kp[0][:].indirect(slots_t[:]), newka[:, 0, :])
+        nc.vector.tensor_copy(kb[0][:], kp[0][:])
+        nc.vector.tensor_copy(kp[1][:].indirect(slots_t[:]), newkb[:, 0, :])
+        nc.vector.tensor_copy(kp[2][:].indirect(slots_t[:]), newkb[:, 1, :])
+        nc.vector.tensor_copy(vp[0][:].indirect(slots_t[:]), newv[:, 0, :])
+        nc.scalar.activation(ki[:, :, 0], kb[0][:].indirect(offs_t[:]), ACT.Copy)
+        nc.gpsimd.tensor_scalar(qi[:], qf[:].rearrange("p t n -> p n t"), 1.0, 0.0, ALU.mult, ALU.add)
+        nc.vector.tensor_copy(kp[3][:].indirect(slots_t[:]), newkb[:, 2, :])
+        nc.scalar.activation(kb[1][:], kp[1][:], ACT.Copy)
+        nc.vector.tensor_copy(ki[:, :, 2], kp[2][:].indirect(offs_t[:]))
+        nc.scalar.activation(ki[:, :, 1], kb[1][:].indirect(offs_t[:]), ACT.Copy)
+        nc.scalar.activation(vb[0][:], vp[0][:], ACT.Copy)
+        nc.scalar.activation(vg[0][:].rearrange("p t s -> p s t"), vb[0][:].indirect(offs_t[:]), ACT.Copy)
+        for t in range(PACK):
+            nc.tensor.transpose(v_ps[:, t, 0:128], vg[0][:, t, :], ident_b[:])
+        nc.vector.tensor_copy(ki[:, :, 3], kp[3][:].indirect(offs_t[:]))
+        nc.vector.quantize_mx(out=kc[:].bitcast(FP8X4), scales=ks[:], in_=ki[:].rearrange("p n t -> p (n t)"))
+        nc.vector.tensor_copy(vsg[:], vs_t[:].indirect(offs_t[:]))
+        for t in range(PACK):
+            nc.tensor.transpose(vs_ps[:, t, :], vsg[:].rearrange("p (s t) -> p t s", t=PACK)[:, t, :], ident_f[:])
+        nc.vector.quantize_mx(out=qc[:].bitcast(FP8X4), scales=qs[:], in_=qi[:].rearrange("p n t -> p (n t)"))
+        nc.scalar.copy(vsc[:], vs_ps[:, :, 0])
+        nc.scalar.activation(th[:], og_t[:], ACT.Tanh, scale=0.5)
+        nc.tensor.matmul_mx(s_ps[0][:], lhsT=qc[:, 0:128].bitcast(FP8X4), lhsT_scale=qs[:, 0:128], rhs=kc[:].bitcast(FP8X4), rhs_scale=ks[:], start=True, stop=True)
+        nc.gpsimd.tensor_scalar(gate[:], th[:], 0.5, 0.5, ALU.mult, ALU.add)
+        nc.scalar.copy(vi[:, 0:128, :], v_ps[:, :, 0:128].rearrange("s t e -> s e t"))
+        nc.tensor.matmul_mx(s_ps[1][:], lhsT=qc[:, 128:256].bitcast(FP8X4), lhsT_scale=qs[:, 128:256], rhs=kc[:].bitcast(FP8X4), rhs_scale=ks[:], start=True, stop=True)
+        nc.vector.tensor_reduce(nm[1][:], s_ps[1][:], axis=AXX, op=ALU.max, negate=True)
+        nc.vector.tensor_copy(vp[1][:].indirect(slots_t[:]), newv[:, 1, :])
+        nc.vector.tensor_copy(vg[1][:].rearrange("p t s -> p s t"), vp[1][:].indirect(offs_t[:]))
+        for t in range(PACK):
+            nc.tensor.transpose(v_ps[:, t, 128:256], vg[1][:, t, :], ident_b[:])
+        nc.vector.tensor_reduce(nm[0][:], s_ps[0][:], axis=AXX, op=ALU.max, negate=True)
+        nc.scalar.copy(vi[:, 128:256, :], v_ps[:, :, 128:256].rearrange("s t e -> s e t"))
+        nc.scalar.activation(pt[1][:], s_ps[1][:].rearrange("q (s t) -> q t s", t=PACK), ACT.Exp, bias=nm[1][:], scale=1.0, accum_out=lt[:, 1:2])
+        for t in range(PACK):
+            nc.tensor.transpose(w_ps[1][:, t, :], pt[1][:, t, :], ident_f[:])
+        nc.vector.tensor_tensor(wi[1][:], w_ps[1][:].rearrange("s t q -> s q t"), vsc[:].unsqueeze(1).to_broadcast([P, P, PACK]), ALU.mult)
+        nc.vector.quantize_mx(out=wc[1][:].bitcast(FP8X4), scales=ws[1][:], in_=wi[1][:].rearrange("p n t -> p (n t)"))
+        nc.scalar.activation(pt[0][:], s_ps[0][:].rearrange("q (s t) -> q t s", t=PACK), ACT.Exp, bias=nm[0][:], scale=1.0, accum_out=lt[:, 0:1])
+        nc.vector.reciprocal(rl[:], lt[:])
+        for t in range(PACK):
+            nc.tensor.transpose(w_ps[0][:, t, :], pt[0][:, t, :], ident_f[:])
+        nc.vector.tensor_tensor(wi[0][:], w_ps[0][:].rearrange("s t q -> s q t"), vsc[:].unsqueeze(1).to_broadcast([P, P, PACK]), ALU.mult)
+        nc.vector.quantize_mx(out=vc[:].bitcast(FP8X4), scales=vsx[:], in_=vi[:].rearrange("p n t -> p (n t)"))
+        for j in range(8):
+            nc.tensor.transpose(y_ps[1][:, :P], kp[3][:, j * P : (j + 1) * P], ident_f[:])
+        for j in range(8):
+            nc.tensor.transpose(y_ps[1][:].bitcast(BF16)[:, :P], qi[:].rearrange("p n t -> p (n t)")[:, j * P : (j + 1) * P], ident_b[:])
+        for j in range(8):
+            nc.tensor.transpose(y_ps[1][:, :P], vp[0][:, j * P : (j + 1) * P], ident_f[:])
+        nc.tensor.matmul_mx(y_ps[1][:], lhsT=wc[1][:].bitcast(FP8X4), lhsT_scale=ws[1][:], rhs=vc[:].bitcast(FP8X4), rhs_scale=vsx[:], start=True, stop=True)
+        nc.vector.quantize_mx(out=wc[0][:].bitcast(FP8X4), scales=ws[0][:], in_=wi[0][:].rearrange("p n t -> p (n t)"))
+        nc.tensor.matmul_mx(y_ps[0][:], lhsT=wc[0][:].bitcast(FP8X4), lhsT_scale=ws[0][:], rhs=vc[:].bitcast(FP8X4), rhs_scale=vsx[:], start=True, stop=True)
+        nc.vector.scalar_tensor_tensor(res[1][:], y_ps[1][:], rl[:, 1:2], gate[:, 1, :], ALU.mult, ALU.mult)
+        nc.sync.dma_start(oview[1], res[1][:])
+        nc.vector.scalar_tensor_tensor(res[0][:], y_ps[0][:], rl[:, 0:1], gate[:, 0, :], ALU.mult, ALU.mult)
+        nc.sync.dma_start(oview[0], res[0][:])

@@ -33,29 +33,26 @@ def tile_attend_x_append128_gate_topk_kernel(tc, qT, kT, vT, new_kT, new_vT, vs,
         kb = [keep.tile([P, T], BF16, name=f"kb{t}") for t in range(PACK)]
         vp = [keep.tile([P, T], F32, name=f"vp{h}") for h in range(ET)]
         vb = [keep.tile([P, T], BF16, name=f"vb{h}") for h in range(ET)]
-        newk = keep.tile([P, PACK, NEW], F32, name="newk")
-        newka = keep.tile([P, 1, NEW], F32, name="newka")
-        newkb = keep.tile([P, 3, NEW], F32, name="newkb")
+        newk0 = keep.tile([P, NEW], F32, name="newk0")
+        newk = keep.tile([P, PACK - 1, NEW], F32, name="newk")
         newv = keep.tile([P, ET, NEW], F32, name="newv")
         qf = keep.tile([P, PACK, NQ], F32, name="qf")
         vs_t = keep.tile([P, T], F32, name="vs_t")
         og_t = keep.tile([P, QT, DV], F32, name="og_t")
         ki = keep.tile([P, N, PACK], BF16, name="ki", align_bytes=64)
-        g2t = keep.tile([P, 2, N], F32, name="g2t")
         qi = keep.tile([P, NQ, PACK], BF16, name="qi", align_bytes=64)
-        qc = keep.tile([P, NQ], U32, name="qc", align_bytes=64)
+        qc = keep.tile([P, NQ], U32, name="qc", tag="qc", align_bytes=64)
         qs = keep.tile([P, NQ], U8, name="qs", align_bytes=64)
         kc = keep.tile([P, N], U32, name="kc", align_bytes=64)
         ks = keep.tile([P, N], U8, name="ks", align_bytes=64)
-        vg = [keep.tile([P, PACK, P], BF16, name=f"vg{h}") for h in range(ET)]
+        vg = [keep.tile([P, N], BF16, name="vg0")]
         vsg = keep.tile([P, N], F32, name="vsg")
         vsc = keep.tile([P, PACK], F32, name="vsc")
         vi = keep.tile([P, DV, PACK], BF16, name="vi", align_bytes=64)
         vc = keep.tile([P, DV], U32, name="vc", align_bytes=64)
         vsx = keep.tile([P, DV], U8, name="vsx", align_bytes=64)
-        th = keep.tile([P, QT, DV], F32, name="th")
         gate = keep.tile([P, QT, DV], F32, name="gate")
-        nm = [keep.tile([P, 1], F32, name=f"nm{a}") for a in range(QT)]
+        nm = [keep.tile([P, 1], F32, name=f"nm{a}", tag=f"nm{a}") for a in range(QT)]
         lt = keep.tile([P, QT], F32, name="lt")
         rl = keep.tile([P, QT], F32, name="rl")
         pt = [keep.tile([P, PACK, P], F32, name=f"pt{a}") for a in range(QT)]
@@ -63,92 +60,87 @@ def tile_attend_x_append128_gate_topk_kernel(tc, qT, kT, vT, new_kT, new_vT, vs,
         wc = [keep.tile([P, P], U32, name=f"wc{a}", align_bytes=64) for a in range(QT)]
         ws = [keep.tile([P, P], U8, name=f"ws{a}", align_bytes=64) for a in range(QT)]
         res = [keep.tile([P, DV], F32, name=f"res{a}") for a in range(QT)]
-        s_ps = [psum.tile([P, N], F32, name=f"s_ps{a}") for a in range(QT)]
+        warm = keep.tile([P, 1], F32, name="warm")
+        warm_out = keep.tile([P, 1], F32, name="warm_out")
+        ident_f = keep.tile([P, P], F32, name="ident_f")
+        s_ps = [psum.tile([P, N], F32, name=f"s_ps{a}", tag=f"s_ps{a}") for a in range(QT)]
         w_ps = [psum.tile([P, PACK, P], F32, name=f"w_ps{a}") for a in range(QT)]
         y_ps = [psum.tile([P, DV], F32, name=f"y_ps{a}") for a in range(QT)]
         vs_ps = psum.tile([P, PACK, P], F32, name="vs_ps")
-        v_ps = psum.tile([P, PACK, DV], BF16, name="v_ps")
         kview = kT.rearrange("(p t) n -> p t n", t=PACK)
         nkview = new_kT.rearrange("(p t) n -> p t n", t=PACK)
         vview = vT.rearrange("(h p) n -> p h n", p=P)
         oview = out[0].rearrange("(a p) e -> a p e", p=P)
+        nc.sync.dma_start(offs_t[:], offs)
+        nc.sync.dma_start(vs_t[0:32, :], vs[0:32, :])
+        nc.vector.memset(vs_t[32:64, :], 0.0)
+        nc.gpsimd.memset(vs_t[64:128, :], 0.0)
         nc.sync.dma_start(slots_t[:], slots)
-        nc.sync.dma_start(newka[:], nkview[:, 0:1, :])
+        nc.sync.dma_start(newk0[:], nkview[:, 0, :])
         nc.sync.dma_start(kp[0][:], kview[:, 0, :])
-        nc.sync.dma_start(newkb[:], nkview[:, 1:4, :])
+        nc.sync.dma_start(newk[:], nkview[:, 1:PACK, :])
         nc.sync.dma_start(kp[1][:], kview[:, 1, :])
         nc.sync.dma_start(kp[2][:], kview[:, 2, :])
-        nc.sync.dma_start(kp[3][:], kview[:, 3, :])
-        nc.sync.dma_start(offs_t[:], offs)
         nc.sync.dma_start(newv[:], new_vT.rearrange("(h p) n -> p h n", p=P))
-        nc.sync.dma_start(qf[:], qT[0].rearrange("(p t) n -> p t n", t=PACK))
         nc.sync.dma_start(vp[0][:], vview[:, 0, :])
+        nc.sync.dma_start(qf[:], qT[0].rearrange("(p t) n -> p t n", t=PACK))
+        nc.sync.dma_start(kp[3][:], kview[:, 3, :])
         nc.sync.dma_start(og_t[:], og[0].rearrange("(a p) e -> p a e", p=P))
-        nc.sync.dma_start(vs_t[:], vs)
         nc.sync.dma_start(vp[1][:], vview[:, 1, :])
-        warm = keep.tile([P, 1], F32, name="warm")
         nc.gpsimd.memset(warm[:], 0.0)
-        warm_out = keep.tile([P, 1], F32, name="warm_out")
         nc.scalar.activation(warm_out[:], warm[:], ACT.Exp)
-        ident_f = keep.tile([P, P], F32, name="ident_f")
         make_identity(nc, ident_f[:])
-        ident_b = keep.tile([P, P], BF16, name="ident_b")
-        make_identity(nc, ident_b[:])
-        nc.vector.tensor_copy(kp[0][:].indirect(slots_t[:]), newka[:, 0, :])
-        nc.vector.tensor_copy(kb[0][:], kp[0][:])
-        nc.vector.tensor_copy(kp[1][:].indirect(slots_t[:]), newkb[:, 0, :])
-        nc.vector.tensor_copy(kp[2][:].indirect(slots_t[:]), newkb[:, 1, :])
-        nc.vector.tensor_copy(vp[0][:].indirect(slots_t[:]), newv[:, 0, :])
-        nc.scalar.activation(ki[:, :, 0], kb[0][:].indirect(offs_t[:]), ACT.Copy)
-        nc.gpsimd.tensor_scalar(qi[:], qf[:].rearrange("p t n -> p n t"), 1.0, 0.0, ALU.mult, ALU.add)
-        nc.vector.tensor_copy(kp[3][:].indirect(slots_t[:]), newkb[:, 2, :])
-        nc.scalar.activation(kb[1][:], kp[1][:], ACT.Copy)
-        nc.vector.tensor_copy(ki[:, :, 2], kp[2][:].indirect(offs_t[:]))
-        nc.scalar.activation(ki[:, :, 1], kb[1][:].indirect(offs_t[:]), ACT.Copy)
-        nc.scalar.activation(vb[0][:], vp[0][:], ACT.Copy)
-        nc.scalar.activation(vg[0][:].rearrange("p t s -> p s t"), vb[0][:].indirect(offs_t[:]), ACT.Copy)
-        for t in range(PACK):
-            nc.tensor.transpose(v_ps[:, t, 0:128], vg[0][:, t, :], ident_b[:])
-        nc.vector.tensor_copy(ki[:, :, 3], kp[3][:].indirect(offs_t[:]))
-        nc.vector.quantize_mx(out=kc[:].bitcast(FP8X4), scales=ks[:], in_=ki[:].rearrange("p n t -> p (n t)"))
         nc.vector.tensor_copy(vsg[:], vs_t[:].indirect(offs_t[:]))
         for t in range(PACK):
             nc.tensor.transpose(vs_ps[:, t, :], vsg[:].rearrange("p (s t) -> p t s", t=PACK)[:, t, :], ident_f[:])
-        nc.vector.quantize_mx(out=qc[:].bitcast(FP8X4), scales=qs[:], in_=qi[:].rearrange("p n t -> p (n t)"))
         nc.scalar.copy(vsc[:], vs_ps[:, :, 0])
-        nc.scalar.activation(th[:], og_t[:], ACT.Tanh, scale=0.5)
+        nc.vector.tensor_copy(kp[0][:].indirect(slots_t[:]), newk0[:])
+        nc.scalar.activation(kb[0][:], kp[0][:], ACT.Copy)
+        nc.scalar.activation(ki[:, :, 0], kb[0][:].indirect(offs_t[:]), ACT.Copy)
+        nc.vector.tensor_copy(kp[1][:].indirect(slots_t[:]), newk[:, 0, :])
+        nc.scalar.activation(kb[1][:], kp[1][:], ACT.Copy)
+        nc.scalar.activation(ki[:, :, 1], kb[1][:].indirect(offs_t[:]), ACT.Copy)
+        nc.vector.tensor_copy(kp[2][:].indirect(slots_t[:]), newk[:, 1, :])
+        nc.vector.tensor_copy(ki[:, :, 2], kp[2][:].indirect(offs_t[:]))
+        nc.vector.tensor_copy(vp[0][:].indirect(slots_t[:]), newv[:, 0, :])
+        nc.scalar.activation(vb[0][:], vp[0][:], ACT.Copy)
+        nc.scalar.activation(vg[0][:], vb[0][:].indirect(offs_t[:]), ACT.Copy)
+        nc.gpsimd.tensor_scalar(qi[:], qf[:].rearrange("p t n -> p n t"), 1.0, 0.0, ALU.mult, ALU.add)
+        nc.vector.tensor_copy(kp[3][:].indirect(slots_t[:]), newk[:, 2, :])
+        nc.vector.tensor_copy(ki[:, :, 3], kp[3][:].indirect(offs_t[:]))
+        nc.vector.quantize_mx(out=qc[:].bitcast(FP8X4), scales=qs[:], in_=qi[:].rearrange("p n t -> p (n t)"))
+        nc.vector.quantize_mx(out=kc[:].bitcast(FP8X4), scales=ks[:], in_=ki[:].rearrange("p n t -> p (n t)"))
         nc.tensor.matmul_mx(s_ps[0][:], lhsT=qc[:, 0:128].bitcast(FP8X4), lhsT_scale=qs[:, 0:128], rhs=kc[:].bitcast(FP8X4), rhs_scale=ks[:], start=True, stop=True)
-        nc.gpsimd.tensor_scalar(gate[:], th[:], 0.5, 0.5, ALU.mult, ALU.add)
-        nc.scalar.copy(vi[:, 0:128, :], v_ps[:, :, 0:128].rearrange("s t e -> s e t"))
         nc.tensor.matmul_mx(s_ps[1][:], lhsT=qc[:, 128:256].bitcast(FP8X4), lhsT_scale=qs[:, 128:256], rhs=kc[:].bitcast(FP8X4), rhs_scale=ks[:], start=True, stop=True)
-        nc.vector.tensor_reduce(nm[1][:], s_ps[1][:], axis=AXX, op=ALU.max, negate=True)
-        nc.vector.tensor_copy(vp[1][:].indirect(slots_t[:]), newv[:, 1, :])
-        nc.vector.tensor_copy(vg[1][:].rearrange("p t s -> p s t"), vp[1][:].indirect(offs_t[:]))
-        for t in range(PACK):
-            nc.tensor.transpose(v_ps[:, t, 128:256], vg[1][:, t, :], ident_b[:])
         nc.vector.tensor_reduce(nm[0][:], s_ps[0][:], axis=AXX, op=ALU.max, negate=True)
-        nc.scalar.copy(vi[:, 128:256, :], v_ps[:, :, 128:256].rearrange("s t e -> s e t"))
+        nc.scalar.activation(pt[0][:], s_ps[0][:].rearrange("q (s t) -> q t s", t=PACK), ACT.Exp, bias=nm[0][:], scale=1.0, accum_out=lt[:, 0:1])
+        for t in range(PACK):
+            nc.tensor.transpose(w_ps[0][:, t, :], pt[0][:, t, :], ident_f[:])
+        nc.vector.tensor_reduce(nm[1][:], s_ps[1][:], axis=AXX, op=ALU.max, negate=True)
         nc.scalar.activation(pt[1][:], s_ps[1][:].rearrange("q (s t) -> q t s", t=PACK), ACT.Exp, bias=nm[1][:], scale=1.0, accum_out=lt[:, 1:2])
         for t in range(PACK):
             nc.tensor.transpose(w_ps[1][:, t, :], pt[1][:, t, :], ident_f[:])
-        nc.vector.tensor_tensor(wi[1][:], w_ps[1][:].rearrange("s t q -> s q t"), vsc[:].unsqueeze(1).to_broadcast([P, P, PACK]), ALU.mult)
-        nc.vector.quantize_mx(out=wc[1][:].bitcast(FP8X4), scales=ws[1][:], in_=wi[1][:].rearrange("p n t -> p (n t)"))
-        nc.scalar.activation(pt[0][:], s_ps[0][:].rearrange("q (s t) -> q t s", t=PACK), ACT.Exp, bias=nm[0][:], scale=1.0, accum_out=lt[:, 0:1])
+        nc.vector.tensor_copy(vp[1][:].indirect(slots_t[:]), newv[:, 1, :])
+        vg.append(keep.tile([P, N], BF16, name="vg1", tag="qc", align_bytes=64))
+        nc.vector.tensor_copy(vg[1][:], vp[1][:].indirect(offs_t[:]))
+        v_ps = psum.tile([P, ET, 2, P], F32, name="v_ps", tag="s_ps0")
+        for u in range(2):
+            nc.tensor.transpose(v_ps[:, 0, u, :], vg[0][:].bitcast(F32)[:, u : N // 2 : 2], ident_f[:])
+        for u in range(2):
+            nc.tensor.transpose(v_ps[:, 1, u, :], vg[1][:].bitcast(F32)[:, u : N // 2 : 2], ident_f[:])
+        nc.scalar.copy(vi[:].rearrange("p n t -> p (n t)").bitcast(F32).rearrange("s (h e u) -> s h e u", h=ET, u=2), v_ps[:].rearrange("s h u e -> s h e u"))
+        th = keep.tile([P, QT, DV], F32, name="th", tag="nm1")
+        nc.scalar.activation(th[:], og_t[:], ACT.Tanh, scale=0.5)
+        nc.gpsimd.tensor_scalar(gate[:], th[:], 0.5, 0.5, ALU.mult, ALU.add)
         nc.vector.reciprocal(rl[:], lt[:])
-        for t in range(PACK):
-            nc.tensor.transpose(w_ps[0][:, t, :], pt[0][:, t, :], ident_f[:])
         nc.vector.tensor_tensor(wi[0][:], w_ps[0][:].rearrange("s t q -> s q t"), vsc[:].unsqueeze(1).to_broadcast([P, P, PACK]), ALU.mult)
-        nc.vector.quantize_mx(out=vc[:].bitcast(FP8X4), scales=vsx[:], in_=vi[:].rearrange("p n t -> p (n t)"))
-        for j in range(8):
-            nc.tensor.transpose(y_ps[1][:, :P], kp[3][:, j * P : (j + 1) * P], ident_f[:])
-        for j in range(8):
-            nc.tensor.transpose(y_ps[1][:].bitcast(BF16)[:, :P], qi[:].rearrange("p n t -> p (n t)")[:, j * P : (j + 1) * P], ident_b[:])
-        for j in range(8):
-            nc.tensor.transpose(y_ps[1][:, :P], vp[0][:, j * P : (j + 1) * P], ident_f[:])
-        nc.tensor.matmul_mx(y_ps[1][:], lhsT=wc[1][:].bitcast(FP8X4), lhsT_scale=ws[1][:], rhs=vc[:].bitcast(FP8X4), rhs_scale=vsx[:], start=True, stop=True)
+        nc.vector.tensor_tensor(wi[1][:], w_ps[1][:].rearrange("s t q -> s q t"), vsc[:].unsqueeze(1).to_broadcast([P, P, PACK]), ALU.mult)
         nc.vector.quantize_mx(out=wc[0][:].bitcast(FP8X4), scales=ws[0][:], in_=wi[0][:].rearrange("p n t -> p (n t)"))
+        nc.vector.quantize_mx(out=vc[:].bitcast(FP8X4), scales=vsx[:], in_=vi[:].rearrange("p n t -> p (n t)"))
+        nc.vector.quantize_mx(out=wc[1][:].bitcast(FP8X4), scales=ws[1][:], in_=wi[1][:].rearrange("p n t -> p (n t)"))
         nc.tensor.matmul_mx(y_ps[0][:], lhsT=wc[0][:].bitcast(FP8X4), lhsT_scale=ws[0][:], rhs=vc[:].bitcast(FP8X4), rhs_scale=vsx[:], start=True, stop=True)
-        nc.vector.scalar_tensor_tensor(res[1][:], y_ps[1][:], rl[:, 1:2], gate[:, 1, :], ALU.mult, ALU.mult)
-        nc.sync.dma_start(oview[1], res[1][:])
+        nc.tensor.matmul_mx(y_ps[1][:], lhsT=wc[1][:].bitcast(FP8X4), lhsT_scale=ws[1][:], rhs=vc[:].bitcast(FP8X4), rhs_scale=vsx[:], start=True, stop=True)
         nc.vector.scalar_tensor_tensor(res[0][:], y_ps[0][:], rl[:, 0:1], gate[:, 0, :], ALU.mult, ALU.mult)
         nc.sync.dma_start(oview[0], res[0][:])
+        nc.vector.scalar_tensor_tensor(res[1][:], y_ps[1][:], rl[:, 1:2], gate[:, 1, :], ALU.mult, ALU.mult)
+        nc.sync.dma_start(oview[1], res[1][:])

@@ -26,6 +26,7 @@ def tile_attend_x_append128_gate_topk_kernel(tc, qT, kT, vT, new_kT, new_vT, vs,
     nc = tc.nc
     with ExitStack() as ctx:
         keep = ctx.enter_context(tc.tile_pool(name="keep", bufs=1))
+        share = ctx.enter_context(tc.tile_pool(name="share", bufs=1))
         psum = ctx.enter_context(tc.psum_pool(name="psum", bufs=1))
         slots_t = keep.tile([P, NEW // 16], U16, name="slots_t")
         offs_t = keep.tile([P, N // 16], U16, name="offs_t")
@@ -40,19 +41,19 @@ def tile_attend_x_append128_gate_topk_kernel(tc, qT, kT, vT, new_kT, new_vT, vs,
         vs_t = keep.tile([P, T], F32, name="vs_t")
         og_t = keep.tile([P, QT, DV], F32, name="og_t")
         ki = keep.tile([P, N, PACK], BF16, name="ki", align_bytes=64)
-        qi = keep.tile([P, NQ, PACK], BF16, name="qi", align_bytes=64)
+        qi = share.tile([P, NQ, PACK], BF16, name="qi", align_bytes=64, offset=0)
         qc = keep.tile([P, NQ], U32, name="qc", tag="qc", align_bytes=64)
         qs = keep.tile([P, NQ], U8, name="qs", align_bytes=64)
         kc = keep.tile([P, N], U32, name="kc", align_bytes=64)
-        ks = keep.tile([P, N], U8, name="ks", align_bytes=64)
-        vg = [keep.tile([P, N], BF16, name="vg0")]
+        vg = []
+        v_ps = []
         vsg = keep.tile([P, N], F32, name="vsg")
         vsc = keep.tile([P, PACK], F32, name="vsc")
-        vi = keep.tile([P, DV, PACK], BF16, name="vi", align_bytes=64)
         vc = keep.tile([P, DV], U32, name="vc", align_bytes=64)
         vsx = keep.tile([P, DV], U8, name="vsx", align_bytes=64)
+        th = keep.tile([P, QT, DV], F32, name="th")
         gate = keep.tile([P, QT, DV], F32, name="gate")
-        nm = [keep.tile([P, 1], F32, name=f"nm{a}", tag=f"nm{a}") for a in range(QT)]
+        nm = [keep.tile([P, 1], F32, name=f"nm{a}", tag=f"nm{a}", align_bytes=64) for a in range(QT)]
         lt = keep.tile([P, QT], F32, name="lt")
         rl = keep.tile([P, QT], F32, name="rl")
         pt = [keep.tile([P, PACK, P], F32, name=f"pt{a}") for a in range(QT)]
@@ -83,8 +84,8 @@ def tile_attend_x_append128_gate_topk_kernel(tc, qT, kT, vT, new_kT, new_vT, vs,
         nc.sync.dma_start(kp[2][:], kview[:, 2, :])
         nc.sync.dma_start(newv[:], new_vT.rearrange("(h p) n -> p h n", p=P))
         nc.sync.dma_start(vp[0][:], vview[:, 0, :])
-        nc.sync.dma_start(qf[:], qT[0].rearrange("(p t) n -> p t n", t=PACK))
         nc.sync.dma_start(kp[3][:], kview[:, 3, :])
+        nc.sync.dma_start(qf[:], qT[0].rearrange("(p t) n -> p t n", t=PACK))
         nc.sync.dma_start(og_t[:], og[0].rearrange("(a p) e -> p a e", p=P))
         nc.sync.dma_start(vp[1][:], vview[:, 1, :])
         nc.gpsimd.memset(warm[:], 0.0)
@@ -104,14 +105,21 @@ def tile_attend_x_append128_gate_topk_kernel(tc, qT, kT, vT, new_kT, new_vT, vs,
         nc.vector.tensor_copy(ki[:, :, 2], kp[2][:].indirect(offs_t[:]))
         nc.vector.tensor_copy(vp[0][:].indirect(slots_t[:]), newv[:, 0, :])
         nc.scalar.activation(vb[0][:], vp[0][:], ACT.Copy)
-        nc.scalar.activation(vg[0][:], vb[0][:].indirect(offs_t[:]), ACT.Copy)
         nc.gpsimd.tensor_scalar(qi[:], qf[:].rearrange("p t n -> p n t"), 1.0, 0.0, ALU.mult, ALU.add)
         nc.vector.tensor_copy(kp[3][:].indirect(slots_t[:]), newk[:, 2, :])
         nc.vector.tensor_copy(ki[:, :, 3], kp[3][:].indirect(offs_t[:]))
         nc.vector.quantize_mx(out=qc[:].bitcast(FP8X4), scales=qs[:], in_=qi[:].rearrange("p n t -> p (n t)"))
+        vg.append(share.tile([P, N], BF16, name="vg0", align_bytes=64, offset=1024))
+        nc.scalar.activation(vg[0][:], vb[0][:].indirect(offs_t[:]), ACT.Copy)
+        nc.scalar.activation(th[:], og_t[:], ACT.Tanh, scale=0.5)
+        nc.gpsimd.tensor_scalar(gate[:], th[:], 0.5, 0.5, ALU.mult, ALU.add)
+        ks = share.tile([P, N], U8, name="ks", align_bytes=64, offset=0)
         nc.vector.quantize_mx(out=kc[:].bitcast(FP8X4), scales=ks[:], in_=ki[:].rearrange("p n t -> p (n t)"))
         nc.tensor.matmul_mx(s_ps[0][:], lhsT=qc[:, 0:128].bitcast(FP8X4), lhsT_scale=qs[:, 0:128], rhs=kc[:].bitcast(FP8X4), rhs_scale=ks[:], start=True, stop=True)
         nc.tensor.matmul_mx(s_ps[1][:], lhsT=qc[:, 128:256].bitcast(FP8X4), lhsT_scale=qs[:, 128:256], rhs=kc[:].bitcast(FP8X4), rhs_scale=ks[:], start=True, stop=True)
+        v_ps.append(psum.tile([P, 2, P], F32, name="v_ps0", tag="v_ps0"))
+        for u in range(2):
+            nc.tensor.transpose(v_ps[0][:, u, :], vg[0][:].bitcast(F32)[:, u : N // 2 : 2], ident_f[:])
         nc.vector.tensor_reduce(nm[0][:], s_ps[0][:], axis=AXX, op=ALU.max, negate=True)
         nc.scalar.activation(pt[0][:], s_ps[0][:].rearrange("q (s t) -> q t s", t=PACK), ACT.Exp, bias=nm[0][:], scale=1.0, accum_out=lt[:, 0:1])
         for t in range(PACK):
@@ -123,15 +131,12 @@ def tile_attend_x_append128_gate_topk_kernel(tc, qT, kT, vT, new_kT, new_vT, vs,
         nc.vector.tensor_copy(vp[1][:].indirect(slots_t[:]), newv[:, 1, :])
         vg.append(keep.tile([P, N], BF16, name="vg1", tag="qc", align_bytes=64))
         nc.vector.tensor_copy(vg[1][:], vp[1][:].indirect(offs_t[:]))
-        v_ps = psum.tile([P, ET, 2, P], F32, name="v_ps", tag="s_ps0")
+        v_ps.append(psum.tile([P, 2, P], F32, name="v_ps1", tag="s_ps1"))
         for u in range(2):
-            nc.tensor.transpose(v_ps[:, 0, u, :], vg[0][:].bitcast(F32)[:, u : N // 2 : 2], ident_f[:])
-        for u in range(2):
-            nc.tensor.transpose(v_ps[:, 1, u, :], vg[1][:].bitcast(F32)[:, u : N // 2 : 2], ident_f[:])
-        nc.scalar.copy(vi[:].rearrange("p n t -> p (n t)").bitcast(F32).rearrange("s (h e u) -> s h e u", h=ET, u=2), v_ps[:].rearrange("s h u e -> s h e u"))
-        th = keep.tile([P, QT, DV], F32, name="th", tag="nm1")
-        nc.scalar.activation(th[:], og_t[:], ACT.Tanh, scale=0.5)
-        nc.gpsimd.tensor_scalar(gate[:], th[:], 0.5, 0.5, ALU.mult, ALU.add)
+            nc.tensor.transpose(v_ps[1][:, u, :], vg[1][:].bitcast(F32)[:, u : N // 2 : 2], ident_f[:])
+        vi = keep.tile([P, DV, PACK], BF16, name="vi", tag="nm1", align_bytes=64)
+        nc.scalar.copy(vi[:, 0:128, :].rearrange("p n t -> p (n t)").bitcast(F32).rearrange("s (e u) -> s e u", u=2), v_ps[0][:].rearrange("s u e -> s e u"))
+        nc.scalar.copy(vi[:, 128:256, :].rearrange("p n t -> p (n t)").bitcast(F32).rearrange("s (e u) -> s e u", u=2), v_ps[1][:].rearrange("s u e -> s e u"))
         nc.vector.reciprocal(rl[:], lt[:])
         nc.vector.tensor_tensor(wi[0][:], w_ps[0][:].rearrange("s t q -> s q t"), vsc[:].unsqueeze(1).to_broadcast([P, P, PACK]), ALU.mult)
         nc.vector.tensor_tensor(wi[1][:], w_ps[1][:].rearrange("s t q -> s q t"), vsc[:].unsqueeze(1).to_broadcast([P, P, PACK]), ALU.mult)

@@ -30,7 +30,7 @@ def tile_attend_x_append128_gate_topk_kernel(tc, qT, kT, vT, new_kT, new_vT, vs,
         psum = ctx.enter_context(tc.psum_pool(name="psum", bufs=1))
         slots_t = keep.tile([P, NEW // 16], U16, name="slots_t")
         offs_t = keep.tile([P, N // 16], U16, name="offs_t")
-        kp = [keep.tile([P, T], F32, name=f"kp{t}") for t in range(PACK)]
+        kp = [keep.tile([P, T], F32, name=f"kp{t}", tag=f"kp{t}") for t in range(PACK)]
         kb = [keep.tile([P, T], BF16, name=f"kb{t}") for t in range(PACK)]
         vp = [keep.tile([P, T], F32, name=f"vp{h}") for h in range(ET)]
         vb = [keep.tile([P, T], BF16, name=f"vb{h}") for h in range(ET)]
@@ -48,7 +48,6 @@ def tile_attend_x_append128_gate_topk_kernel(tc, qT, kT, vT, new_kT, new_vT, vs,
         vg = []
         v_ps = []
         vsg = keep.tile([P, N], F32, name="vsg")
-        vsc = keep.tile([P, PACK], F32, name="vsc")
         vc = keep.tile([P, DV], U32, name="vc", align_bytes=64)
         vsx = keep.tile([P, DV], U8, name="vsx", align_bytes=64)
         th = keep.tile([P, QT, DV], F32, name="th")
@@ -72,10 +71,9 @@ def tile_attend_x_append128_gate_topk_kernel(tc, qT, kT, vT, new_kT, new_vT, vs,
         nkview = new_kT.rearrange("(p t) n -> p t n", t=PACK)
         vview = vT.rearrange("(h p) n -> p h n", p=P)
         oview = out[0].rearrange("(a p) e -> a p e", p=P)
+        nc.vector.memset(vs_t[:], 0.0)
+        nc.scalar.dma_start(vs_t[0:1, :], vs[0:1, :])
         nc.sync.dma_start(offs_t[:], offs)
-        nc.sync.dma_start(vs_t[0:32, :], vs[0:32, :])
-        nc.vector.memset(vs_t[32:64, :], 0.0)
-        nc.gpsimd.memset(vs_t[64:128, :], 0.0)
         nc.sync.dma_start(slots_t[:], slots)
         nc.sync.dma_start(newk0[:], nkview[:, 0, :])
         nc.sync.dma_start(kp[0][:], kview[:, 0, :])
@@ -94,9 +92,10 @@ def tile_attend_x_append128_gate_topk_kernel(tc, qT, kT, vT, new_kT, new_vT, vs,
         nc.vector.tensor_copy(vsg[:], vs_t[:].indirect(offs_t[:]))
         for t in range(PACK):
             nc.tensor.transpose(vs_ps[:, t, :], vsg[:].rearrange("p (s t) -> p t s", t=PACK)[:, t, :], ident_f[:])
-        nc.scalar.copy(vsc[:], vs_ps[:, :, 0])
         nc.vector.tensor_copy(kp[0][:].indirect(slots_t[:]), newk0[:])
         nc.scalar.activation(kb[0][:], kp[0][:], ACT.Copy)
+        vsc = keep.tile([P, PACK], F32, name="vsc", tag="kp0")
+        nc.scalar.copy(vsc[:], vs_ps[:, :, 0])
         nc.scalar.activation(ki[:, :, 0], kb[0][:].indirect(offs_t[:]), ACT.Copy)
         nc.vector.tensor_copy(kp[1][:].indirect(slots_t[:]), newk[:, 0, :])
         nc.scalar.activation(kb[1][:], kp[1][:], ACT.Copy)

@@ -71,12 +71,12 @@ def tile_attend_x_append128_gate_topk_kernel(tc, qT, kT, vT, new_kT, new_vT, vs,
         nkview = new_kT.rearrange("(p t) n -> p t n", t=PACK)
         vview = vT.rearrange("(h p) n -> p h n", p=P)
         oview = out[0].rearrange("(a p) e -> a p e", p=P)
-        nc.vector.memset(vs_t[:], 0.0)
-        nc.scalar.dma_start(vs_t[0:1, :], vs[0:1, :])
-        nc.sync.dma_start(offs_t[:], offs)
         nc.sync.dma_start(slots_t[:], slots)
         nc.sync.dma_start(newk0[:], nkview[:, 0, :])
         nc.sync.dma_start(kp[0][:], kview[:, 0, :])
+        nc.sync.dma_start(offs_t[:], offs)
+        nc.gpsimd.memset(vs_t[:], 0.0)
+        nc.sync.dma_start(vs_t[0:1, :], vs[0:1, :])
         nc.sync.dma_start(newk[:], nkview[:, 1:PACK, :])
         nc.sync.dma_start(kp[1][:], kview[:, 1, :])
         nc.sync.dma_start(kp[2][:], kview[:, 2, :])
@@ -89,16 +89,16 @@ def tile_attend_x_append128_gate_topk_kernel(tc, qT, kT, vT, new_kT, new_vT, vs,
         nc.gpsimd.memset(warm[:], 0.0)
         nc.scalar.activation(warm_out[:], warm[:], ACT.Exp)
         make_identity(nc, ident_f[:])
+        nc.vector.tensor_copy(kp[0][:].indirect(slots_t[:]), newk0[:])
         nc.vector.tensor_copy(vsg[:], vs_t[:].indirect(offs_t[:]))
         for t in range(PACK):
             nc.tensor.transpose(vs_ps[:, t, :], vsg[:].rearrange("p (s t) -> p t s", t=PACK)[:, t, :], ident_f[:])
-        nc.vector.tensor_copy(kp[0][:].indirect(slots_t[:]), newk0[:])
         nc.scalar.activation(kb[0][:], kp[0][:], ACT.Copy)
-        vsc = keep.tile([P, PACK], F32, name="vsc", tag="kp0")
-        nc.scalar.copy(vsc[:], vs_ps[:, :, 0])
         nc.scalar.activation(ki[:, :, 0], kb[0][:].indirect(offs_t[:]), ACT.Copy)
         nc.vector.tensor_copy(kp[1][:].indirect(slots_t[:]), newk[:, 0, :])
         nc.scalar.activation(kb[1][:], kp[1][:], ACT.Copy)
+        vsc = keep.tile([P, PACK], F32, name="vsc", tag="kp1")
+        nc.scalar.copy(vsc[:], vs_ps[:, :, 0])
         nc.scalar.activation(ki[:, :, 1], kb[1][:].indirect(offs_t[:]), ACT.Copy)
         nc.vector.tensor_copy(kp[2][:].indirect(slots_t[:]), newk[:, 1, :])
         nc.vector.tensor_copy(ki[:, :, 2], kp[2][:].indirect(offs_t[:]))

@@ -36,11 +36,11 @@ def tile_attend_x_append128_gate_topk_kernel(tc, qT, kT, vT, new_kT, new_vT, vs,
         vb = [keep.tile([P, T], BF16, name=f"vb{h}") for h in range(ET)]
         newk0 = keep.tile([P, NEW], F32, name="newk0")
         newk = keep.tile([P, PACK - 1, NEW], F32, name="newk")
-        newv = keep.tile([P, ET, NEW], F32, name="newv")
+        newv = [keep.tile([P, NEW], F32, name=f"newv{h}") for h in range(ET)]
         qf = keep.tile([P, PACK, NQ], F32, name="qf")
         vs_t = keep.tile([P, T], F32, name="vs_t")
         og_t = keep.tile([P, QT, DV], F32, name="og_t")
-        ki = keep.tile([P, N, PACK], BF16, name="ki", align_bytes=64)
+        ki = keep.tile([P, N, PACK], BF16, name="ki", tag="ki", align_bytes=64)
         qi = share.tile([P, NQ, PACK], BF16, name="qi", align_bytes=64, offset=0)
         qc = keep.tile([P, NQ], U32, name="qc", tag="qc", align_bytes=64)
         qs = keep.tile([P, NQ], U8, name="qs", align_bytes=64)
@@ -70,50 +70,54 @@ def tile_attend_x_append128_gate_topk_kernel(tc, qT, kT, vT, new_kT, new_vT, vs,
         kview = kT.rearrange("(p t) n -> p t n", t=PACK)
         nkview = new_kT.rearrange("(p t) n -> p t n", t=PACK)
         vview = vT.rearrange("(h p) n -> p h n", p=P)
+        nvview = new_vT.rearrange("(h p) n -> p h n", p=P)
         oview = out[0].rearrange("(a p) e -> a p e", p=P)
         nc.sync.dma_start(slots_t[:], slots)
         nc.sync.dma_start(newk0[:], nkview[:, 0, :])
         nc.sync.dma_start(kp[0][:], kview[:, 0, :])
+        nc.sync.dma_start(og_t[:], og[0].rearrange("(a p) e -> p a e", p=P))
         nc.sync.dma_start(offs_t[:], offs)
-        nc.gpsimd.memset(vs_t[:], 0.0)
-        nc.sync.dma_start(vs_t[0:1, :], vs[0:1, :])
         nc.sync.dma_start(newk[:], nkview[:, 1:PACK, :])
         nc.sync.dma_start(kp[1][:], kview[:, 1, :])
         nc.sync.dma_start(kp[2][:], kview[:, 2, :])
-        nc.sync.dma_start(newv[:], new_vT.rearrange("(h p) n -> p h n", p=P))
-        nc.sync.dma_start(vp[0][:], vview[:, 0, :])
         nc.sync.dma_start(kp[3][:], kview[:, 3, :])
+        nc.sync.dma_start(newv[0][:], nvview[:, 0, :])
+        nc.sync.dma_start(vp[0][:], vview[:, 0, :])
+        nc.gpsimd.memset(vs_t[:], 0.0)
+        nc.sync.dma_start(vs_t[0:1, :], vs[0:1, :])
         nc.sync.dma_start(qf[:], qT[0].rearrange("(p t) n -> p t n", t=PACK))
-        nc.sync.dma_start(og_t[:], og[0].rearrange("(a p) e -> p a e", p=P))
+        nc.sync.dma_start(newv[1][:], nvview[:, 1, :])
         nc.sync.dma_start(vp[1][:], vview[:, 1, :])
         nc.gpsimd.memset(warm[:], 0.0)
         nc.scalar.activation(warm_out[:], warm[:], ACT.Exp)
         make_identity(nc, ident_f[:])
+        nc.scalar.activation(th[:], og_t[:], ACT.Tanh, scale=0.5)
+        nc.gpsimd.tensor_scalar(gate[:], th[:], 0.5, 0.5, ALU.mult, ALU.add)
         nc.vector.tensor_copy(kp[0][:].indirect(slots_t[:]), newk0[:])
+        nc.vector.tensor_copy(kb[0][:], kp[0][:])
+        nc.scalar.activation(ki[:, :, 0], kb[0][:].indirect(offs_t[:]), ACT.Copy)
+        nc.vector.tensor_copy(kp[1][:].indirect(slots_t[:]), newk[:, 0, :])
+        nc.vector.tensor_copy(kb[1][:], kp[1][:])
+        nc.scalar.activation(ki[:, :, 1], kb[1][:].indirect(offs_t[:]), ACT.Copy)
+        nc.vector.tensor_copy(kp[2][:].indirect(slots_t[:]), newk[:, 1, :])
+        nc.vector.tensor_copy(kb[2][:], kp[2][:])
+        nc.scalar.activation(ki[:, :, 2], kb[2][:].indirect(offs_t[:]), ACT.Copy)
+        nc.vector.tensor_copy(kp[3][:].indirect(slots_t[:]), newk[:, 2, :])
+        nc.vector.tensor_copy(kb[3][:], kp[3][:])
+        nc.scalar.activation(ki[:, :, 3], kb[3][:].indirect(offs_t[:]), ACT.Copy)
+        nc.vector.tensor_copy(vp[0][:].indirect(slots_t[:]), newv[0][:])
+        nc.scalar.activation(vb[0][:], vp[0][:], ACT.Copy)
         nc.vector.tensor_copy(vsg[:], vs_t[:].indirect(offs_t[:]))
         for t in range(PACK):
             nc.tensor.transpose(vs_ps[:, t, :], vsg[:].rearrange("p (s t) -> p t s", t=PACK)[:, t, :], ident_f[:])
-        nc.scalar.activation(kb[0][:], kp[0][:], ACT.Copy)
-        nc.scalar.activation(ki[:, :, 0], kb[0][:].indirect(offs_t[:]), ACT.Copy)
-        nc.vector.tensor_copy(kp[1][:].indirect(slots_t[:]), newk[:, 0, :])
-        nc.scalar.activation(kb[1][:], kp[1][:], ACT.Copy)
-        vsc = keep.tile([P, PACK], F32, name="vsc", tag="kp1")
-        nc.scalar.copy(vsc[:], vs_ps[:, :, 0])
-        nc.scalar.activation(ki[:, :, 1], kb[1][:].indirect(offs_t[:]), ACT.Copy)
-        nc.vector.tensor_copy(kp[2][:].indirect(slots_t[:]), newk[:, 1, :])
-        nc.vector.tensor_copy(ki[:, :, 2], kp[2][:].indirect(offs_t[:]))
-        nc.vector.tensor_copy(vp[0][:].indirect(slots_t[:]), newv[:, 0, :])
-        nc.scalar.activation(vb[0][:], vp[0][:], ACT.Copy)
         nc.gpsimd.tensor_scalar(qi[:], qf[:].rearrange("p t n -> p n t"), 1.0, 0.0, ALU.mult, ALU.add)
-        nc.vector.tensor_copy(kp[3][:].indirect(slots_t[:]), newk[:, 2, :])
-        nc.vector.tensor_copy(ki[:, :, 3], kp[3][:].indirect(offs_t[:]))
         nc.vector.quantize_mx(out=qc[:].bitcast(FP8X4), scales=qs[:], in_=qi[:].rearrange("p n t -> p (n t)"))
         vg.append(share.tile([P, N], BF16, name="vg0", align_bytes=64, offset=1024))
         nc.scalar.activation(vg[0][:], vb[0][:].indirect(offs_t[:]), ACT.Copy)
-        nc.scalar.activation(th[:], og_t[:], ACT.Tanh, scale=0.5)
-        nc.gpsimd.tensor_scalar(gate[:], th[:], 0.5, 0.5, ALU.mult, ALU.add)
         ks = share.tile([P, N], U8, name="ks", align_bytes=64, offset=0)
         nc.vector.quantize_mx(out=kc[:].bitcast(FP8X4), scales=ks[:], in_=ki[:].rearrange("p n t -> p (n t)"))
+        vsc = keep.tile([P, PACK], F32, name="vsc", tag="ki", align_bytes=64)
+        nc.scalar.copy(vsc[:], vs_ps[:, :, 0])
         nc.tensor.matmul_mx(s_ps[0][:], lhsT=qc[:, 0:128].bitcast(FP8X4), lhsT_scale=qs[:, 0:128], rhs=kc[:].bitcast(FP8X4), rhs_scale=ks[:], start=True, stop=True)
         nc.tensor.matmul_mx(s_ps[1][:], lhsT=qc[:, 128:256].bitcast(FP8X4), lhsT_scale=qs[:, 128:256], rhs=kc[:].bitcast(FP8X4), rhs_scale=ks[:], start=True, stop=True)
         v_ps.append(psum.tile([P, 2, P], F32, name="v_ps0", tag="v_ps0"))
@@ -127,7 +131,7 @@ def tile_attend_x_append128_gate_topk_kernel(tc, qT, kT, vT, new_kT, new_vT, vs,
         nc.scalar.activation(pt[1][:], s_ps[1][:].rearrange("q (s t) -> q t s", t=PACK), ACT.Exp, bias=nm[1][:], scale=1.0, accum_out=lt[:, 1:2])
         for t in range(PACK):
             nc.tensor.transpose(w_ps[1][:, t, :], pt[1][:, t, :], ident_f[:])
-        nc.vector.tensor_copy(vp[1][:].indirect(slots_t[:]), newv[:, 1, :])
+        nc.vector.tensor_copy(vp[1][:].indirect(slots_t[:]), newv[1][:])
         vg.append(keep.tile([P, N], BF16, name="vg1", tag="qc", align_bytes=64))
         nc.vector.tensor_copy(vg[1][:], vp[1][:].indirect(offs_t[:]))
         v_ps.append(psum.tile([P, 2, P], F32, name="v_ps1", tag="s_ps1"))

@@ -36,7 +36,7 @@ def tile_attend_x_append128_gate_topk_kernel(tc, qT, kT, vT, new_kT, new_vT, vs,
         vb = [keep.tile([P, T], BF16, name=f"vb{h}") for h in range(ET)]
         newk0 = keep.tile([P, NEW], F32, name="newk0")
         newk = keep.tile([P, PACK - 1, NEW], F32, name="newk")
-        newv = [keep.tile([P, NEW], F32, name=f"newv{h}") for h in range(ET)]
+        newv = keep.tile([P, ET, NEW], F32, name="newv")
         qf = keep.tile([P, PACK, NQ], F32, name="qf")
         vs_t = keep.tile([P, T], F32, name="vs_t")
         og_t = keep.tile([P, QT, DV], F32, name="og_t")
@@ -50,9 +50,8 @@ def tile_attend_x_append128_gate_topk_kernel(tc, qT, kT, vT, new_kT, new_vT, vs,
         vsg = keep.tile([P, N], F32, name="vsg")
         vc = keep.tile([P, DV], U32, name="vc", align_bytes=64)
         vsx = keep.tile([P, DV], U8, name="vsx", align_bytes=64)
-        th = keep.tile([P, QT, DV], F32, name="th")
         gate = keep.tile([P, QT, DV], F32, name="gate")
-        nm = [keep.tile([P, 1], F32, name=f"nm{a}", tag=f"nm{a}", align_bytes=64) for a in range(QT)]
+        nm = [keep.tile([P, 1], F32, name="nm0"), share.tile([P, 32], F32, name="nm1", align_bytes=64, offset=4096 - 64)[:, 0:1]]
         lt = keep.tile([P, QT], F32, name="lt")
         rl = keep.tile([P, QT], F32, name="rl")
         pt = [keep.tile([P, PACK, P], F32, name=f"pt{a}") for a in range(QT)]
@@ -72,27 +71,24 @@ def tile_attend_x_append128_gate_topk_kernel(tc, qT, kT, vT, new_kT, new_vT, vs,
         vview = vT.rearrange("(h p) n -> p h n", p=P)
         nvview = new_vT.rearrange("(h p) n -> p h n", p=P)
         oview = out[0].rearrange("(a p) e -> a p e", p=P)
+        nc.sync.dma_start(kp[0][:], kview[:, 0, :])
         nc.sync.dma_start(slots_t[:], slots)
         nc.sync.dma_start(newk0[:], nkview[:, 0, :])
-        nc.sync.dma_start(kp[0][:], kview[:, 0, :])
-        nc.sync.dma_start(og_t[:], og[0].rearrange("(a p) e -> p a e", p=P))
         nc.sync.dma_start(offs_t[:], offs)
         nc.sync.dma_start(newk[:], nkview[:, 1:PACK, :])
         nc.sync.dma_start(kp[1][:], kview[:, 1, :])
         nc.sync.dma_start(kp[2][:], kview[:, 2, :])
         nc.sync.dma_start(kp[3][:], kview[:, 3, :])
-        nc.sync.dma_start(newv[0][:], nvview[:, 0, :])
+        nc.sync.dma_start(newv[:], new_vT.rearrange("(h p) n -> p h n", p=P))
         nc.sync.dma_start(vp[0][:], vview[:, 0, :])
         nc.gpsimd.memset(vs_t[:], 0.0)
         nc.sync.dma_start(vs_t[0:1, :], vs[0:1, :])
         nc.sync.dma_start(qf[:], qT[0].rearrange("(p t) n -> p t n", t=PACK))
-        nc.sync.dma_start(newv[1][:], nvview[:, 1, :])
+        nc.sync.dma_start(og_t[:], og[0].rearrange("(a p) e -> p a e", p=P))
         nc.sync.dma_start(vp[1][:], vview[:, 1, :])
         nc.gpsimd.memset(warm[:], 0.0)
         nc.scalar.activation(warm_out[:], warm[:], ACT.Exp)
         make_identity(nc, ident_f[:])
-        nc.scalar.activation(th[:], og_t[:], ACT.Tanh, scale=0.5)
-        nc.gpsimd.tensor_scalar(gate[:], th[:], 0.5, 0.5, ALU.mult, ALU.add)
         nc.vector.tensor_copy(kp[0][:].indirect(slots_t[:]), newk0[:])
         nc.vector.tensor_copy(kb[0][:], kp[0][:])
         nc.scalar.activation(ki[:, :, 0], kb[0][:].indirect(offs_t[:]), ACT.Copy)
@@ -105,7 +101,7 @@ def tile_attend_x_append128_gate_topk_kernel(tc, qT, kT, vT, new_kT, new_vT, vs,
         nc.vector.tensor_copy(kp[3][:].indirect(slots_t[:]), newk[:, 2, :])
         nc.vector.tensor_copy(kb[3][:], kp[3][:])
         nc.scalar.activation(ki[:, :, 3], kb[3][:].indirect(offs_t[:]), ACT.Copy)
-        nc.vector.tensor_copy(vp[0][:].indirect(slots_t[:]), newv[0][:])
+        nc.vector.tensor_copy(vp[0][:].indirect(slots_t[:]), newv[:, 0, :])
         nc.scalar.activation(vb[0][:], vp[0][:], ACT.Copy)
         nc.vector.tensor_copy(vsg[:], vs_t[:].indirect(offs_t[:]))
         for t in range(PACK):
@@ -127,18 +123,21 @@ def tile_attend_x_append128_gate_topk_kernel(tc, qT, kT, vT, new_kT, new_vT, vs,
         nc.scalar.activation(pt[0][:], s_ps[0][:].rearrange("q (s t) -> q t s", t=PACK), ACT.Exp, bias=nm[0][:], scale=1.0, accum_out=lt[:, 0:1])
         for t in range(PACK):
             nc.tensor.transpose(w_ps[0][:, t, :], pt[0][:, t, :], ident_f[:])
-        nc.vector.tensor_reduce(nm[1][:], s_ps[1][:], axis=AXX, op=ALU.max, negate=True)
-        nc.scalar.activation(pt[1][:], s_ps[1][:].rearrange("q (s t) -> q t s", t=PACK), ACT.Exp, bias=nm[1][:], scale=1.0, accum_out=lt[:, 1:2])
+        nc.vector.tensor_reduce(nm[1], s_ps[1][:], axis=AXX, op=ALU.max, negate=True)
+        nc.scalar.activation(pt[1][:], s_ps[1][:].rearrange("q (s t) -> q t s", t=PACK), ACT.Exp, bias=nm[1], scale=1.0, accum_out=lt[:, 1:2])
         for t in range(PACK):
             nc.tensor.transpose(w_ps[1][:, t, :], pt[1][:, t, :], ident_f[:])
-        nc.vector.tensor_copy(vp[1][:].indirect(slots_t[:]), newv[1][:])
+        nc.vector.tensor_copy(vp[1][:].indirect(slots_t[:]), newv[:, 1, :])
         vg.append(keep.tile([P, N], BF16, name="vg1", tag="qc", align_bytes=64))
         nc.vector.tensor_copy(vg[1][:], vp[1][:].indirect(offs_t[:]))
         v_ps.append(psum.tile([P, 2, P], F32, name="v_ps1", tag="s_ps1"))
         for u in range(2):
             nc.tensor.transpose(v_ps[1][:, u, :], vg[1][:].bitcast(F32)[:, u : N // 2 : 2], ident_f[:])
-        vi = keep.tile([P, DV, PACK], BF16, name="vi", tag="nm1", align_bytes=64)
+        vi = share.tile([P, DV, PACK], BF16, name="vi", align_bytes=64, offset=2048)
         nc.scalar.copy(vi[:, 0:128, :].rearrange("p n t -> p (n t)").bitcast(F32).rearrange("s (e u) -> s e u", u=2), v_ps[0][:].rearrange("s u e -> s e u"))
+        th = share.tile([P, QT, DV], F32, name="th", align_bytes=64, offset=4096)
+        nc.scalar.activation(th[:], og_t[:], ACT.Tanh, scale=0.5)
+        nc.gpsimd.tensor_scalar(gate[:], th[:], 0.5, 0.5, ALU.mult, ALU.add)
         nc.scalar.copy(vi[:, 128:256, :].rearrange("p n t -> p (n t)").bitcast(F32).rearrange("s (e u) -> s e u", u=2), v_ps[1][:].rearrange("s u e -> s e u"))
         nc.vector.reciprocal(rl[:], lt[:])
         nc.vector.tensor_tensor(wi[0][:], w_ps[0][:].rearrange("s t q -> s q t"), vsc[:].unsqueeze(1).to_broadcast([P, P, PACK]), ALU.mult)

@@ -111,10 +111,12 @@ def tile_attend_x_append128_gate_topk_kernel(tc, qT, kT, vT, new_kT, new_vT, vs,
         vg.append(share.tile([P, N], BF16, name="vg0", align_bytes=64, offset=1024))
         nc.scalar.activation(vg[0][:], vb[0][:].indirect(offs_t[:]), ACT.Copy)
         ks = share.tile([P, N], U8, name="ks", align_bytes=64, offset=0)
-        nc.vector.quantize_mx(out=kc[:].bitcast(FP8X4), scales=ks[:], in_=ki[:].rearrange("p n t -> p (n t)"))
+        nc.vector.quantize_mx(out=kc[:, 0:256].bitcast(FP8X4), scales=ks[:, 0:256], in_=ki[:, 0:256, :].rearrange("p n t -> p (n t)"))
+        nc.vector.quantize_mx(out=kc[:, 256:512].bitcast(FP8X4), scales=ks[:, 256:512], in_=ki[:, 256:512, :].rearrange("p n t -> p (n t)"))
         vsc = keep.tile([P, PACK], F32, name="vsc", tag="ki", align_bytes=64)
         nc.scalar.copy(vsc[:], vs_ps[:, :, 0])
-        nc.tensor.matmul_mx(s_ps[0][:], lhsT=qc[:, 0:128].bitcast(FP8X4), lhsT_scale=qs[:, 0:128], rhs=kc[:].bitcast(FP8X4), rhs_scale=ks[:], start=True, stop=True)
+        nc.tensor.matmul_mx(s_ps[0][:, 0:256], lhsT=qc[:, 0:128].bitcast(FP8X4), lhsT_scale=qs[:, 0:128], rhs=kc[:, 0:256].bitcast(FP8X4), rhs_scale=ks[:, 0:256], start=True, stop=True)
+        nc.tensor.matmul_mx(s_ps[0][:, 256:512], lhsT=qc[:, 0:128].bitcast(FP8X4), lhsT_scale=qs[:, 0:128], rhs=kc[:, 256:512].bitcast(FP8X4), rhs_scale=ks[:, 256:512], start=True, stop=True)
         nc.tensor.matmul_mx(s_ps[1][:], lhsT=qc[:, 128:256].bitcast(FP8X4), lhsT_scale=qs[:, 128:256], rhs=kc[:].bitcast(FP8X4), rhs_scale=ks[:], start=True, stop=True)
         v_ps.append(psum.tile([P, 2, P], F32, name="v_ps0", tag="v_ps0"))
         for u in range(2):
@@ -141,9 +143,10 @@ def tile_attend_x_append128_gate_topk_kernel(tc, qT, kT, vT, new_kT, new_vT, vs,
         nc.scalar.copy(vi[:, 128:256, :].rearrange("p n t -> p (n t)").bitcast(F32).rearrange("s (e u) -> s e u", u=2), v_ps[1][:].rearrange("s u e -> s e u"))
         nc.vector.reciprocal(rl[:], lt[:])
         nc.vector.tensor_tensor(wi[0][:], w_ps[0][:].rearrange("s t q -> s q t"), vsc[:].unsqueeze(1).to_broadcast([P, P, PACK]), ALU.mult)
+        nc.vector.quantize_mx(out=vc[:, 0:128].bitcast(FP8X4), scales=vsx[:, 0:128], in_=vi[:, 0:128, :].rearrange("p n t -> p (n t)"))
         nc.vector.tensor_tensor(wi[1][:], w_ps[1][:].rearrange("s t q -> s q t"), vsc[:].unsqueeze(1).to_broadcast([P, P, PACK]), ALU.mult)
         nc.vector.quantize_mx(out=wc[0][:].bitcast(FP8X4), scales=ws[0][:], in_=wi[0][:].rearrange("p n t -> p (n t)"))
-        nc.vector.quantize_mx(out=vc[:].bitcast(FP8X4), scales=vsx[:], in_=vi[:].rearrange("p n t -> p (n t)"))
+        nc.vector.quantize_mx(out=vc[:, 128:256].bitcast(FP8X4), scales=vsx[:, 128:256], in_=vi[:, 128:256, :].rearrange("p n t -> p (n t)"))
         nc.vector.quantize_mx(out=wc[1][:].bitcast(FP8X4), scales=ws[1][:], in_=wi[1][:].rearrange("p n t -> p (n t)"))
         nc.tensor.matmul_mx(y_ps[0][:], lhsT=wc[0][:].bitcast(FP8X4), lhsT_scale=ws[0][:], rhs=vc[:].bitcast(FP8X4), rhs_scale=vsx[:], start=True, stop=True)
         nc.tensor.matmul_mx(y_ps[1][:], lhsT=wc[1][:].bitcast(FP8X4), lhsT_scale=ws[1][:], rhs=vc[:].bitcast(FP8X4), rhs_scale=vsx[:], start=True, stop=True)

@@ -90,7 +90,8 @@ def tile_attend_x_append128_gate_topk_kernel(tc, qT, kT, vT, new_kT, new_vT, vs,
         nc.scalar.activation(warm_out[:], warm[:], ACT.Exp)
         make_identity(nc, ident_f[:])
         nc.vector.tensor_copy(kp[0][:].indirect(slots_t[:]), newk0[:])
-        nc.vector.tensor_copy(kb[0][:], kp[0][:])
+        nc.vector.tensor_copy(kb[0][:, :688], kp[0][:, :688])
+        nc.scalar.activation(kb[0][:, 688:], kp[0][:, 688:], ACT.Copy)
         nc.scalar.activation(ki[:, :, 0], kb[0][:].indirect(offs_t[:]), ACT.Copy)
         nc.vector.tensor_copy(kp[1][:].indirect(slots_t[:]), newk[:, 0, :])
         nc.vector.tensor_copy(kb[1][:], kp[1][:])
@@ -146,10 +147,12 @@ def tile_attend_x_append128_gate_topk_kernel(tc, qT, kT, vT, new_kT, new_vT, vs,
         nc.vector.quantize_mx(out=vc[:, 0:128].bitcast(FP8X4), scales=vsx[:, 0:128], in_=vi[:, 0:128, :].rearrange("p n t -> p (n t)"))
         nc.vector.tensor_tensor(wi[1][:], w_ps[1][:].rearrange("s t q -> s q t"), vsc[:].unsqueeze(1).to_broadcast([P, P, PACK]), ALU.mult)
         nc.vector.quantize_mx(out=wc[0][:].bitcast(FP8X4), scales=ws[0][:], in_=wi[0][:].rearrange("p n t -> p (n t)"))
-        nc.vector.quantize_mx(out=vc[:, 128:256].bitcast(FP8X4), scales=vsx[:, 128:256], in_=vi[:, 128:256, :].rearrange("p n t -> p (n t)"))
         nc.vector.quantize_mx(out=wc[1][:].bitcast(FP8X4), scales=ws[1][:], in_=wi[1][:].rearrange("p n t -> p (n t)"))
-        nc.tensor.matmul_mx(y_ps[0][:], lhsT=wc[0][:].bitcast(FP8X4), lhsT_scale=ws[0][:], rhs=vc[:].bitcast(FP8X4), rhs_scale=vsx[:], start=True, stop=True)
-        nc.tensor.matmul_mx(y_ps[1][:], lhsT=wc[1][:].bitcast(FP8X4), lhsT_scale=ws[1][:], rhs=vc[:].bitcast(FP8X4), rhs_scale=vsx[:], start=True, stop=True)
+        nc.vector.quantize_mx(out=vc[:, 128:256].bitcast(FP8X4), scales=vsx[:, 128:256], in_=vi[:, 128:256, :].rearrange("p n t -> p (n t)"))
+        nc.tensor.matmul_mx(y_ps[0][:, 0:128], lhsT=wc[0][:].bitcast(FP8X4), lhsT_scale=ws[0][:], rhs=vc[:, 0:128].bitcast(FP8X4), rhs_scale=vsx[:, 0:128], start=True, stop=True)
+        nc.tensor.matmul_mx(y_ps[0][:, 128:256], lhsT=wc[0][:].bitcast(FP8X4), lhsT_scale=ws[0][:], rhs=vc[:, 128:256].bitcast(FP8X4), rhs_scale=vsx[:, 128:256], start=True, stop=True)
+        nc.tensor.matmul_mx(y_ps[1][:, 0:128], lhsT=wc[1][:].bitcast(FP8X4), lhsT_scale=ws[1][:], rhs=vc[:, 0:128].bitcast(FP8X4), rhs_scale=vsx[:, 0:128], start=True, stop=True)
+        nc.tensor.matmul_mx(y_ps[1][:, 128:256], lhsT=wc[1][:].bitcast(FP8X4), lhsT_scale=ws[1][:], rhs=vc[:, 128:256].bitcast(FP8X4), rhs_scale=vsx[:, 128:256], start=True, stop=True)
         nc.vector.scalar_tensor_tensor(res[0][:], y_ps[0][:], rl[:, 0:1], gate[:, 0, :], ALU.mult, ALU.mult)
         nc.sync.dma_start(oview[0], res[0][:])
         nc.vector.scalar_tensor_tensor(res[1][:], y_ps[1][:], rl[:, 1:2], gate[:, 1, :], ALU.mult, ALU.mult)

@@ -30,7 +30,7 @@ def tile_attend_x_append128_gate_topk_kernel(tc, qT, kT, vT, new_kT, new_vT, vs,
         psum = ctx.enter_context(tc.psum_pool(name="psum", bufs=1))
         slots_t = keep.tile([P, NEW // 16], U16, name="slots_t")
         offs_t = keep.tile([P, N // 16], U16, name="offs_t")
-        kp = [keep.tile([P, T], F32, name=f"kp{t}", tag=f"kp{t}") for t in range(PACK)]
+        kp = [keep.tile([P, T], F32, name=f"kp{t}", tag=f"kp{t}") for t in range(PACK - 1)] + [share.tile([P, T], F32, name="kp3", align_bytes=64, offset=0)]
         kb = [keep.tile([P, T], BF16, name=f"kb{t}") for t in range(PACK)]
         vp = [keep.tile([P, T], F32, name=f"vp{h}") for h in range(ET)]
         vb = [keep.tile([P, T], BF16, name=f"vb{h}") for h in range(ET)]
@@ -50,7 +50,6 @@ def tile_attend_x_append128_gate_topk_kernel(tc, qT, kT, vT, new_kT, new_vT, vs,
         vsg = keep.tile([P, N], F32, name="vsg")
         vc = keep.tile([P, DV], U32, name="vc", align_bytes=64)
         vsx = keep.tile([P, DV], U8, name="vsx", align_bytes=64)
-        gate = keep.tile([P, QT, DV], F32, name="gate")
         nm = [keep.tile([P, 1], F32, name="nm0"), share.tile([P, 32], F32, name="nm1", align_bytes=64, offset=4096 - 64)[:, 0:1]]
         lt = keep.tile([P, QT], F32, name="lt")
         rl = keep.tile([P, QT], F32, name="rl")
@@ -107,7 +106,7 @@ def tile_attend_x_append128_gate_topk_kernel(tc, qT, kT, vT, new_kT, new_vT, vs,
         nc.vector.tensor_copy(vsg[:], vs_t[:].indirect(offs_t[:]))
         for t in range(PACK):
             nc.tensor.transpose(vs_ps[:, t, :], vsg[:].rearrange("p (s t) -> p t s", t=PACK)[:, t, :], ident_f[:])
-        nc.gpsimd.tensor_scalar(qi[:], qf[:].rearrange("p t n -> p n t"), 1.0, 0.0, ALU.mult, ALU.add)
+        nc.gpsimd.tensor_scalar(qi[:].rearrange("p (c i) t -> p c t i", i=2), qf[:].rearrange("p t (c i) -> p c t i", i=2), 1.0, 0.0, ALU.mult, ALU.add)
         nc.vector.quantize_mx(out=qc[:].bitcast(FP8X4), scales=qs[:], in_=qi[:].rearrange("p n t -> p (n t)"))
         vg.append(share.tile([P, N], BF16, name="vg0", align_bytes=64, offset=1024))
         nc.scalar.activation(vg[0][:], vb[0][:].indirect(offs_t[:]), ACT.Copy)
@@ -140,8 +139,9 @@ def tile_attend_x_append128_gate_topk_kernel(tc, qT, kT, vT, new_kT, new_vT, vs,
         nc.scalar.copy(vi[:, 0:128, :].rearrange("p n t -> p (n t)").bitcast(F32).rearrange("s (e u) -> s e u", u=2), v_ps[0][:].rearrange("s u e -> s e u"))
         th = share.tile([P, QT, DV], F32, name="th", align_bytes=64, offset=4096)
         nc.scalar.activation(th[:], og_t[:], ACT.Tanh, scale=0.5)
-        nc.gpsimd.tensor_scalar(gate[:], th[:], 0.5, 0.5, ALU.mult, ALU.add)
         nc.scalar.copy(vi[:, 128:256, :].rearrange("p n t -> p (n t)").bitcast(F32).rearrange("s (e u) -> s e u", u=2), v_ps[1][:].rearrange("s u e -> s e u"))
+        gate = keep.tile([P, QT, DV], F32, name="gate", tag="qc", align_bytes=64)
+        nc.scalar.activation(gate[:], th[:], ACT.Copy, scale=0.5, bias=0.5)
         nc.vector.reciprocal(rl[:], lt[:])
         nc.vector.tensor_tensor(wi[0][:], w_ps[0][:].rearrange("s t q -> s q t"), vsc[:].unsqueeze(1).to_broadcast([P, P, PACK]), ALU.mult)
         nc.vector.quantize_mx(out=vc[:, 0:128].bitcast(FP8X4), scales=vsx[:, 0:128], in_=vi[:, 0:128, :].rearrange("p n t -> p (n t)"))

@@ -18,39 +18,49 @@ P = 128
 PACK = 4
 QT = NQ // P
 ET = DV // P
+HALF = N // 2
+CAST_SPLIT = 688
 
 FLOPS = 2 * NQ * N * (D + DV)
 
 
 def tile_attend_x_append128_gate_topk_kernel(tc, qT, kT, vT, new_kT, new_vT, vs, og, offs, slots, out):
     nc = tc.nc
+
+    def quantize(codes, scales, words):
+        nc.vector.quantize_mx(out=codes.bitcast(FP8X4), scales=scales, in_=words.rearrange("p n t -> p (n t)"))
+
+    def product(acc, lhs_codes, lhs_scales, rhs_codes, rhs_scales):
+        nc.tensor.matmul_mx(acc, lhsT=lhs_codes.bitcast(FP8X4), lhsT_scale=lhs_scales, rhs=rhs_codes.bitcast(FP8X4), rhs_scale=rhs_scales, start=True, stop=True)
+
     with ExitStack() as ctx:
         keep = ctx.enter_context(tc.tile_pool(name="keep", bufs=1))
         share = ctx.enter_context(tc.tile_pool(name="share", bufs=1))
         psum = ctx.enter_context(tc.psum_pool(name="psum", bufs=1))
         slots_t = keep.tile([P, NEW // 16], U16, name="slots_t")
         offs_t = keep.tile([P, N // 16], U16, name="offs_t")
-        kp = [keep.tile([P, T], F32, name=f"kp{t}", tag=f"kp{t}") for t in range(PACK - 1)] + [share.tile([P, T], F32, name="kp3", align_bytes=64, offset=0)]
-        kb = [keep.tile([P, T], BF16, name=f"kb{t}") for t in range(PACK)]
+        kp = [keep.tile([P, T], F32, name=f"kp{t}") for t in range(PACK)]
+        kb = [keep.tile([P, T], BF16, name=f"kb{t}") for t in range(2)]
         vp = [keep.tile([P, T], F32, name=f"vp{h}") for h in range(ET)]
-        vb = [keep.tile([P, T], BF16, name=f"vb{h}") for h in range(ET)]
         newk0 = keep.tile([P, NEW], F32, name="newk0")
-        newk = keep.tile([P, PACK - 1, NEW], F32, name="newk")
+        newk = keep.tile([P, PACK - 1, NEW], F32, name="newk", tag="newk")
         newv = keep.tile([P, ET, NEW], F32, name="newv")
         qf = keep.tile([P, PACK, NQ], F32, name="qf")
         vs_t = keep.tile([P, T], F32, name="vs_t")
         og_t = keep.tile([P, QT, DV], F32, name="og_t")
-        ki = keep.tile([P, N, PACK], BF16, name="ki", tag="ki", align_bytes=64)
+        pairs = [keep.tile([P, 2, HALF, 2], BF16, name=f"pairs{c}") for c in range(2)]
+        ki = [keep.tile([P, HALF, PACK], BF16, name=f"ki{c}", tag=f"ki{c}", align_bytes=64) for c in range(2)]
         qi = share.tile([P, NQ, PACK], BF16, name="qi", align_bytes=64, offset=0)
         qc = keep.tile([P, NQ], U32, name="qc", tag="qc", align_bytes=64)
         qs = keep.tile([P, NQ], U8, name="qs", align_bytes=64)
+        vb = keep.tile([P, T], BF16, name="vb")
         kc = keep.tile([P, N], U32, name="kc", align_bytes=64)
-        vg = []
-        v_ps = []
         vsg = keep.tile([P, N], F32, name="vsg")
+        vi = [share.tile([P, P, PACK], BF16, name="vi0", align_bytes=64, offset=5120), keep.tile([P, P, PACK], BF16, name="vi1", align_bytes=64)]
         vc = keep.tile([P, DV], U32, name="vc", align_bytes=64)
         vsx = keep.tile([P, DV], U8, name="vsx", align_bytes=64)
-        nm = [keep.tile([P, 1], F32, name="nm0"), share.tile([P, 32], F32, name="nm1", align_bytes=64, offset=4096 - 64)[:, 0:1]]
+        th = share.tile([P, QT, DV], F32, name="th", align_bytes=64, offset=6144)
+        nm = [keep.tile([P, 1], F32, name="nm0")[:], share.tile([P, 32], F32, name="nm1", align_bytes=64, offset=6144 - 64)[:, 0:1]]
         lt = keep.tile([P, QT], F32, name="lt")
         rl = keep.tile([P, QT], F32, name="rl")
         pt = [keep.tile([P, PACK, P], F32, name=f"pt{a}") for a in range(QT)]
@@ -68,92 +78,97 @@ def tile_attend_x_append128_gate_topk_kernel(tc, qT, kT, vT, new_kT, new_vT, vs,
         kview = kT.rearrange("(p t) n -> p t n", t=PACK)
         nkview = new_kT.rearrange("(p t) n -> p t n", t=PACK)
         vview = vT.rearrange("(h p) n -> p h n", p=P)
-        nvview = new_vT.rearrange("(h p) n -> p h n", p=P)
         oview = out[0].rearrange("(a p) e -> a p e", p=P)
+
         nc.sync.dma_start(kp[0][:], kview[:, 0, :])
         nc.sync.dma_start(slots_t[:], slots)
         nc.sync.dma_start(newk0[:], nkview[:, 0, :])
         nc.sync.dma_start(offs_t[:], offs)
         nc.sync.dma_start(newk[:], nkview[:, 1:PACK, :])
-        nc.sync.dma_start(kp[1][:], kview[:, 1, :])
-        nc.sync.dma_start(kp[2][:], kview[:, 2, :])
-        nc.sync.dma_start(kp[3][:], kview[:, 3, :])
-        nc.sync.dma_start(newv[:], new_vT.rearrange("(h p) n -> p h n", p=P))
-        nc.sync.dma_start(vp[0][:], vview[:, 0, :])
         nc.gpsimd.memset(vs_t[:], 0.0)
         nc.sync.dma_start(vs_t[0:1, :], vs[0:1, :])
+        for t in range(1, PACK):
+            nc.sync.dma_start(kp[t][:], kview[:, t, :])
+        nc.sync.dma_start(newv[:], new_vT.rearrange("(h p) n -> p h n", p=P))
         nc.sync.dma_start(qf[:], qT[0].rearrange("(p t) n -> p t n", t=PACK))
+        for h in range(ET):
+            nc.sync.dma_start(vp[h][:], vview[:, h, :])
         nc.sync.dma_start(og_t[:], og[0].rearrange("(a p) e -> p a e", p=P))
-        nc.sync.dma_start(vp[1][:], vview[:, 1, :])
+
         nc.gpsimd.memset(warm[:], 0.0)
         nc.scalar.activation(warm_out[:], warm[:], ACT.Exp)
         make_identity(nc, ident_f[:])
+
         nc.vector.tensor_copy(kp[0][:].indirect(slots_t[:]), newk0[:])
-        nc.vector.tensor_copy(kb[0][:, :688], kp[0][:, :688])
-        nc.scalar.activation(kb[0][:, 688:], kp[0][:, 688:], ACT.Copy)
-        nc.scalar.activation(ki[:, :, 0], kb[0][:].indirect(offs_t[:]), ACT.Copy)
-        nc.vector.tensor_copy(kp[1][:].indirect(slots_t[:]), newk[:, 0, :])
-        nc.vector.tensor_copy(kb[1][:], kp[1][:])
-        nc.scalar.activation(ki[:, :, 1], kb[1][:].indirect(offs_t[:]), ACT.Copy)
-        nc.vector.tensor_copy(kp[2][:].indirect(slots_t[:]), newk[:, 1, :])
-        nc.vector.tensor_copy(kb[2][:], kp[2][:])
-        nc.scalar.activation(ki[:, :, 2], kb[2][:].indirect(offs_t[:]), ACT.Copy)
-        nc.vector.tensor_copy(kp[3][:].indirect(slots_t[:]), newk[:, 2, :])
-        nc.vector.tensor_copy(kb[3][:], kp[3][:])
-        nc.scalar.activation(ki[:, :, 3], kb[3][:].indirect(offs_t[:]), ACT.Copy)
-        nc.vector.tensor_copy(vp[0][:].indirect(slots_t[:]), newv[:, 0, :])
-        nc.scalar.activation(vb[0][:], vp[0][:], ACT.Copy)
         nc.vector.tensor_copy(vsg[:], vs_t[:].indirect(offs_t[:]))
         for t in range(PACK):
             nc.tensor.transpose(vs_ps[:, t, :], vsg[:].rearrange("p (s t) -> p t s", t=PACK)[:, t, :], ident_f[:])
-        nc.gpsimd.tensor_scalar(qi[:].rearrange("p (c i) t -> p c t i", i=2), qf[:].rearrange("p t (c i) -> p c t i", i=2), 1.0, 0.0, ALU.mult, ALU.add)
-        nc.vector.quantize_mx(out=qc[:].bitcast(FP8X4), scales=qs[:], in_=qi[:].rearrange("p n t -> p (n t)"))
-        vg.append(share.tile([P, N], BF16, name="vg0", align_bytes=64, offset=1024))
-        nc.scalar.activation(vg[0][:], vb[0][:].indirect(offs_t[:]), ACT.Copy)
+        for t in range(1, PACK):
+            nc.vector.tensor_copy(kp[t][:].indirect(slots_t[:]), newk[:, t - 1, :])
+        for t in range(2):
+            nc.scalar.activation(kb[t][:], kp[t][:], ACT.Copy)
+            for c in range(2):
+                nc.scalar.activation(pairs[c][:, 0, :, t], kb[t][:].indirect(offs_t[:, c * 16 : (c + 1) * 16]), ACT.Copy)
+        for t in range(2):
+            for c in range(2):
+                nc.vector.tensor_copy(pairs[c][:, 1, :, t], kp[2 + t][:].indirect(offs_t[:, c * 16 : (c + 1) * 16]))
+        for c in range(2):
+            words = ki[c][:].rearrange("p n t -> p (n t)").bitcast(F32).rearrange("p (n u) -> p n u", u=2)
+            nc.scalar.copy(words, pairs[c][:].rearrange("p u n t -> p u (n t)").bitcast(F32).rearrange("p u n -> p n u"))
+
+        for a in range(QT):
+            nc.gpsimd.tensor_scalar(qi[:, a * P : (a + 1) * P, :], qf[:, :, a * P : (a + 1) * P].rearrange("p t n -> p n t"), 1.0, 0.0, ALU.mult, ALU.add)
+        nc.vector.tensor_copy(vp[0][:].indirect(slots_t[:]), newv[:, 0, :])
+        quantize(qc[:], qs[:], qi[:])
+        nc.scalar.activation(vb[:], vp[0][:], ACT.Copy)
+        vg = [share.tile([P, N], BF16, name="vg0", align_bytes=64, offset=512), keep.tile([P, N], BF16, name="vg1", tag="qc", align_bytes=64)]
+        nc.scalar.activation(vg[0][:], vb[:].indirect(offs_t[:]), ACT.Copy)
+
         ks = share.tile([P, N], U8, name="ks", align_bytes=64, offset=0)
-        nc.vector.quantize_mx(out=kc[:, 0:256].bitcast(FP8X4), scales=ks[:, 0:256], in_=ki[:, 0:256, :].rearrange("p n t -> p (n t)"))
-        nc.vector.quantize_mx(out=kc[:, 256:512].bitcast(FP8X4), scales=ks[:, 256:512], in_=ki[:, 256:512, :].rearrange("p n t -> p (n t)"))
-        vsc = keep.tile([P, PACK], F32, name="vsc", tag="ki", align_bytes=64)
-        nc.scalar.copy(vsc[:], vs_ps[:, :, 0])
-        nc.tensor.matmul_mx(s_ps[0][:, 0:256], lhsT=qc[:, 0:128].bitcast(FP8X4), lhsT_scale=qs[:, 0:128], rhs=kc[:, 0:256].bitcast(FP8X4), rhs_scale=ks[:, 0:256], start=True, stop=True)
-        nc.tensor.matmul_mx(s_ps[0][:, 256:512], lhsT=qc[:, 0:128].bitcast(FP8X4), lhsT_scale=qs[:, 0:128], rhs=kc[:, 256:512].bitcast(FP8X4), rhs_scale=ks[:, 256:512], start=True, stop=True)
-        nc.tensor.matmul_mx(s_ps[1][:], lhsT=qc[:, 128:256].bitcast(FP8X4), lhsT_scale=qs[:, 128:256], rhs=kc[:].bitcast(FP8X4), rhs_scale=ks[:], start=True, stop=True)
-        v_ps.append(psum.tile([P, 2, P], F32, name="v_ps0", tag="v_ps0"))
-        for u in range(2):
-            nc.tensor.transpose(v_ps[0][:, u, :], vg[0][:].bitcast(F32)[:, u : N // 2 : 2], ident_f[:])
-        nc.vector.tensor_reduce(nm[0][:], s_ps[0][:], axis=AXX, op=ALU.max, negate=True)
-        nc.scalar.activation(pt[0][:], s_ps[0][:].rearrange("q (s t) -> q t s", t=PACK), ACT.Exp, bias=nm[0][:], scale=1.0, accum_out=lt[:, 0:1])
-        for t in range(PACK):
-            nc.tensor.transpose(w_ps[0][:, t, :], pt[0][:, t, :], ident_f[:])
-        nc.vector.tensor_reduce(nm[1], s_ps[1][:], axis=AXX, op=ALU.max, negate=True)
-        nc.scalar.activation(pt[1][:], s_ps[1][:].rearrange("q (s t) -> q t s", t=PACK), ACT.Exp, bias=nm[1], scale=1.0, accum_out=lt[:, 1:2])
-        for t in range(PACK):
-            nc.tensor.transpose(w_ps[1][:, t, :], pt[1][:, t, :], ident_f[:])
+        for c in range(2):
+            cols = slice(c * HALF, (c + 1) * HALF)
+            quantize(kc[:, cols], ks[:, cols], ki[c][:])
+            product(s_ps[0][:, cols], qc[:, 0:P], qs[:, 0:P], kc[:, cols], ks[:, cols])
+        product(s_ps[1][:], qc[:, P:NQ], qs[:, P:NQ], kc[:], ks[:])
         nc.vector.tensor_copy(vp[1][:].indirect(slots_t[:]), newv[:, 1, :])
-        vg.append(keep.tile([P, N], BF16, name="vg1", tag="qc", align_bytes=64))
+
+        vsc = keep.tile([P, PACK], F32, name="vsc", tag="ki1", align_bytes=64)
+        nc.scalar.copy(vsc[:], vs_ps[:, :, 0])
+
+        v_ps = [psum.tile([P, 2, P], F32, name="v_ps0"), psum.tile([P, 2, P], F32, name="v_ps1", tag="s_ps1")]
+
+        def turn_values(h):
+            for u in range(2):
+                nc.tensor.transpose(v_ps[h][:, u, :], vg[h][:].bitcast(F32)[:, u : N // 2 : 2], ident_f[:])
+
+        turn_values(0)
+        for a in range(QT):
+            nc.vector.tensor_reduce(nm[a], s_ps[a][:], axis=AXX, op=ALU.max, negate=True)
+            nc.scalar.activation(pt[a][:], s_ps[a][:].rearrange("q (s t) -> q t s", t=PACK), ACT.Exp, bias=nm[a], scale=1.0, accum_out=lt[:, a : a + 1])
+            for t in range(PACK):
+                nc.tensor.transpose(w_ps[a][:, t, :], pt[a][:, t, :], ident_f[:])
         nc.vector.tensor_copy(vg[1][:], vp[1][:].indirect(offs_t[:]))
-        v_ps.append(psum.tile([P, 2, P], F32, name="v_ps1", tag="s_ps1"))
-        for u in range(2):
-            nc.tensor.transpose(v_ps[1][:, u, :], vg[1][:].bitcast(F32)[:, u : N // 2 : 2], ident_f[:])
-        vi = share.tile([P, DV, PACK], BF16, name="vi", align_bytes=64, offset=2048)
-        nc.scalar.copy(vi[:, 0:128, :].rearrange("p n t -> p (n t)").bitcast(F32).rearrange("s (e u) -> s e u", u=2), v_ps[0][:].rearrange("s u e -> s e u"))
-        th = share.tile([P, QT, DV], F32, name="th", align_bytes=64, offset=4096)
+        turn_values(1)
+
+        def weave_values(h):
+            nc.scalar.copy(vi[h][:].rearrange("p n t -> p (n t)").bitcast(F32).rearrange("s (e u) -> s e u", u=2), v_ps[h][:].rearrange("s u e -> s e u"))
+
+        weave_values(0)
         nc.scalar.activation(th[:], og_t[:], ACT.Tanh, scale=0.5)
-        nc.scalar.copy(vi[:, 128:256, :].rearrange("p n t -> p (n t)").bitcast(F32).rearrange("s (e u) -> s e u", u=2), v_ps[1][:].rearrange("s u e -> s e u"))
+        weave_values(1)
         gate = keep.tile([P, QT, DV], F32, name="gate", tag="qc", align_bytes=64)
         nc.scalar.activation(gate[:], th[:], ACT.Copy, scale=0.5, bias=0.5)
         nc.vector.reciprocal(rl[:], lt[:])
         nc.vector.tensor_tensor(wi[0][:], w_ps[0][:].rearrange("s t q -> s q t"), vsc[:].unsqueeze(1).to_broadcast([P, P, PACK]), ALU.mult)
-        nc.vector.quantize_mx(out=vc[:, 0:128].bitcast(FP8X4), scales=vsx[:, 0:128], in_=vi[:, 0:128, :].rearrange("p n t -> p (n t)"))
+        quantize(vc[:, 0:P], vsx[:, 0:P], vi[0][:])
         nc.vector.tensor_tensor(wi[1][:], w_ps[1][:].rearrange("s t q -> s q t"), vsc[:].unsqueeze(1).to_broadcast([P, P, PACK]), ALU.mult)
-        nc.vector.quantize_mx(out=wc[0][:].bitcast(FP8X4), scales=ws[0][:], in_=wi[0][:].rearrange("p n t -> p (n t)"))
-        nc.vector.quantize_mx(out=wc[1][:].bitcast(FP8X4), scales=ws[1][:], in_=wi[1][:].rearrange("p n t -> p (n t)"))
-        nc.vector.quantize_mx(out=vc[:, 128:256].bitcast(FP8X4), scales=vsx[:, 128:256], in_=vi[:, 128:256, :].rearrange("p n t -> p (n t)"))
-        nc.tensor.matmul_mx(y_ps[0][:, 0:128], lhsT=wc[0][:].bitcast(FP8X4), lhsT_scale=ws[0][:], rhs=vc[:, 0:128].bitcast(FP8X4), rhs_scale=vsx[:, 0:128], start=True, stop=True)
-        nc.tensor.matmul_mx(y_ps[0][:, 128:256], lhsT=wc[0][:].bitcast(FP8X4), lhsT_scale=ws[0][:], rhs=vc[:, 128:256].bitcast(FP8X4), rhs_scale=vsx[:, 128:256], start=True, stop=True)
-        nc.tensor.matmul_mx(y_ps[1][:, 0:128], lhsT=wc[1][:].bitcast(FP8X4), lhsT_scale=ws[1][:], rhs=vc[:, 0:128].bitcast(FP8X4), rhs_scale=vsx[:, 0:128], start=True, stop=True)
-        nc.tensor.matmul_mx(y_ps[1][:, 128:256], lhsT=wc[1][:].bitcast(FP8X4), lhsT_scale=ws[1][:], rhs=vc[:, 128:256].bitcast(FP8X4), rhs_scale=vsx[:, 128:256], start=True, stop=True)
-        nc.vector.scalar_tensor_tensor(res[0][:], y_ps[0][:], rl[:, 0:1], gate[:, 0, :], ALU.mult, ALU.mult)
-        nc.sync.dma_start(oview[0], res[0][:])
-        nc.vector.scalar_tensor_tensor(res[1][:], y_ps[1][:], rl[:, 1:2], gate[:, 1, :], ALU.mult, ALU.mult)
-        nc.sync.dma_start(oview[1], res[1][:])
+        for a in range(QT):
+            quantize(wc[a][:], ws[a][:], wi[a][:])
+        quantize(vc[:, P:DV], vsx[:, P:DV], vi[1][:])
+        for a in range(QT):
+            for h in range(ET):
+                cols = slice(h * P, (h + 1) * P)
+                product(y_ps[a][:, cols], wc[a][:], ws[a][:], vc[:, cols], vsx[:, cols])
+        for a in range(QT):
+            nc.vector.scalar_tensor_tensor(res[a][:], y_ps[a][:], rl[:, a : a + 1], gate[:, a, :], ALU.mult, ALU.mult)
+            nc.sync.dma_start(oview[a], res[a][:])

@@ -45,12 +45,12 @@ def tile_attend_x_append128_gate_topk_kernel(tc, qT, kT, vT, new_kT, new_vT, vs,
         newk0 = keep.tile([P, NEW], F32, name="newk0")
         newk = keep.tile([P, PACK - 1, NEW], F32, name="newk", tag="newk")
         newv = keep.tile([P, ET, NEW], F32, name="newv")
-        qf = keep.tile([P, PACK, NQ], F32, name="qf")
+        qf = share.tile([P, PACK, NQ], F32, name="qf", align_bytes=64, offset=0)
         vs_t = keep.tile([P, T], F32, name="vs_t")
         og_t = keep.tile([P, QT, DV], F32, name="og_t")
         pairs = [keep.tile([P, 2, HALF, 2], BF16, name=f"pairs{c}") for c in range(2)]
         ki = [keep.tile([P, HALF, PACK], BF16, name=f"ki{c}", tag=f"ki{c}", align_bytes=64) for c in range(2)]
-        qi = share.tile([P, NQ, PACK], BF16, name="qi", align_bytes=64, offset=0)
+        qi = keep.tile([P, NQ, PACK], BF16, name="qi", align_bytes=64)
         qc = keep.tile([P, NQ], U32, name="qc", tag="qc", align_bytes=64)
         qs = keep.tile([P, NQ], U8, name="qs", align_bytes=64)
         vb = keep.tile([P, T], BF16, name="vb")
@@ -62,9 +62,8 @@ def tile_attend_x_append128_gate_topk_kernel(tc, qT, kT, vT, new_kT, new_vT, vs,
         th = share.tile([P, QT, DV], F32, name="th", align_bytes=64, offset=6144)
         nm = [keep.tile([P, 1], F32, name="nm0")[:], share.tile([P, 32], F32, name="nm1", align_bytes=64, offset=6144 - 64)[:, 0:1]]
         lt = keep.tile([P, QT], F32, name="lt")
-        rl = keep.tile([P, QT], F32, name="rl")
         pt = [keep.tile([P, PACK, P], F32, name=f"pt{a}") for a in range(QT)]
-        wi = [keep.tile([P, P, PACK], BF16, name=f"wi{a}", align_bytes=64) for a in range(QT)]
+        wi = [keep.tile([P, P, PACK], BF16, name=f"wi{a}", tag=f"wi{a}", align_bytes=64) for a in range(QT)]
         wc = [keep.tile([P, P], U32, name=f"wc{a}", align_bytes=64) for a in range(QT)]
         ws = [keep.tile([P, P], U8, name=f"ws{a}", align_bytes=64) for a in range(QT)]
         res = [keep.tile([P, DV], F32, name=f"res{a}") for a in range(QT)]
@@ -85,7 +84,7 @@ def tile_attend_x_append128_gate_topk_kernel(tc, qT, kT, vT, new_kT, new_vT, vs,
         nc.sync.dma_start(newk0[:], nkview[:, 0, :])
         nc.sync.dma_start(offs_t[:], offs)
         nc.sync.dma_start(newk[:], nkview[:, 1:PACK, :])
-        nc.gpsimd.memset(vs_t[:], 0.0)
+        nc.vector.memset(vs_t[:], 0.0)
         nc.sync.dma_start(vs_t[0:1, :], vs[0:1, :])
         for t in range(1, PACK):
             nc.sync.dma_start(kp[t][:], kview[:, t, :])
@@ -121,7 +120,7 @@ def tile_attend_x_append128_gate_topk_kernel(tc, qT, kT, vT, new_kT, new_vT, vs,
         nc.vector.tensor_copy(vp[0][:].indirect(slots_t[:]), newv[:, 0, :])
         quantize(qc[:], qs[:], qi[:])
         nc.scalar.activation(vb[:], vp[0][:], ACT.Copy)
-        vg = [share.tile([P, N], BF16, name="vg0", align_bytes=64, offset=512), keep.tile([P, N], BF16, name="vg1", tag="qc", align_bytes=64)]
+        vg = [keep.tile([P, N], BF16, name="vg0", align_bytes=64), keep.tile([P, N], BF16, name="vg1", tag="qc", align_bytes=64)]
         nc.scalar.activation(vg[0][:], vb[:].indirect(offs_t[:]), ACT.Copy)
 
         ks = share.tile([P, N], U8, name="ks", align_bytes=64, offset=0)
@@ -158,13 +157,14 @@ def tile_attend_x_append128_gate_topk_kernel(tc, qT, kT, vT, new_kT, new_vT, vs,
         weave_values(1)
         gate = keep.tile([P, QT, DV], F32, name="gate", tag="qc", align_bytes=64)
         nc.scalar.activation(gate[:], th[:], ACT.Copy, scale=0.5, bias=0.5)
-        nc.vector.reciprocal(rl[:], lt[:])
         nc.vector.tensor_tensor(wi[0][:], w_ps[0][:].rearrange("s t q -> s q t"), vsc[:].unsqueeze(1).to_broadcast([P, P, PACK]), ALU.mult)
         quantize(vc[:, 0:P], vsx[:, 0:P], vi[0][:])
         nc.vector.tensor_tensor(wi[1][:], w_ps[1][:].rearrange("s t q -> s q t"), vsc[:].unsqueeze(1).to_broadcast([P, P, PACK]), ALU.mult)
         for a in range(QT):
             quantize(wc[a][:], ws[a][:], wi[a][:])
         quantize(vc[:, P:DV], vsx[:, P:DV], vi[1][:])
+        rl = keep.tile([P, QT], F32, name="rl", tag="wi0", align_bytes=64)
+        nc.vector.reciprocal(rl[:], lt[:])
         for a in range(QT):
             for h in range(ET):
                 cols = slice(h * P, (h + 1) * P)

@@ -19,7 +19,7 @@ PACK = 4
 QT = NQ // P
 ET = DV // P
 HALF = N // 2
-CAST_SPLIT = 688
+CAST_SPLIT = 320
 
 FLOPS = 2 * NQ * N * (D + DV)
 
@@ -102,6 +102,8 @@ def tile_attend_x_append128_gate_topk_kernel(tc, qT, kT, vT, new_kT, new_vT, vs,
         nc.vector.tensor_copy(vsg[:], vs_t[:].indirect(offs_t[:]))
         for t in range(PACK):
             nc.tensor.transpose(vs_ps[:, t, :], vsg[:].rearrange("p (s t) -> p t s", t=PACK)[:, t, :], ident_f[:])
+        vsc = keep.tile([P, PACK], F32, name="vsc")
+        nc.scalar.copy(vsc[:], vs_ps[:, :, 0])
         for t in range(1, PACK):
             nc.vector.tensor_copy(kp[t][:].indirect(slots_t[:]), newk[:, t - 1, :])
         for t in range(2):
@@ -119,7 +121,8 @@ def tile_attend_x_append128_gate_topk_kernel(tc, qT, kT, vT, new_kT, new_vT, vs,
             nc.gpsimd.tensor_scalar(qi[:, a * P : (a + 1) * P, :], qf[:, :, a * P : (a + 1) * P].rearrange("p t n -> p n t"), 1.0, 0.0, ALU.mult, ALU.add)
         nc.vector.tensor_copy(vp[0][:].indirect(slots_t[:]), newv[:, 0, :])
         quantize(qc[:], qs[:], qi[:])
-        nc.scalar.activation(vb[:], vp[0][:], ACT.Copy)
+        nc.vector.tensor_copy(vb[:, :CAST_SPLIT], vp[0][:, :CAST_SPLIT])
+        nc.scalar.activation(vb[:, CAST_SPLIT:], vp[0][:, CAST_SPLIT:], ACT.Copy)
         vg = [keep.tile([P, N], BF16, name="vg0", align_bytes=64), keep.tile([P, N], BF16, name="vg1", tag="qc", align_bytes=64)]
         nc.scalar.activation(vg[0][:], vb[:].indirect(offs_t[:]), ACT.Copy)
 
@@ -131,8 +134,6 @@ def tile_attend_x_append128_gate_topk_kernel(tc, qT, kT, vT, new_kT, new_vT, vs,
         product(s_ps[1][:], qc[:, P:NQ], qs[:, P:NQ], kc[:], ks[:])
         nc.vector.tensor_copy(vp[1][:].indirect(slots_t[:]), newv[:, 1, :])
 
-        vsc = keep.tile([P, PACK], F32, name="vsc", tag="ki1", align_bytes=64)
-        nc.scalar.copy(vsc[:], vs_ps[:, :, 0])
 
         v_ps = [psum.tile([P, 2, P], F32, name="v_ps0"), psum.tile([P, 2, P], F32, name="v_ps1", tag="s_ps1")]
 

@@ -16,10 +16,16 @@ AXX = mybir.AxisListType.X
 D, DV, T, N, NQ, NEW = 512, 256, 1024, 512, 256, 128
 P = 128
 PACK = 4
+PAIR = 2
+LIST_ROWS = 16
 QT = NQ // P
 ET = DV // P
 HALF = N // 2
 CAST_SPLIT = 320
+AT_QUERIES = 0
+AT_WOVEN_VALUES = 5120
+AT_TANH = 6144
+MX_ALIGN = 64
 
 FLOPS = 2 * NQ * N * (D + DV)
 
@@ -27,149 +33,170 @@ FLOPS = 2 * NQ * N * (D + DV)
 def tile_attend_x_append128_gate_topk_kernel(tc, qT, kT, vT, new_kT, new_vT, vs, og, offs, slots, out):
     nc = tc.nc
 
-    def quantize(codes, scales, words):
-        nc.vector.quantize_mx(out=codes.bitcast(FP8X4), scales=scales, in_=words.rearrange("p n t -> p (n t)"))
+    def quantize(codes, scales, woven):
+        nc.vector.quantize_mx(out=codes.bitcast(FP8X4), scales=scales, in_=woven.rearrange("p n t -> p (n t)"))
 
     def product(acc, lhs_codes, lhs_scales, rhs_codes, rhs_scales):
-        nc.tensor.matmul_mx(acc, lhsT=lhs_codes.bitcast(FP8X4), lhsT_scale=lhs_scales, rhs=rhs_codes.bitcast(FP8X4), rhs_scale=rhs_scales, start=True, stop=True)
+        nc.tensor.matmul_mx(
+            acc, lhsT=lhs_codes.bitcast(FP8X4), lhsT_scale=lhs_scales, rhs=rhs_codes.bitcast(FP8X4), rhs_scale=rhs_scales, start=True, stop=True
+        )
+
+    def as_words(woven):
+        return woven.rearrange("p n t -> p (n t)").bitcast(F32).rearrange("p (n u) -> p n u", u=PACK // PAIR)
 
     with ExitStack() as ctx:
         keep = ctx.enter_context(tc.tile_pool(name="keep", bufs=1))
-        share = ctx.enter_context(tc.tile_pool(name="share", bufs=1))
+        overlap = ctx.enter_context(tc.tile_pool(name="overlap", bufs=1))
         psum = ctx.enter_context(tc.psum_pool(name="psum", bufs=1))
-        slots_t = keep.tile([P, NEW // 16], U16, name="slots_t")
-        offs_t = keep.tile([P, N // 16], U16, name="offs_t")
-        kp = [keep.tile([P, T], F32, name=f"kp{t}") for t in range(PACK)]
-        kb = [keep.tile([P, T], BF16, name=f"kb{t}") for t in range(2)]
-        vp = [keep.tile([P, T], F32, name=f"vp{h}") for h in range(ET)]
-        newk0 = keep.tile([P, NEW], F32, name="newk0")
-        newk = keep.tile([P, PACK - 1, NEW], F32, name="newk", tag="newk")
-        newv = keep.tile([P, ET, NEW], F32, name="newv")
-        qf = share.tile([P, PACK, NQ], F32, name="qf", align_bytes=64, offset=0)
+
+        slots_t = keep.tile([P, NEW // LIST_ROWS], U16, name="slots_t")
+        offs_t = keep.tile([P, N // LIST_ROWS], U16, name="offs_t")
+        k_plane = [keep.tile([P, T], F32, name=f"k_plane{t}") for t in range(PACK)]
+        k_cast = [keep.tile([P, T], BF16, name=f"k_cast{t}") for t in range(PAIR)]
+        v_tile = [keep.tile([P, T], F32, name=f"v_tile{h}") for h in range(ET)]
+        new_k_first = keep.tile([P, NEW], F32, name="new_k_first")
+        new_k_rest = keep.tile([P, PACK - 1, NEW], F32, name="new_k_rest")
+        new_v = keep.tile([P, ET, NEW], F32, name="new_v")
+        q_planes = overlap.tile([P, PACK, NQ], F32, name="q_planes", align_bytes=MX_ALIGN, offset=AT_QUERIES)
         vs_t = keep.tile([P, T], F32, name="vs_t")
         og_t = keep.tile([P, QT, DV], F32, name="og_t")
-        pairs = [keep.tile([P, 2, HALF, 2], BF16, name=f"pairs{c}") for c in range(2)]
-        ki = [keep.tile([P, HALF, PACK], BF16, name=f"ki{c}", tag=f"ki{c}", align_bytes=64) for c in range(2)]
-        qi = keep.tile([P, NQ, PACK], BF16, name="qi", align_bytes=64)
-        qc = keep.tile([P, NQ], U32, name="qc", tag="qc", align_bytes=64)
-        qs = keep.tile([P, NQ], U8, name="qs", align_bytes=64)
-        vb = keep.tile([P, T], BF16, name="vb")
-        kc = keep.tile([P, N], U32, name="kc", align_bytes=64)
-        vsg = keep.tile([P, N], F32, name="vsg")
-        vi = [share.tile([P, P, PACK], BF16, name="vi0", align_bytes=64, offset=5120), keep.tile([P, P, PACK], BF16, name="vi1", align_bytes=64)]
-        vc = keep.tile([P, DV], U32, name="vc", align_bytes=64)
-        vsx = keep.tile([P, DV], U8, name="vsx", align_bytes=64)
-        th = share.tile([P, QT, DV], F32, name="th", align_bytes=64, offset=6144)
-        nm = [keep.tile([P, 1], F32, name="nm0")[:], share.tile([P, 32], F32, name="nm1", align_bytes=64, offset=6144 - 64)[:, 0:1]]
-        lt = keep.tile([P, QT], F32, name="lt")
-        pt = [keep.tile([P, PACK, P], F32, name=f"pt{a}") for a in range(QT)]
-        wi = [keep.tile([P, P, PACK], BF16, name=f"wi{a}", tag=f"wi{a}", align_bytes=64) for a in range(QT)]
-        wc = [keep.tile([P, P], U32, name=f"wc{a}", align_bytes=64) for a in range(QT)]
-        ws = [keep.tile([P, P], U8, name=f"ws{a}", align_bytes=64) for a in range(QT)]
-        res = [keep.tile([P, DV], F32, name=f"res{a}") for a in range(QT)]
-        warm = keep.tile([P, 1], F32, name="warm")
-        warm_out = keep.tile([P, 1], F32, name="warm_out")
-        ident_f = keep.tile([P, P], F32, name="ident_f")
-        s_ps = [psum.tile([P, N], F32, name=f"s_ps{a}", tag=f"s_ps{a}") for a in range(QT)]
-        w_ps = [psum.tile([P, PACK, P], F32, name=f"w_ps{a}") for a in range(QT)]
+        k_pairs = [keep.tile([P, PACK // PAIR, HALF, PAIR], BF16, name=f"k_pairs{c}") for c in range(2)]
+        k_woven = [keep.tile([P, HALF, PACK], BF16, name=f"k_woven{c}", align_bytes=MX_ALIGN) for c in range(2)]
+        q_woven = keep.tile([P, NQ, PACK], BF16, name="q_woven", align_bytes=MX_ALIGN)
+        q_codes = keep.tile([P, NQ], U32, name="q_codes", tag="q_codes", align_bytes=MX_ALIGN)
+        q_scales = keep.tile([P, NQ], U8, name="q_scales", align_bytes=MX_ALIGN)
+        v_cast = keep.tile([P, T], BF16, name="v_cast")
+        k_codes = keep.tile([P, N], U32, name="k_codes", align_bytes=MX_ALIGN)
+        vs_row = keep.tile([P, N], F32, name="vs_row")
+        v_woven = [
+            overlap.tile([P, P, PACK], BF16, name="v_woven0", align_bytes=MX_ALIGN, offset=AT_WOVEN_VALUES),
+            keep.tile([P, P, PACK], BF16, name="v_woven1", align_bytes=MX_ALIGN),
+        ]
+        v_codes = keep.tile([P, DV], U32, name="v_codes", align_bytes=MX_ALIGN)
+        v_scales = keep.tile([P, DV], U8, name="v_scales", align_bytes=MX_ALIGN)
+        tanh_t = overlap.tile([P, QT, DV], F32, name="tanh_t", align_bytes=MX_ALIGN, offset=AT_TANH)
+        neg_max = [
+            keep.tile([P, 1], F32, name="neg_max0")[:],
+            overlap.tile([P, 2 * MX_ALIGN // 4], F32, name="neg_max1", align_bytes=MX_ALIGN, offset=AT_TANH - MX_ALIGN)[:, 0:1],
+        ]
+        row_sum = keep.tile([P, QT], F32, name="row_sum")
+        p_t = [keep.tile([P, PACK, P], F32, name=f"p_t{a}") for a in range(QT)]
+        w_woven = [keep.tile([P, P, PACK], BF16, name=f"w_woven{a}", tag=f"w_woven{a}", align_bytes=MX_ALIGN) for a in range(QT)]
+        w_codes = [keep.tile([P, P], U32, name=f"w_codes{a}", align_bytes=MX_ALIGN) for a in range(QT)]
+        w_scales = [keep.tile([P, P], U8, name=f"w_scales{a}", align_bytes=MX_ALIGN) for a in range(QT)]
+        result = [keep.tile([P, DV], F32, name=f"result{a}") for a in range(QT)]
+        identity = keep.tile([P, P], F32, name="identity")
+        score_ps = [psum.tile([P, N], F32, name=f"score_ps{a}", tag=f"score_ps{a}") for a in range(QT)]
+        p_ps = [psum.tile([P, PACK, P], F32, name=f"p_ps{a}") for a in range(QT)]
         y_ps = [psum.tile([P, DV], F32, name=f"y_ps{a}") for a in range(QT)]
         vs_ps = psum.tile([P, PACK, P], F32, name="vs_ps")
-        kview = kT.rearrange("(p t) n -> p t n", t=PACK)
-        nkview = new_kT.rearrange("(p t) n -> p t n", t=PACK)
-        vview = vT.rearrange("(h p) n -> p h n", p=P)
-        oview = out[0].rearrange("(a p) e -> a p e", p=P)
 
-        nc.sync.dma_start(kp[0][:], kview[:, 0, :])
+        k_rows = kT.rearrange("(p t) n -> p t n", t=PACK)
+        new_k_rows = new_kT.rearrange("(p t) n -> p t n", t=PACK)
+        v_rows = vT.rearrange("(h p) n -> p h n", p=P)
+        out_rows = out[0].rearrange("(a p) e -> a p e", p=P)
+        offs_half = [offs_t[:, c * HALF // LIST_ROWS : (c + 1) * HALF // LIST_ROWS] for c in range(2)]
+
+        nc.sync.dma_start(k_plane[0][:], k_rows[:, 0, :])
         nc.sync.dma_start(slots_t[:], slots)
-        nc.sync.dma_start(newk0[:], nkview[:, 0, :])
+        nc.sync.dma_start(new_k_first[:], new_k_rows[:, 0, :])
         nc.sync.dma_start(offs_t[:], offs)
-        nc.sync.dma_start(newk[:], nkview[:, 1:PACK, :])
+        nc.sync.dma_start(new_k_rest[:], new_k_rows[:, 1:PACK, :])
         nc.vector.memset(vs_t[:], 0.0)
         nc.sync.dma_start(vs_t[0:1, :], vs[0:1, :])
         for t in range(1, PACK):
-            nc.sync.dma_start(kp[t][:], kview[:, t, :])
-        nc.sync.dma_start(newv[:], new_vT.rearrange("(h p) n -> p h n", p=P))
-        nc.sync.dma_start(qf[:], qT[0].rearrange("(p t) n -> p t n", t=PACK))
+            nc.sync.dma_start(k_plane[t][:], k_rows[:, t, :])
+        nc.sync.dma_start(new_v[:], new_vT.rearrange("(h p) n -> p h n", p=P))
+        nc.sync.dma_start(q_planes[:], qT[0].rearrange("(p t) n -> p t n", t=PACK))
         for h in range(ET):
-            nc.sync.dma_start(vp[h][:], vview[:, h, :])
+            nc.sync.dma_start(v_tile[h][:], v_rows[:, h, :])
         nc.sync.dma_start(og_t[:], og[0].rearrange("(a p) e -> p a e", p=P))
 
-        nc.gpsimd.memset(warm[:], 0.0)
-        nc.scalar.activation(warm_out[:], warm[:], ACT.Exp)
-        make_identity(nc, ident_f[:])
+        make_identity(nc, identity[:])
 
-        nc.vector.tensor_copy(kp[0][:].indirect(slots_t[:]), newk0[:])
-        nc.vector.tensor_copy(vsg[:], vs_t[:].indirect(offs_t[:]))
+        nc.vector.tensor_copy(k_plane[0][:].indirect(slots_t[:]), new_k_first[:])
+        nc.vector.tensor_copy(vs_row[:], vs_t[:].indirect(offs_t[:]))
         for t in range(PACK):
-            nc.tensor.transpose(vs_ps[:, t, :], vsg[:].rearrange("p (s t) -> p t s", t=PACK)[:, t, :], ident_f[:])
-        vsc = keep.tile([P, PACK], F32, name="vsc")
-        nc.scalar.copy(vsc[:], vs_ps[:, :, 0])
+            nc.tensor.transpose(vs_ps[:, t, :], vs_row[:].rearrange("p (s t) -> p t s", t=PACK)[:, t, :], identity[:])
+        vs_col = keep.tile([P, PACK], F32, name="vs_col")
+        nc.scalar.copy(vs_col[:], vs_ps[:, :, 0])
         for t in range(1, PACK):
-            nc.vector.tensor_copy(kp[t][:].indirect(slots_t[:]), newk[:, t - 1, :])
-        for t in range(2):
-            nc.scalar.activation(kb[t][:], kp[t][:], ACT.Copy)
+            nc.vector.tensor_copy(k_plane[t][:].indirect(slots_t[:]), new_k_rest[:, t - 1, :])
+
+        for j in range(PAIR):
+            nc.scalar.activation(k_cast[j][:], k_plane[j][:], ACT.Copy)
             for c in range(2):
-                nc.scalar.activation(pairs[c][:, 0, :, t], kb[t][:].indirect(offs_t[:, c * 16 : (c + 1) * 16]), ACT.Copy)
-        for t in range(2):
+                nc.scalar.activation(k_pairs[c][:, 0, :, j], k_cast[j][:].indirect(offs_half[c]), ACT.Copy)
+        for j in range(PAIR):
             for c in range(2):
-                nc.vector.tensor_copy(pairs[c][:, 1, :, t], kp[2 + t][:].indirect(offs_t[:, c * 16 : (c + 1) * 16]))
+                nc.vector.tensor_copy(k_pairs[c][:, 1, :, j], k_plane[PAIR + j][:].indirect(offs_half[c]))
         for c in range(2):
-            words = ki[c][:].rearrange("p n t -> p (n t)").bitcast(F32).rearrange("p (n u) -> p n u", u=2)
-            nc.scalar.copy(words, pairs[c][:].rearrange("p u n t -> p u (n t)").bitcast(F32).rearrange("p u n -> p n u"))
+            nc.scalar.copy(as_words(k_woven[c][:]), k_pairs[c][:].rearrange("p u n j -> p u (n j)").bitcast(F32).rearrange("p u n -> p n u"))
 
         for a in range(QT):
-            nc.gpsimd.tensor_scalar(qi[:, a * P : (a + 1) * P, :], qf[:, :, a * P : (a + 1) * P].rearrange("p t n -> p n t"), 1.0, 0.0, ALU.mult, ALU.add)
-        nc.vector.tensor_copy(vp[0][:].indirect(slots_t[:]), newv[:, 0, :])
-        quantize(qc[:], qs[:], qi[:])
-        nc.vector.tensor_copy(vb[:, :CAST_SPLIT], vp[0][:, :CAST_SPLIT])
-        nc.scalar.activation(vb[:, CAST_SPLIT:], vp[0][:, CAST_SPLIT:], ACT.Copy)
-        vg = [keep.tile([P, N], BF16, name="vg0", align_bytes=64), keep.tile([P, N], BF16, name="vg1", tag="qc", align_bytes=64)]
-        nc.scalar.activation(vg[0][:], vb[:].indirect(offs_t[:]), ACT.Copy)
+            rows = slice(a * P, (a + 1) * P)
+            nc.gpsimd.tensor_scalar(q_woven[:, rows, :], q_planes[:, :, rows].rearrange("p t n -> p n t"), 1.0, 0.0, ALU.mult, ALU.add)
 
-        ks = share.tile([P, N], U8, name="ks", align_bytes=64, offset=0)
+        nc.vector.tensor_copy(v_tile[0][:].indirect(slots_t[:]), new_v[:, 0, :])
+        quantize(q_codes[:], q_scales[:], q_woven[:])
+        nc.vector.tensor_copy(v_cast[:, :CAST_SPLIT], v_tile[0][:, :CAST_SPLIT])
+        nc.scalar.activation(v_cast[:, CAST_SPLIT:], v_tile[0][:, CAST_SPLIT:], ACT.Copy)
+        v_picked = [
+            keep.tile([P, N], BF16, name="v_picked0", align_bytes=MX_ALIGN),
+            keep.tile([P, N], BF16, name="v_picked1", tag="q_codes", align_bytes=MX_ALIGN),
+        ]
+        nc.scalar.activation(v_picked[0][:], v_cast[:].indirect(offs_t[:]), ACT.Copy)
+
+        k_scales = overlap.tile([P, N], U8, name="k_scales", align_bytes=MX_ALIGN, offset=AT_QUERIES)
         for c in range(2):
             cols = slice(c * HALF, (c + 1) * HALF)
-            quantize(kc[:, cols], ks[:, cols], ki[c][:])
-            product(s_ps[0][:, cols], qc[:, 0:P], qs[:, 0:P], kc[:, cols], ks[:, cols])
-        product(s_ps[1][:], qc[:, P:NQ], qs[:, P:NQ], kc[:], ks[:])
-        nc.vector.tensor_copy(vp[1][:].indirect(slots_t[:]), newv[:, 1, :])
+            quantize(k_codes[:, cols], k_scales[:, cols], k_woven[c][:])
+            product(score_ps[0][:, cols], q_codes[:, 0:P], q_scales[:, 0:P], k_codes[:, cols], k_scales[:, cols])
+        product(score_ps[1][:], q_codes[:, P:NQ], q_scales[:, P:NQ], k_codes[:], k_scales[:])
+        nc.vector.tensor_copy(v_tile[1][:].indirect(slots_t[:]), new_v[:, 1, :])
 
-
-        v_ps = [psum.tile([P, 2, P], F32, name="v_ps0"), psum.tile([P, 2, P], F32, name="v_ps1", tag="s_ps1")]
+        v_ps = [psum.tile([P, PACK // PAIR, P], F32, name="v_ps0"), psum.tile([P, PACK // PAIR, P], F32, name="v_ps1", tag="score_ps1")]
 
         def turn_values(h):
-            for u in range(2):
-                nc.tensor.transpose(v_ps[h][:, u, :], vg[h][:].bitcast(F32)[:, u : N // 2 : 2], ident_f[:])
+            for u in range(PACK // PAIR):
+                nc.tensor.transpose(v_ps[h][:, u, :], v_picked[h][:].bitcast(F32)[:, u : N // PAIR : PACK // PAIR], identity[:])
+
+        def weave_values(h):
+            nc.scalar.copy(as_words(v_woven[h][:]), v_ps[h][:].rearrange("s u e -> s e u"))
+
+        def weigh(a):
+            nc.vector.tensor_tensor(w_woven[a][:], p_ps[a][:].rearrange("s t q -> s q t"), vs_col[:].unsqueeze(1).to_broadcast([P, P, PACK]), ALU.mult)
 
         turn_values(0)
         for a in range(QT):
-            nc.vector.tensor_reduce(nm[a], s_ps[a][:], axis=AXX, op=ALU.max, negate=True)
-            nc.scalar.activation(pt[a][:], s_ps[a][:].rearrange("q (s t) -> q t s", t=PACK), ACT.Exp, bias=nm[a], scale=1.0, accum_out=lt[:, a : a + 1])
+            nc.vector.tensor_reduce(neg_max[a], score_ps[a][:], axis=AXX, op=ALU.max, negate=True)
+            nc.scalar.activation(
+                p_t[a][:], score_ps[a][:].rearrange("q (s t) -> q t s", t=PACK), ACT.Exp, bias=neg_max[a], scale=1.0, accum_out=row_sum[:, a : a + 1]
+            )
             for t in range(PACK):
-                nc.tensor.transpose(w_ps[a][:, t, :], pt[a][:, t, :], ident_f[:])
-        nc.vector.tensor_copy(vg[1][:], vp[1][:].indirect(offs_t[:]))
+                nc.tensor.transpose(p_ps[a][:, t, :], p_t[a][:, t, :], identity[:])
+        nc.vector.tensor_copy(v_picked[1][:], v_tile[1][:].indirect(offs_t[:]))
         turn_values(1)
 
-        def weave_values(h):
-            nc.scalar.copy(vi[h][:].rearrange("p n t -> p (n t)").bitcast(F32).rearrange("s (e u) -> s e u", u=2), v_ps[h][:].rearrange("s u e -> s e u"))
-
         weave_values(0)
-        nc.scalar.activation(th[:], og_t[:], ACT.Tanh, scale=0.5)
+        nc.scalar.activation(tanh_t[:], og_t[:], ACT.Tanh, scale=0.5)
         weave_values(1)
-        gate = keep.tile([P, QT, DV], F32, name="gate", tag="qc", align_bytes=64)
-        nc.scalar.activation(gate[:], th[:], ACT.Copy, scale=0.5, bias=0.5)
-        nc.vector.tensor_tensor(wi[0][:], w_ps[0][:].rearrange("s t q -> s q t"), vsc[:].unsqueeze(1).to_broadcast([P, P, PACK]), ALU.mult)
-        quantize(vc[:, 0:P], vsx[:, 0:P], vi[0][:])
-        nc.vector.tensor_tensor(wi[1][:], w_ps[1][:].rearrange("s t q -> s q t"), vsc[:].unsqueeze(1).to_broadcast([P, P, PACK]), ALU.mult)
+        gate = keep.tile([P, QT, DV], F32, name="gate", tag="q_codes", align_bytes=MX_ALIGN)
+        nc.scalar.activation(gate[:], tanh_t[:], ACT.Copy, scale=0.5, bias=0.5)
+
+        weigh(0)
+        quantize(v_codes[:, 0:P], v_scales[:, 0:P], v_woven[0][:])
+        weigh(1)
         for a in range(QT):
-            quantize(wc[a][:], ws[a][:], wi[a][:])
-        quantize(vc[:, P:DV], vsx[:, P:DV], vi[1][:])
-        rl = keep.tile([P, QT], F32, name="rl", tag="wi0", align_bytes=64)
-        nc.vector.reciprocal(rl[:], lt[:])
+            quantize(w_codes[a][:], w_scales[a][:], w_woven[a][:])
+        quantize(v_codes[:, P:DV], v_scales[:, P:DV], v_woven[1][:])
+        inv_sum = keep.tile([P, QT], F32, name="inv_sum", tag="w_woven0", align_bytes=MX_ALIGN)
+        nc.vector.reciprocal(inv_sum[:], row_sum[:])
+
         for a in range(QT):
             for h in range(ET):
                 cols = slice(h * P, (h + 1) * P)
-                product(y_ps[a][:, cols], wc[a][:], ws[a][:], vc[:, cols], vsx[:, cols])
+                product(y_ps[a][:, cols], w_codes[a][:], w_scales[a][:], v_codes[:, cols], v_scales[:, cols])
         for a in range(QT):
-            nc.vector.scalar_tensor_tensor(res[a][:], y_ps[a][:], rl[:, a : a + 1], gate[:, a, :], ALU.mult, ALU.mult)
-            nc.sync.dma_start(oview[a], res[a][:])
+            nc.vector.scalar_tensor_tensor(result[a][:], y_ps[a][:], inv_sum[:, a : a + 1], gate[:, a, :], ALU.mult, ALU.mult)
+            nc.sync.dma_start(out_rows[a], result[a][:])

@@ -152,7 +152,10 @@ def tile_attend_x_append128_gate_topk_kernel(tc, qT, kT, vT, new_kT, new_vT, vs,
             cols = slice(c * HALF, (c + 1) * HALF)
             quantize(k_codes[:, cols], k_scales[:, cols], k_woven[c][:])
             product(score_ps[0][:, cols], q_codes[:, 0:P], q_scales[:, 0:P], k_codes[:, cols], k_scales[:, cols])
-        product(score_ps[1][:], q_codes[:, P:NQ], q_scales[:, P:NQ], k_codes[:], k_scales[:])
+            if c == 0:
+                product(score_ps[1][:, 0:P], q_codes[:, P:NQ], q_scales[:, P:NQ], k_codes[:, 0:P], k_scales[:, 0:P])
+        for cols in (slice(P, HALF), slice(HALF, N)):
+            product(score_ps[1][:, cols], q_codes[:, P:NQ], q_scales[:, P:NQ], k_codes[:, cols], k_scales[:, cols])
         nc.vector.tensor_copy(v_tile[1][:].indirect(slots_t[:]), new_v[:, 1, :])
 
         v_ps = [psum.tile([P, PACK // PAIR, P], F32, name="v_ps0"), psum.tile([P, PACK // PAIR, P], F32, name="v_ps1", tag="score_ps1")]

@@ -22,9 +22,11 @@ QT = NQ // P
 ET = DV // P
 HALF = N // 2
 CAST_SPLIT = 320
+FIRST_CAST_SPLIT = 448
 AT_QUERIES = 0
 AT_WOVEN_VALUES = 5120
 AT_TANH = 6144
+AT_LAST_KEYS = 8192
 MX_ALIGN = 64
 
 FLOPS = 2 * NQ * N * (D + DV)
@@ -51,11 +53,12 @@ def tile_attend_x_append128_gate_topk_kernel(tc, qT, kT, vT, new_kT, new_vT, vs,
 
         slots_t = keep.tile([P, NEW // LIST_ROWS], U16, name="slots_t")
         offs_t = keep.tile([P, N // LIST_ROWS], U16, name="offs_t")
-        k_plane = [keep.tile([P, T], F32, name=f"k_plane{t}") for t in range(PACK)]
+        k_plane = [keep.tile([P, T], F32, name=f"k_plane{t}") for t in range(PACK - 1)]
+        k_plane.append(overlap.tile([P, T], F32, name="k_plane3", align_bytes=MX_ALIGN, offset=AT_LAST_KEYS))
         k_cast = [keep.tile([P, T], BF16, name=f"k_cast{t}") for t in range(PAIR)]
         v_tile = [keep.tile([P, T], F32, name=f"v_tile{h}") for h in range(ET)]
-        new_k_first = keep.tile([P, NEW], F32, name="new_k_first")
-        new_k_rest = keep.tile([P, PACK - 1, NEW], F32, name="new_k_rest")
+        new_k_first = keep.tile([P, PACK - 1, NEW], F32, name="new_k_first")
+        new_k_last = keep.tile([P, NEW], F32, name="new_k_last")
         new_v = keep.tile([P, ET, NEW], F32, name="new_v")
         q_planes = overlap.tile([P, PACK, NQ], F32, name="q_planes", align_bytes=MX_ALIGN, offset=AT_QUERIES)
         vs_t = keep.tile([P, T], F32, name="vs_t")
@@ -97,15 +100,15 @@ def tile_attend_x_append128_gate_topk_kernel(tc, qT, kT, vT, new_kT, new_vT, vs,
         out_rows = out[0].rearrange("(a p) e -> a p e", p=P)
         offs_half = [offs_t[:, c * HALF // LIST_ROWS : (c + 1) * HALF // LIST_ROWS] for c in range(2)]
 
+        nc.sync.dma_start(offs_t[:], offs)
+        nc.sync.dma_start(vs_t[P - 1 : P, :], vs[0:1, :])
+        nc.vector.memset(vs_t[0 : P - 1, :], 0.0)
         nc.sync.dma_start(k_plane[0][:], k_rows[:, 0, :])
         nc.sync.dma_start(slots_t[:], slots)
-        nc.sync.dma_start(new_k_first[:], new_k_rows[:, 0, :])
-        nc.sync.dma_start(offs_t[:], offs)
-        nc.sync.dma_start(new_k_rest[:], new_k_rows[:, 1:PACK, :])
-        nc.vector.memset(vs_t[:], 0.0)
-        nc.sync.dma_start(vs_t[0:1, :], vs[0:1, :])
+        nc.sync.dma_start(new_k_first[:], new_k_rows[:, 0 : PACK - 1, :])
         for t in range(1, PACK):
             nc.sync.dma_start(k_plane[t][:], k_rows[:, t, :])
+        nc.sync.dma_start(new_k_last[:], new_k_rows[:, PACK - 1, :])
         nc.sync.dma_start(new_v[:], new_vT.rearrange("(h p) n -> p h n", p=P))
         nc.sync.dma_start(q_planes[:], qT[0].rearrange("(p t) n -> p t n", t=PACK))
         for h in range(ET):
@@ -114,17 +117,19 @@ def tile_attend_x_append128_gate_topk_kernel(tc, qT, kT, vT, new_kT, new_vT, vs,
 
         make_identity(nc, identity[:])
 
-        nc.vector.tensor_copy(k_plane[0][:].indirect(slots_t[:]), new_k_first[:])
         nc.vector.tensor_copy(vs_row[:], vs_t[:].indirect(offs_t[:]))
+        nc.vector.tensor_copy(k_plane[0][:].indirect(slots_t[:]), new_k_first[:, 0, :])
         for t in range(PACK):
             nc.tensor.transpose(vs_ps[:, t, :], vs_row[:].rearrange("p (s t) -> p t s", t=PACK)[:, t, :], identity[:])
-        vs_col = keep.tile([P, PACK], F32, name="vs_col")
-        nc.scalar.copy(vs_col[:], vs_ps[:, :, 0])
-        for t in range(1, PACK):
-            nc.vector.tensor_copy(k_plane[t][:].indirect(slots_t[:]), new_k_rest[:, t - 1, :])
+        for t in range(1, PACK - 1):
+            nc.vector.tensor_copy(k_plane[t][:].indirect(slots_t[:]), new_k_first[:, t, :])
+        nc.vector.tensor_copy(k_plane[PACK - 1][:].indirect(slots_t[:]), new_k_last[:])
 
         for j in range(PAIR):
-            nc.scalar.activation(k_cast[j][:], k_plane[j][:], ACT.Copy)
+            shared = FIRST_CAST_SPLIT if j == 0 else 0
+            if shared:
+                nc.vector.tensor_copy(k_cast[j][:, :shared], k_plane[j][:, :shared])
+            nc.scalar.activation(k_cast[j][:, shared:], k_plane[j][:, shared:], ACT.Copy)
             for c in range(2):
                 nc.scalar.activation(k_pairs[c][:, 0, :, j], k_cast[j][:].indirect(offs_half[c]), ACT.Copy)
         for j in range(PAIR):
@@ -132,6 +137,9 @@ def tile_attend_x_append128_gate_topk_kernel(tc, qT, kT, vT, new_kT, new_vT, vs,
                 nc.vector.tensor_copy(k_pairs[c][:, 1, :, j], k_plane[PAIR + j][:].indirect(offs_half[c]))
         for c in range(2):
             nc.scalar.copy(as_words(k_woven[c][:]), k_pairs[c][:].rearrange("p u n j -> p u (n j)").bitcast(F32).rearrange("p u n -> p n u"))
+
+        vs_col = overlap.tile([P, PACK], F32, name="vs_col", align_bytes=MX_ALIGN, offset=AT_LAST_KEYS)
+        nc.scalar.copy(vs_col[:], vs_ps[:, :, P - 1])
 
         for a in range(QT):
             rows = slice(a * P, (a + 1) * P)

@@ -87,17 +87,16 @@ def tile_attend_x_append128_gate_topk_kernel(tc, qT, kT, vT, new_kT, new_vT, vs,
         w_woven = [keep.tile([P, P, PACK], BF16, name=f"w_woven{a}", tag=f"w_woven{a}", align_bytes=MX_ALIGN) for a in range(QT)]
         w_codes = [keep.tile([P, P], U32, name=f"w_codes{a}", align_bytes=MX_ALIGN) for a in range(QT)]
         w_scales = [keep.tile([P, P], U8, name=f"w_scales{a}", align_bytes=MX_ALIGN) for a in range(QT)]
-        result = [keep.tile([P, DV], F32, name=f"result{a}") for a in range(QT)]
+        result = [keep.tile([P, QT, P], F32, name=f"result{h}") for h in range(ET)]
         identity = keep.tile([P, P], F32, name="identity")
         score_ps = [psum.tile([P, N], F32, name=f"score_ps{a}", tag=f"score_ps{a}") for a in range(QT)]
         p_ps = [psum.tile([P, PACK, P], F32, name=f"p_ps{a}") for a in range(QT)]
-        y_ps = [psum.tile([P, DV], F32, name=f"y_ps{a}") for a in range(QT)]
-        vs_ps = psum.tile([P, PACK, P], F32, name="vs_ps")
+        vs_ps = psum.tile([P, PACK, P], F32, name="vs_ps", tag="vs_ps")
 
         k_rows = kT.rearrange("(p t) n -> p t n", t=PACK)
         new_k_rows = new_kT.rearrange("(p t) n -> p t n", t=PACK)
         v_rows = vT.rearrange("(h p) n -> p h n", p=P)
-        out_rows = out[0].rearrange("(a p) e -> a p e", p=P)
+        out_rows = out[0].rearrange("(a p) (h e) -> h p a e", p=P, e=P)
         offs_half = [offs_t[:, c * HALF // LIST_ROWS : (c + 1) * HALF // LIST_ROWS] for c in range(2)]
 
         nc.sync.dma_start(offs_t[:], offs)
@@ -193,7 +192,8 @@ def tile_attend_x_append128_gate_topk_kernel(tc, qT, kT, vT, new_kT, new_vT, vs,
         nc.scalar.activation(tanh_t[:], og_t[:], ACT.Tanh, scale=0.5)
         weave_values(1)
         gate = keep.tile([P, QT, DV], F32, name="gate", tag="q_codes", align_bytes=MX_ALIGN)
-        nc.scalar.activation(gate[:], tanh_t[:], ACT.Copy, scale=0.5, bias=0.5)
+        for h in range(ET):
+            nc.scalar.activation(gate[:, :, h * P : (h + 1) * P], tanh_t[:, :, h * P : (h + 1) * P], ACT.Copy, scale=0.5, bias=0.5)
 
         weigh(0)
         quantize(v_codes[:, 0:P], v_scales[:, 0:P], v_woven[0][:])
@@ -204,10 +204,16 @@ def tile_attend_x_append128_gate_topk_kernel(tc, qT, kT, vT, new_kT, new_vT, vs,
         inv_sum = keep.tile([P, QT], F32, name="inv_sum", tag="w_woven0", align_bytes=MX_ALIGN)
         nc.vector.reciprocal(inv_sum[:], row_sum[:])
 
-        for a in range(QT):
-            for h in range(ET):
-                cols = slice(h * P, (h + 1) * P)
-                product(y_ps[a][:, cols], w_codes[a][:], w_scales[a][:], v_codes[:, cols], v_scales[:, cols])
-        for a in range(QT):
-            nc.vector.scalar_tensor_tensor(result[a][:], y_ps[a][:], inv_sum[:, a : a + 1], gate[:, a, :], ALU.mult, ALU.mult)
-            nc.sync.dma_start(out_rows[a], result[a][:])
+        y_ps = [
+            [psum.tile([P, P], F32, name="y_ps00"), psum.tile([P, P], F32, name="y_ps01", tag="vs_ps")],
+            [psum.tile([P, P], F32, name="y_ps10"), psum.tile([P, P], F32, name="y_ps11", tag="score_ps0")],
+        ]
+        for h in range(ET):
+            cols = slice(h * P, (h + 1) * P)
+            for a in range(QT):
+                product(y_ps[a][h][:], w_codes[a][:], w_scales[a][:], v_codes[:, cols], v_scales[:, cols])
+        for h in range(ET):
+            cols = slice(h * P, (h + 1) * P)
+            for a in range(QT):
+                nc.vector.scalar_tensor_tensor(result[h][:, a, :], y_ps[a][h][:], inv_sum[:, a : a + 1], gate[:, a, cols], ALU.mult, ALU.mult)
+            nc.sync.dma_start(out_rows[h], result[h][:])

@@ -22,7 +22,6 @@ QT = NQ // P
 ET = DV // P
 HALF = N // 2
 CAST_SPLIT = 320
-FIRST_CAST_SPLIT = 448
 AT_QUERIES = 0
 AT_WOVEN_VALUES = 5120
 AT_TANH = 6144
@@ -57,8 +56,8 @@ def tile_attend_x_append128_gate_topk_kernel(tc, qT, kT, vT, new_kT, new_vT, vs,
         k_plane.append(overlap.tile([P, T], F32, name="k_plane3", align_bytes=MX_ALIGN, offset=AT_LAST_KEYS))
         k_cast = [keep.tile([P, T], BF16, name=f"k_cast{t}") for t in range(PAIR)]
         v_tile = [keep.tile([P, T], F32, name=f"v_tile{h}") for h in range(ET)]
-        new_k_first = keep.tile([P, PACK - 1, NEW], F32, name="new_k_first")
-        new_k_last = keep.tile([P, NEW], F32, name="new_k_last")
+        new_k_first = keep.tile([P, NEW], F32, name="new_k_first")
+        new_k_rest = keep.tile([P, PACK - 1, NEW], F32, name="new_k_rest")
         new_v = keep.tile([P, ET, NEW], F32, name="new_v")
         q_planes = overlap.tile([P, PACK, NQ], F32, name="q_planes", align_bytes=MX_ALIGN, offset=AT_QUERIES)
         vs_t = keep.tile([P, T], F32, name="vs_t")
@@ -99,15 +98,15 @@ def tile_attend_x_append128_gate_topk_kernel(tc, qT, kT, vT, new_kT, new_vT, vs,
         out_rows = out[0].rearrange("(a p) (h e) -> h p a e", p=P, e=P)
         offs_half = [offs_t[:, c * HALF // LIST_ROWS : (c + 1) * HALF // LIST_ROWS] for c in range(2)]
 
-        nc.sync.dma_start(offs_t[:], offs)
-        nc.sync.dma_start(vs_t[P - 1 : P, :], vs[0:1, :])
-        nc.vector.memset(vs_t[0 : P - 1, :], 0.0)
         nc.sync.dma_start(k_plane[0][:], k_rows[:, 0, :])
         nc.sync.dma_start(slots_t[:], slots)
-        nc.sync.dma_start(new_k_first[:], new_k_rows[:, 0 : PACK - 1, :])
+        nc.scalar.dma_start(new_k_first[:], new_k_rows[:, 0, :])
+        nc.scalar.dma_start(vs_t[P - 1 : P, :], vs[0:1, :])
+        nc.sync.dma_start(offs_t[:], offs)
+        nc.sync.dma_start(new_k_rest[:], new_k_rows[:, 1:PACK, :])
+        nc.vector.memset(vs_t[0 : P - 1, :], 0.0)
         for t in range(1, PACK):
             nc.sync.dma_start(k_plane[t][:], k_rows[:, t, :])
-        nc.sync.dma_start(new_k_last[:], new_k_rows[:, PACK - 1, :])
         nc.sync.dma_start(new_v[:], new_vT.rearrange("(h p) n -> p h n", p=P))
         nc.sync.dma_start(q_planes[:], qT[0].rearrange("(p t) n -> p t n", t=PACK))
         for h in range(ET):
@@ -116,19 +115,15 @@ def tile_attend_x_append128_gate_topk_kernel(tc, qT, kT, vT, new_kT, new_vT, vs,
 
         make_identity(nc, identity[:])
 
+        nc.vector.tensor_copy(k_plane[0][:].indirect(slots_t[:]), new_k_first[:])
         nc.vector.tensor_copy(vs_row[:], vs_t[:].indirect(offs_t[:]))
-        nc.vector.tensor_copy(k_plane[0][:].indirect(slots_t[:]), new_k_first[:, 0, :])
         for t in range(PACK):
             nc.tensor.transpose(vs_ps[:, t, :], vs_row[:].rearrange("p (s t) -> p t s", t=PACK)[:, t, :], identity[:])
-        for t in range(1, PACK - 1):
-            nc.vector.tensor_copy(k_plane[t][:].indirect(slots_t[:]), new_k_first[:, t, :])
-        nc.vector.tensor_copy(k_plane[PACK - 1][:].indirect(slots_t[:]), new_k_last[:])
+        for t in range(1, PACK):
+            nc.vector.tensor_copy(k_plane[t][:].indirect(slots_t[:]), new_k_rest[:, t - 1, :])
 
         for j in range(PAIR):
-            shared = FIRST_CAST_SPLIT if j == 0 else 0
-            if shared:
-                nc.vector.tensor_copy(k_cast[j][:, :shared], k_plane[j][:, :shared])
-            nc.scalar.activation(k_cast[j][:, shared:], k_plane[j][:, shared:], ACT.Copy)
+            nc.scalar.activation(k_cast[j][:], k_plane[j][:], ACT.Copy)
             for c in range(2):
                 nc.scalar.activation(k_pairs[c][:, 0, :, j], k_cast[j][:].indirect(offs_half[c]), ACT.Copy)
         for j in range(PAIR):

@@ -21,7 +21,7 @@ LIST_ROWS = 16
 QT = NQ // P
 ET = DV // P
 HALF = N // 2
-CAST_SPLIT = 320
+CAST_SPLIT = 576
 AT_QUERIES = 0
 AT_WOVEN_VALUES = 5120
 AT_TANH = 6144
@@ -52,12 +52,17 @@ def tile_attend_x_append128_gate_topk_kernel(tc, qT, kT, vT, new_kT, new_vT, vs,
 
         slots_t = keep.tile([P, NEW // LIST_ROWS], U16, name="slots_t")
         offs_t = keep.tile([P, N // LIST_ROWS], U16, name="offs_t")
-        k_plane = [keep.tile([P, T], F32, name=f"k_plane{t}") for t in range(PACK - 1)]
-        k_plane.append(overlap.tile([P, T], F32, name="k_plane3", align_bytes=MX_ALIGN, offset=AT_LAST_KEYS))
+        k_plane = [
+            keep.tile([P, T], F32, name="k_plane0"),
+            overlap.tile([P, T], F32, name="k_plane1", align_bytes=MX_ALIGN, offset=AT_LAST_KEYS),
+            keep.tile([P, T], F32, name="k_plane2"),
+            keep.tile([P, T], F32, name="k_plane3"),
+        ]
         k_cast = [keep.tile([P, T], BF16, name=f"k_cast{t}") for t in range(PAIR)]
         v_tile = [keep.tile([P, T], F32, name=f"v_tile{h}") for h in range(ET)]
         new_k_first = keep.tile([P, NEW], F32, name="new_k_first")
         new_k_rest = keep.tile([P, PACK - 1, NEW], F32, name="new_k_rest")
+        new_v_loaded = keep.tile([P, ET, NEW], F32, name="new_v_loaded")
         new_v = keep.tile([P, ET, NEW], F32, name="new_v")
         q_planes = overlap.tile([P, PACK, NQ], F32, name="q_planes", align_bytes=MX_ALIGN, offset=AT_QUERIES)
         vs_t = keep.tile([P, T], F32, name="vs_t")
@@ -107,13 +112,18 @@ def tile_attend_x_append128_gate_topk_kernel(tc, qT, kT, vT, new_kT, new_vT, vs,
         nc.vector.memset(vs_t[0 : P - 1, :], 0.0)
         for t in range(1, PACK):
             nc.sync.dma_start(k_plane[t][:], k_rows[:, t, :])
-        nc.sync.dma_start(new_v[:], new_vT.rearrange("(h p) n -> p h n", p=P))
+        nc.sync.dma_start(new_v_loaded[:], new_vT.rearrange("(h p) n -> p h n", p=P))
         nc.sync.dma_start(q_planes[:], qT[0].rearrange("(p t) n -> p t n", t=PACK))
         for h in range(ET):
             nc.sync.dma_start(v_tile[h][:], v_rows[:, h, :])
         nc.sync.dma_start(og_t[:], og[0].rearrange("(a p) e -> p a e", p=P))
 
         make_identity(nc, identity[:])
+        for c in range(2):
+            nc.gpsimd.memset(k_pairs[c][:, 1, 0, 0:1], 1.0)
+            nc.gpsimd.memset(k_pairs[c][:, 1, 0, 1:2], 0.0)
+        for h in range(ET):
+            nc.gpsimd.tensor_scalar(new_v[:, h, :], new_v_loaded[:, h, :], k_pairs[h][:, 1, 0, 0:1], k_pairs[h][:, 1, 0, 1:2], ALU.mult, ALU.add)
 
         nc.vector.tensor_copy(k_plane[0][:].indirect(slots_t[:]), new_k_first[:])
         nc.vector.tensor_copy(vs_row[:], vs_t[:].indirect(offs_t[:]))
@@ -126,8 +136,8 @@ def tile_attend_x_append128_gate_topk_kernel(tc, qT, kT, vT, new_kT, new_vT, vs,
             nc.scalar.activation(k_cast[j][:], k_plane[j][:], ACT.Copy)
             for c in range(2):
                 nc.scalar.activation(k_pairs[c][:, 0, :, j], k_cast[j][:].indirect(offs_half[c]), ACT.Copy)
-        for j in range(PAIR):
-            for c in range(2):
+        for c in range(2):
+            for j in range(PAIR):
                 nc.vector.tensor_copy(k_pairs[c][:, 1, :, j], k_plane[PAIR + j][:].indirect(offs_half[c]))
         for c in range(2):
             nc.scalar.copy(as_words(k_woven[c][:]), k_pairs[c][:].rearrange("p u n j -> p u (n j)").bitcast(F32).rearrange("p u n -> p n u"))

@@ -21,7 +21,7 @@ LIST_ROWS = 16
 QT = NQ // P
 ET = DV // P
 HALF = N // 2
-CAST_SPLIT = 576
+CAST_SPLIT = 448
 AT_QUERIES = 0
 AT_WOVEN_VALUES = 5120
 AT_TANH = 6144
@@ -44,6 +44,9 @@ def tile_attend_x_append128_gate_topk_kernel(tc, qT, kT, vT, new_kT, new_vT, vs,
 
     def as_words(woven):
         return woven.rearrange("p n t -> p (n t)").bitcast(F32).rearrange("p (n u) -> p n u", u=PACK // PAIR)
+
+    def dealt(picked):
+        return picked[:].rearrange("p (u s j) -> p s u j", u=PACK // PAIR, j=PAIR)
 
     with ExitStack() as ctx:
         keep = ctx.enter_context(tc.tile_pool(name="keep", bufs=1))
@@ -119,11 +122,13 @@ def tile_attend_x_append128_gate_topk_kernel(tc, qT, kT, vT, new_kT, new_vT, vs,
         nc.sync.dma_start(og_t[:], og[0].rearrange("(a p) e -> p a e", p=P))
 
         make_identity(nc, identity[:])
-        for c in range(2):
-            nc.gpsimd.memset(k_pairs[c][:, 1, 0, 0:1], 1.0)
-            nc.gpsimd.memset(k_pairs[c][:, 1, 0, 1:2], 0.0)
+        one = [k_pairs[1][:, 1, 0, 0:1], k_pairs[0][:, 1, 0, 1:2]]
+        zero = k_pairs[1][:, 1, 0, 1:2]
         for h in range(ET):
-            nc.gpsimd.tensor_scalar(new_v[:, h, :], new_v_loaded[:, h, :], k_pairs[h][:, 1, 0, 0:1], k_pairs[h][:, 1, 0, 1:2], ALU.mult, ALU.add)
+            nc.vector.memset(one[h], 1.0)
+        nc.vector.memset(zero, 0.0)
+        nc.gpsimd.tensor_scalar(new_v[:, 0, :], new_v_loaded[:, 0, :], one[0], 0.0, ALU.mult, ALU.add)
+        nc.gpsimd.tensor_scalar(new_v[:, 1, :], new_v_loaded[:, 1, :], one[1], zero, ALU.mult, ALU.add)
 
         nc.vector.tensor_copy(k_plane[0][:].indirect(slots_t[:]), new_k_first[:])
         nc.vector.tensor_copy(vs_row[:], vs_t[:].indirect(offs_t[:]))
@@ -136,8 +141,8 @@ def tile_attend_x_append128_gate_topk_kernel(tc, qT, kT, vT, new_kT, new_vT, vs,
             nc.scalar.activation(k_cast[j][:], k_plane[j][:], ACT.Copy)
             for c in range(2):
                 nc.scalar.activation(k_pairs[c][:, 0, :, j], k_cast[j][:].indirect(offs_half[c]), ACT.Copy)
-        for c in range(2):
-            for j in range(PAIR):
+        for j in range(PAIR):
+            for c in range(2):
                 nc.vector.tensor_copy(k_pairs[c][:, 1, :, j], k_plane[PAIR + j][:].indirect(offs_half[c]))
         for c in range(2):
             nc.scalar.copy(as_words(k_woven[c][:]), k_pairs[c][:].rearrange("p u n j -> p u (n j)").bitcast(F32).rearrange("p u n -> p n u"))
@@ -157,7 +162,7 @@ def tile_attend_x_append128_gate_topk_kernel(tc, qT, kT, vT, new_kT, new_vT, vs,
             keep.tile([P, N], BF16, name="v_picked0", align_bytes=MX_ALIGN),
             keep.tile([P, N], BF16, name="v_picked1", tag="q_codes", align_bytes=MX_ALIGN),
         ]
-        nc.scalar.activation(v_picked[0][:], v_cast[:].indirect(offs_t[:]), ACT.Copy)
+        nc.scalar.activation(dealt(v_picked[0]), v_cast[:].indirect(offs_t[:]), ACT.Copy)
 
         k_scales = overlap.tile([P, N], U8, name="k_scales", align_bytes=MX_ALIGN, offset=AT_QUERIES)
         for c in range(2):
@@ -174,7 +179,7 @@ def tile_attend_x_append128_gate_topk_kernel(tc, qT, kT, vT, new_kT, new_vT, vs,
 
         def turn_values(h):
             for u in range(PACK // PAIR):
-                nc.tensor.transpose(v_ps[h][:, u, :], v_picked[h][:].bitcast(F32)[:, u : N // PAIR : PACK // PAIR], identity[:])
+                nc.tensor.transpose(v_ps[h][:, u, :], v_picked[h][:].bitcast(F32)[:, u * P : (u + 1) * P], identity[:])
 
         def weave_values(h):
             nc.scalar.copy(as_words(v_woven[h][:]), v_ps[h][:].rearrange("s u e -> s e u"))
@@ -190,15 +195,14 @@ def tile_attend_x_append128_gate_topk_kernel(tc, qT, kT, vT, new_kT, new_vT, vs,
             )
             for t in range(PACK):
                 nc.tensor.transpose(p_ps[a][:, t, :], p_t[a][:, t, :], identity[:])
-        nc.vector.tensor_copy(v_picked[1][:], v_tile[1][:].indirect(offs_t[:]))
+        nc.vector.tensor_copy(dealt(v_picked[1]), v_tile[1][:].indirect(offs_t[:]))
         turn_values(1)
 
-        weave_values(0)
         nc.scalar.activation(tanh_t[:], og_t[:], ACT.Tanh, scale=0.5)
+        weave_values(0)
+        gate = keep.tile([P, QT, DV], F32, name="gate")
+        nc.scalar.activation(gate[:], tanh_t[:], ACT.Copy, scale=0.5, bias=0.5)
         weave_values(1)
-        gate = keep.tile([P, QT, DV], F32, name="gate", tag="q_codes", align_bytes=MX_ALIGN)
-        for h in range(ET):
-            nc.scalar.activation(gate[:, :, h * P : (h + 1) * P], tanh_t[:, :, h * P : (h + 1) * P], ACT.Copy, scale=0.5, bias=0.5)
 
         weigh(0)
         quantize(v_codes[:, 0:P], v_scales[:, 0:P], v_woven[0][:])

@@ -21,7 +21,7 @@ LIST_ROWS = 16
 QT = NQ // P
 ET = DV // P
 HALF = N // 2
-CAST_SPLIT = 448
+CAST_SPLIT = 256
 AT_QUERIES = 0
 AT_WOVEN_VALUES = 5120
 AT_TANH = 6144
@@ -150,9 +150,7 @@ def tile_attend_x_append128_gate_topk_kernel(tc, qT, kT, vT, new_kT, new_vT, vs,
         vs_col = overlap.tile([P, PACK], F32, name="vs_col", align_bytes=MX_ALIGN, offset=AT_LAST_KEYS)
         nc.scalar.copy(vs_col[:], vs_ps[:, :, P - 1])
 
-        for a in range(QT):
-            rows = slice(a * P, (a + 1) * P)
-            nc.gpsimd.tensor_scalar(q_woven[:, rows, :], q_planes[:, :, rows].rearrange("p t n -> p n t"), 1.0, 0.0, ALU.mult, ALU.add)
+        nc.gpsimd.tensor_scalar(q_woven[:], q_planes[:].rearrange("p t n -> p n t"), 1.0, 0.0, ALU.mult, ALU.add)
 
         nc.vector.tensor_copy(v_tile[0][:].indirect(slots_t[:]), new_v[:, 0, :])
         quantize(q_codes[:], q_scales[:], q_woven[:])

@@ -150,7 +150,9 @@ def tile_attend_x_append128_gate_topk_kernel(tc, qT, kT, vT, new_kT, new_vT, vs,
         vs_col = overlap.tile([P, PACK], F32, name="vs_col", align_bytes=MX_ALIGN, offset=AT_LAST_KEYS)
         nc.scalar.copy(vs_col[:], vs_ps[:, :, P - 1])
 
-        nc.gpsimd.tensor_scalar(q_woven[:], q_planes[:].rearrange("p t n -> p n t"), 1.0, 0.0, ALU.mult, ALU.add)
+        nc.gpsimd.tensor_scalar(
+            q_woven[:].rearrange("p (c i) t -> p c t i", i=PACK), q_planes[:].rearrange("p t (c i) -> p c t i", i=PACK), 1.0, 0.0, ALU.mult, ALU.add
+        )
 
         nc.vector.tensor_copy(v_tile[0][:].indirect(slots_t[:]), new_v[:, 0, :])
         quantize(q_codes[:], q_scales[:], q_woven[:])

@@ -21,11 +21,6 @@ LIST_ROWS = 16
 QT = NQ // P
 ET = DV // P
 HALF = N // 2
-CAST_SPLIT = 256
-AT_QUERIES = 0
-AT_WOVEN_VALUES = 5120
-AT_TANH = 6144
-AT_LAST_KEYS = 8192
 MX_ALIGN = 64
 
 FLOPS = 2 * NQ * N * (D + DV)
@@ -45,9 +40,6 @@ def tile_attend_x_append128_gate_topk_kernel(tc, qT, kT, vT, new_kT, new_vT, vs,
     def as_words(woven):
         return woven.rearrange("p n t -> p (n t)").bitcast(F32).rearrange("p (n u) -> p n u", u=PACK // PAIR)
 
-    def dealt(picked):
-        return picked[:].rearrange("p (u s j) -> p s u j", u=PACK // PAIR, j=PAIR)
-
     with ExitStack() as ctx:
         keep = ctx.enter_context(tc.tile_pool(name="keep", bufs=1))
         overlap = ctx.enter_context(tc.tile_pool(name="overlap", bufs=1))
@@ -55,49 +47,42 @@ def tile_attend_x_append128_gate_topk_kernel(tc, qT, kT, vT, new_kT, new_vT, vs,
 
         slots_t = keep.tile([P, NEW // LIST_ROWS], U16, name="slots_t")
         offs_t = keep.tile([P, N // LIST_ROWS], U16, name="offs_t")
-        k_plane = [
-            keep.tile([P, T], F32, name="k_plane0"),
-            overlap.tile([P, T], F32, name="k_plane1", align_bytes=MX_ALIGN, offset=AT_LAST_KEYS),
-            keep.tile([P, T], F32, name="k_plane2"),
-            keep.tile([P, T], F32, name="k_plane3"),
-        ]
-        k_cast = [keep.tile([P, T], BF16, name=f"k_cast{t}") for t in range(PAIR)]
+        k_plane = [keep.tile([P, T], F32, name=f"k_plane{t}") for t in range(PACK)]
         v_tile = [keep.tile([P, T], F32, name=f"v_tile{h}") for h in range(ET)]
+        new_k_loaded = keep.tile([P, NEW], F32, name="new_k_loaded")
         new_k_first = keep.tile([P, NEW], F32, name="new_k_first")
         new_k_rest = keep.tile([P, PACK - 1, NEW], F32, name="new_k_rest")
-        new_v_loaded = keep.tile([P, ET, NEW], F32, name="new_v_loaded")
         new_v = keep.tile([P, ET, NEW], F32, name="new_v")
-        q_planes = overlap.tile([P, PACK, NQ], F32, name="q_planes", align_bytes=MX_ALIGN, offset=AT_QUERIES)
+        q_planes = overlap.tile([P, PACK, NQ], F32, name="q_planes", align_bytes=MX_ALIGN, offset=0)
         vs_t = keep.tile([P, T], F32, name="vs_t")
         og_t = keep.tile([P, QT, DV], F32, name="og_t")
-        k_pairs = [keep.tile([P, PACK // PAIR, HALF, PAIR], BF16, name=f"k_pairs{c}") for c in range(2)]
+        k_pairs_row = keep.tile([P, N * PACK], BF16, name="k_pairs_row")
+        k_pairs = k_pairs_row[:].rearrange("p (c u i j) -> p c u i j", c=2, u=PACK // PAIR, j=PAIR)
         k_woven = [keep.tile([P, HALF, PACK], BF16, name=f"k_woven{c}", align_bytes=MX_ALIGN) for c in range(2)]
         q_woven = keep.tile([P, NQ, PACK], BF16, name="q_woven", align_bytes=MX_ALIGN)
         q_codes = keep.tile([P, NQ], U32, name="q_codes", tag="q_codes", align_bytes=MX_ALIGN)
         q_scales = keep.tile([P, NQ], U8, name="q_scales", align_bytes=MX_ALIGN)
-        v_cast = keep.tile([P, T], BF16, name="v_cast")
         k_codes = keep.tile([P, N], U32, name="k_codes", align_bytes=MX_ALIGN)
+        k_scales = [keep.tile([P, HALF], U8, name="k_scales0", align_bytes=MX_ALIGN)[:], overlap.tile([P, HALF], U8, name="k_scales1", align_bytes=MX_ALIGN, offset=2 * N)[:]]
         vs_row = keep.tile([P, N], F32, name="vs_row")
-        v_woven = [
-            overlap.tile([P, P, PACK], BF16, name="v_woven0", align_bytes=MX_ALIGN, offset=AT_WOVEN_VALUES),
-            keep.tile([P, P, PACK], BF16, name="v_woven1", align_bytes=MX_ALIGN),
-        ]
+        v_picked1 = keep.tile([P, N], BF16, name="v_picked1")
+        v_woven = [keep.tile([P, P, PACK], BF16, name=f"v_woven{h}", align_bytes=MX_ALIGN) for h in range(ET)]
         v_codes = keep.tile([P, DV], U32, name="v_codes", align_bytes=MX_ALIGN)
         v_scales = keep.tile([P, DV], U8, name="v_scales", align_bytes=MX_ALIGN)
-        tanh_t = overlap.tile([P, QT, DV], F32, name="tanh_t", align_bytes=MX_ALIGN, offset=AT_TANH)
-        neg_max = [
-            keep.tile([P, 1], F32, name="neg_max0")[:],
-            overlap.tile([P, 2 * MX_ALIGN // 4], F32, name="neg_max1", align_bytes=MX_ALIGN, offset=AT_TANH - MX_ALIGN)[:, 0:1],
-        ]
-        row_sum = keep.tile([P, QT], F32, name="row_sum")
+        tanh_t = keep.tile([P, QT, DV], F32, name="tanh_t")
+        gate = keep.tile([P, QT, DV], F32, name="gate")
+        neg_max = [v_picked1[:, N - PAIR : N].bitcast(F32), tanh_t[:, 0, 0:1]]
+        row_sum = new_v[:, 1, 0:QT]
+        vs_col = new_k_rest[:, PACK - 2, 0:PACK]
+        inv_sum = keep.tile([P, QT], F32, name="inv_sum")
         p_t = [keep.tile([P, PACK, P], F32, name=f"p_t{a}") for a in range(QT)]
-        w_woven = [keep.tile([P, P, PACK], BF16, name=f"w_woven{a}", tag=f"w_woven{a}", align_bytes=MX_ALIGN) for a in range(QT)]
+        w_woven = [keep.tile([P, P, PACK], BF16, name=f"w_woven{a}", align_bytes=MX_ALIGN) for a in range(QT)]
         w_codes = [keep.tile([P, P], U32, name=f"w_codes{a}", align_bytes=MX_ALIGN) for a in range(QT)]
         w_scales = [keep.tile([P, P], U8, name=f"w_scales{a}", align_bytes=MX_ALIGN) for a in range(QT)]
         result = [keep.tile([P, QT, P], F32, name=f"result{h}") for h in range(ET)]
         identity = keep.tile([P, P], F32, name="identity")
         score_ps = [psum.tile([P, N], F32, name=f"score_ps{a}", tag=f"score_ps{a}") for a in range(QT)]
-        p_ps = [psum.tile([P, PACK, P], F32, name=f"p_ps{a}") for a in range(QT)]
+        p_ps = [psum.tile([P, PACK, P], F32, name=f"p_ps{a}", tag=f"p_ps{a}") for a in range(QT)]
         vs_ps = psum.tile([P, PACK, P], F32, name="vs_ps", tag="vs_ps")
 
         k_rows = kT.rearrange("(p t) n -> p t n", t=PACK)
@@ -106,88 +91,65 @@ def tile_attend_x_append128_gate_topk_kernel(tc, qT, kT, vT, new_kT, new_vT, vs,
         out_rows = out[0].rearrange("(a p) (h e) -> h p a e", p=P, e=P)
         offs_half = [offs_t[:, c * HALF // LIST_ROWS : (c + 1) * HALF // LIST_ROWS] for c in range(2)]
 
+        nc.sync.dma_start(offs_t[:], offs)
+        nc.scalar.dma_start(vs_t[P - 1 : P, :], vs[0:1, :])
+        nc.scalar.dma_start(new_k_loaded[:], new_k_rows[:, 0, :])
         nc.sync.dma_start(k_plane[0][:], k_rows[:, 0, :])
         nc.sync.dma_start(slots_t[:], slots)
-        nc.scalar.dma_start(new_k_first[:], new_k_rows[:, 0, :])
-        nc.scalar.dma_start(vs_t[P - 1 : P, :], vs[0:1, :])
-        nc.sync.dma_start(offs_t[:], offs)
         nc.sync.dma_start(new_k_rest[:], new_k_rows[:, 1:PACK, :])
         nc.vector.memset(vs_t[0 : P - 1, :], 0.0)
         for t in range(1, PACK):
             nc.sync.dma_start(k_plane[t][:], k_rows[:, t, :])
-        nc.sync.dma_start(new_v_loaded[:], new_vT.rearrange("(h p) n -> p h n", p=P))
         nc.sync.dma_start(q_planes[:], qT[0].rearrange("(p t) n -> p t n", t=PACK))
+        nc.sync.dma_start(new_v[:], new_vT.rearrange("(h p) n -> p h n", p=P))
         for h in range(ET):
             nc.sync.dma_start(v_tile[h][:], v_rows[:, h, :])
         nc.sync.dma_start(og_t[:], og[0].rearrange("(a p) e -> p a e", p=P))
 
         make_identity(nc, identity[:])
-        one = [k_pairs[1][:, 1, 0, 0:1], k_pairs[0][:, 1, 0, 1:2]]
-        zero = k_pairs[1][:, 1, 0, 1:2]
-        for h in range(ET):
-            nc.vector.memset(one[h], 1.0)
-        nc.vector.memset(zero, 0.0)
-        nc.gpsimd.tensor_scalar(new_v[:, 0, :], new_v_loaded[:, 0, :], one[0], 0.0, ALU.mult, ALU.add)
-        nc.gpsimd.tensor_scalar(new_v[:, 1, :], new_v_loaded[:, 1, :], one[1], zero, ALU.mult, ALU.add)
+        nc.scalar.activation(new_k_first[:], new_k_loaded[:], ACT.Copy)
 
-        nc.vector.tensor_copy(k_plane[0][:].indirect(slots_t[:]), new_k_first[:])
         nc.vector.tensor_copy(vs_row[:], vs_t[:].indirect(offs_t[:]))
         for t in range(PACK):
             nc.tensor.transpose(vs_ps[:, t, :], vs_row[:].rearrange("p (s t) -> p t s", t=PACK)[:, t, :], identity[:])
-        for t in range(1, PACK):
-            nc.vector.tensor_copy(k_plane[t][:].indirect(slots_t[:]), new_k_rest[:, t - 1, :])
 
-        for j in range(PAIR):
-            nc.scalar.activation(k_cast[j][:], k_plane[j][:], ACT.Copy)
-            for c in range(2):
-                nc.scalar.activation(k_pairs[c][:, 0, :, j], k_cast[j][:].indirect(offs_half[c]), ACT.Copy)
-        for j in range(PAIR):
-            for c in range(2):
-                nc.vector.tensor_copy(k_pairs[c][:, 1, :, j], k_plane[PAIR + j][:].indirect(offs_half[c]))
+        for t in range(PACK):
+            source = new_k_first[:] if t == 0 else new_k_rest[:, t - 1, :]
+            nc.scalar.activation(k_plane[t][:].indirect(slots_t[:]), source, ACT.Copy)
+            u, j = divmod(t, PAIR)
+            if t < PACK - 1:
+                nc.vector.tensor_copy(k_pairs[:, :, u, :, j], k_plane[t][:].indirect(offs_t[:]))
+            else:
+                for c in range(2):
+                    nc.vector.tensor_copy(k_pairs[:, c, u, :, j], k_plane[t][:].indirect(offs_half[c]))
+        nc.scalar.copy(vs_col, vs_ps[:, :, P - 1])
         for c in range(2):
-            nc.scalar.copy(as_words(k_woven[c][:]), k_pairs[c][:].rearrange("p u n j -> p u (n j)").bitcast(F32).rearrange("p u n -> p n u"))
-
-        vs_col = overlap.tile([P, PACK], F32, name="vs_col", align_bytes=MX_ALIGN, offset=AT_LAST_KEYS)
-        nc.scalar.copy(vs_col[:], vs_ps[:, :, P - 1])
+            nc.scalar.copy(as_words(k_woven[c][:]), k_pairs_row[:, c * 2 * N : (c + 1) * 2 * N].bitcast(F32).rearrange("p (u n) -> p n u", u=PACK // PAIR))
 
         nc.gpsimd.tensor_scalar(
             q_woven[:].rearrange("p (c i) t -> p c t i", i=PACK), q_planes[:].rearrange("p t (c i) -> p c t i", i=PACK), 1.0, 0.0, ALU.mult, ALU.add
         )
 
-        nc.vector.tensor_copy(v_tile[0][:].indirect(slots_t[:]), new_v[:, 0, :])
+        quantize(k_codes[:, 0:HALF], k_scales[0], k_woven[0][:])
         quantize(q_codes[:], q_scales[:], q_woven[:])
-        nc.vector.tensor_copy(v_cast[:, :CAST_SPLIT], v_tile[0][:, :CAST_SPLIT])
-        nc.scalar.activation(v_cast[:, CAST_SPLIT:], v_tile[0][:, CAST_SPLIT:], ACT.Copy)
-        v_picked = [
-            keep.tile([P, N], BF16, name="v_picked0", align_bytes=MX_ALIGN),
-            keep.tile([P, N], BF16, name="v_picked1", tag="q_codes", align_bytes=MX_ALIGN),
-        ]
-        nc.scalar.activation(dealt(v_picked[0]), v_cast[:].indirect(offs_t[:]), ACT.Copy)
+        quantize(k_codes[:, HALF:N], k_scales[1], k_woven[1][:])
+        for a in range(QT):
+            rows = slice(a * P, (a + 1) * P)
+            for c in range(2):
+                cols = slice(c * HALF, (c + 1) * HALF)
+                product(score_ps[a][:, cols], q_codes[:, rows], q_scales[:, rows], k_codes[:, cols], k_scales[c])
 
-        k_scales = overlap.tile([P, N], U8, name="k_scales", align_bytes=MX_ALIGN, offset=AT_QUERIES)
-        for c in range(2):
-            cols = slice(c * HALF, (c + 1) * HALF)
-            quantize(k_codes[:, cols], k_scales[:, cols], k_woven[c][:])
-            product(score_ps[0][:, cols], q_codes[:, 0:P], q_scales[:, 0:P], k_codes[:, cols], k_scales[:, cols])
-            if c == 0:
-                product(score_ps[1][:, 0:P], q_codes[:, P:NQ], q_scales[:, P:NQ], k_codes[:, 0:P], k_scales[:, 0:P])
-        for cols in (slice(P, HALF), slice(HALF, N)):
-            product(score_ps[1][:, cols], q_codes[:, P:NQ], q_scales[:, P:NQ], k_codes[:, cols], k_scales[:, cols])
-        nc.vector.tensor_copy(v_tile[1][:].indirect(slots_t[:]), new_v[:, 1, :])
+        v_picked = [keep.tile([P, N], BF16, name="v_picked0", tag="q_codes", align_bytes=MX_ALIGN), v_picked1]
+        nc.vector.tensor_copy(v_tile[0][:].indirect(slots_t[:]), new_v[:, 0, :])
+        nc.scalar.activation(v_tile[1][:].indirect(slots_t[:]), new_v[:, 1, :], ACT.Copy)
 
-        v_ps = [psum.tile([P, PACK // PAIR, P], F32, name="v_ps0"), psum.tile([P, PACK // PAIR, P], F32, name="v_ps1", tag="score_ps1")]
-
-        def turn_values(h):
-            for u in range(PACK // PAIR):
-                nc.tensor.transpose(v_ps[h][:, u, :], v_picked[h][:].bitcast(F32)[:, u * P : (u + 1) * P], identity[:])
-
-        def weave_values(h):
-            nc.scalar.copy(as_words(v_woven[h][:]), v_ps[h][:].rearrange("s u e -> s e u"))
+        def gather_values_half(c):
+            nc.scalar.activation(v_picked[1][:, c * HALF : (c + 1) * HALF], v_tile[1][:].indirect(offs_half[c]), ACT.Copy)
 
         def weigh(a):
-            nc.vector.tensor_tensor(w_woven[a][:], p_ps[a][:].rearrange("s t q -> s q t"), vs_col[:].unsqueeze(1).to_broadcast([P, P, PACK]), ALU.mult)
+            nc.vector.tensor_tensor(w_woven[a][:], p_ps[a][:].rearrange("s t q -> s q t"), vs_col.unsqueeze(1).to_broadcast([P, P, PACK]), ALU.mult)
 
-        turn_values(0)
+        gather_values_half(0)
         for a in range(QT):
             nc.vector.tensor_reduce(neg_max[a], score_ps[a][:], axis=AXX, op=ALU.max, negate=True)
             nc.scalar.activation(
@@ -195,27 +157,31 @@ def tile_attend_x_append128_gate_topk_kernel(tc, qT, kT, vT, new_kT, new_vT, vs,
             )
             for t in range(PACK):
                 nc.tensor.transpose(p_ps[a][:, t, :], p_t[a][:, t, :], identity[:])
-        nc.vector.tensor_copy(dealt(v_picked[1]), v_tile[1][:].indirect(offs_t[:]))
-        turn_values(1)
+        nc.vector.tensor_copy(v_picked[0][:], v_tile[0][:].indirect(offs_t[:]))
+        gather_values_half(1)
+        v_ps = [psum.tile([P, PACK // PAIR, P], F32, name=f"v_ps{h}", tag=f"score_ps{1 - h}") for h in range(ET)]
+        for h in range(ET):
+            for u in range(PACK // PAIR):
+                nc.tensor.transpose(v_ps[h][:, u, :], v_picked[h][:].bitcast(F32).rearrange("p (s u) -> p u s", u=PAIR)[:, u, :], identity[:])
 
         nc.scalar.activation(tanh_t[:], og_t[:], ACT.Tanh, scale=0.5)
-        weave_values(0)
-        gate = keep.tile([P, QT, DV], F32, name="gate")
-        nc.scalar.activation(gate[:], tanh_t[:], ACT.Copy, scale=0.5, bias=0.5)
-        weave_values(1)
+        for h in range(ET):
+            nc.scalar.copy(as_words(v_woven[h][:]), v_ps[h][:].rearrange("s u e -> s e u"))
+        for h in range(ET):
+            cols = slice(h * P, (h + 1) * P)
+            nc.scalar.activation(gate[:, :, cols], tanh_t[:, :, cols], ACT.Copy, scale=0.5, bias=0.5)
 
         weigh(0)
-        quantize(v_codes[:, 0:P], v_scales[:, 0:P], v_woven[0][:])
         weigh(1)
         for a in range(QT):
             quantize(w_codes[a][:], w_scales[a][:], w_woven[a][:])
+        quantize(v_codes[:, 0:P], v_scales[:, 0:P], v_woven[0][:])
         quantize(v_codes[:, P:DV], v_scales[:, P:DV], v_woven[1][:])
-        inv_sum = keep.tile([P, QT], F32, name="inv_sum", tag="w_woven0", align_bytes=MX_ALIGN)
-        nc.vector.reciprocal(inv_sum[:], row_sum[:])
+        nc.vector.reciprocal(inv_sum[:], row_sum)
 
         y_ps = [
             [psum.tile([P, P], F32, name="y_ps00"), psum.tile([P, P], F32, name="y_ps01", tag="vs_ps")],
-            [psum.tile([P, P], F32, name="y_ps10"), psum.tile([P, P], F32, name="y_ps11", tag="score_ps0")],
+            [psum.tile([P, P], F32, name="y_ps10"), psum.tile([P, P], F32, name="y_ps11")],
         ]
         for h in range(ET):
             cols = slice(h * P, (h + 1) * P)

@@ -58,12 +58,15 @@ def tile_attend_x_append128_gate_topk_kernel(tc, qT, kT, vT, new_kT, new_vT, vs,
         og_t = keep.tile([P, QT, DV], F32, name="og_t")
         k_pairs_row = keep.tile([P, N * PACK], BF16, name="k_pairs_row")
         k_pairs = k_pairs_row[:].rearrange("p (c u i j) -> p c u i j", c=2, u=PACK // PAIR, j=PAIR)
-        k_woven = [keep.tile([P, HALF, PACK], BF16, name=f"k_woven{c}", align_bytes=MX_ALIGN) for c in range(2)]
+        k_woven = [
+            overlap.tile([P, HALF, PACK], BF16, name="k_woven0", align_bytes=MX_ALIGN, offset=0),
+            overlap.tile([P, HALF, PACK], BF16, name="k_woven1", align_bytes=MX_ALIGN, offset=2048),
+        ]
         q_woven = keep.tile([P, NQ, PACK], BF16, name="q_woven", align_bytes=MX_ALIGN)
         q_codes = keep.tile([P, NQ], U32, name="q_codes", tag="q_codes", align_bytes=MX_ALIGN)
         q_scales = keep.tile([P, NQ], U8, name="q_scales", align_bytes=MX_ALIGN)
         k_codes = keep.tile([P, N], U32, name="k_codes", align_bytes=MX_ALIGN)
-        k_scales = [keep.tile([P, HALF], U8, name="k_scales0", align_bytes=MX_ALIGN)[:], overlap.tile([P, HALF], U8, name="k_scales1", align_bytes=MX_ALIGN, offset=2 * N)[:]]
+        k_scales = [keep.tile([P, HALF], U8, name=f"k_scales{c}", align_bytes=MX_ALIGN)[:] for c in range(2)]
         vs_row = keep.tile([P, N], F32, name="vs_row")
         v_picked1 = keep.tile([P, N], BF16, name="v_picked1")
         v_woven = [keep.tile([P, P, PACK], BF16, name=f"v_woven{h}", align_bytes=MX_ALIGN) for h in range(ET)]
@@ -71,7 +74,7 @@ def tile_attend_x_append128_gate_topk_kernel(tc, qT, kT, vT, new_kT, new_vT, vs,
         v_scales = keep.tile([P, DV], U8, name="v_scales", align_bytes=MX_ALIGN)
         tanh_t = keep.tile([P, QT, DV], F32, name="tanh_t")
         gate = keep.tile([P, QT, DV], F32, name="gate")
-        neg_max = [v_picked1[:, N - PAIR : N].bitcast(F32), tanh_t[:, 0, 0:1]]
+        neg_max = [as_words(v_woven[1][:])[:, 0, 0:1], gate[:, 0, 0:1]]
         row_sum = new_v[:, 1, 0:QT]
         vs_col = new_k_rest[:, PACK - 2, 0:PACK]
         inv_sum = keep.tile([P, QT], F32, name="inv_sum")
@@ -89,7 +92,6 @@ def tile_attend_x_append128_gate_topk_kernel(tc, qT, kT, vT, new_kT, new_vT, vs,
         new_k_rows = new_kT.rearrange("(p t) n -> p t n", t=PACK)
         v_rows = vT.rearrange("(h p) n -> p h n", p=P)
         out_rows = out[0].rearrange("(a p) (h e) -> h p a e", p=P, e=P)
-        offs_half = [offs_t[:, c * HALF // LIST_ROWS : (c + 1) * HALF // LIST_ROWS] for c in range(2)]
 
         nc.sync.dma_start(offs_t[:], offs)
         nc.scalar.dma_start(vs_t[P - 1 : P, :], vs[0:1, :])
@@ -102,7 +104,7 @@ def tile_attend_x_append128_gate_topk_kernel(tc, qT, kT, vT, new_kT, new_vT, vs,
             nc.sync.dma_start(k_plane[t][:], k_rows[:, t, :])
         nc.sync.dma_start(q_planes[:], qT[0].rearrange("(p t) n -> p t n", t=PACK))
         nc.sync.dma_start(new_v[:], new_vT.rearrange("(h p) n -> p h n", p=P))
-        for h in range(ET):
+        for h in (1, 0):
             nc.sync.dma_start(v_tile[h][:], v_rows[:, h, :])
         nc.sync.dma_start(og_t[:], og[0].rearrange("(a p) e -> p a e", p=P))
 
@@ -117,21 +119,14 @@ def tile_attend_x_append128_gate_topk_kernel(tc, qT, kT, vT, new_kT, new_vT, vs,
             source = new_k_first[:] if t == 0 else new_k_rest[:, t - 1, :]
             nc.scalar.activation(k_plane[t][:].indirect(slots_t[:]), source, ACT.Copy)
             u, j = divmod(t, PAIR)
-            if t < PACK - 1:
-                nc.vector.tensor_copy(k_pairs[:, :, u, :, j], k_plane[t][:].indirect(offs_t[:]))
-            else:
-                for c in range(2):
-                    nc.vector.tensor_copy(k_pairs[:, c, u, :, j], k_plane[t][:].indirect(offs_half[c]))
+            nc.vector.tensor_copy(k_pairs[:, :, u, :, j], k_plane[t][:].indirect(offs_t[:]))
         nc.scalar.copy(vs_col, vs_ps[:, :, P - 1])
+        nc.scalar.activation(q_woven[:], q_planes[:].rearrange("p t n -> p n t"), ACT.Copy)
+        quantize(q_codes[:], q_scales[:], q_woven[:])
         for c in range(2):
-            nc.scalar.copy(as_words(k_woven[c][:]), k_pairs_row[:, c * 2 * N : (c + 1) * 2 * N].bitcast(F32).rearrange("p (u n) -> p n u", u=PACK // PAIR))
-
-        nc.gpsimd.tensor_scalar(
-            q_woven[:].rearrange("p (c i) t -> p c t i", i=PACK), q_planes[:].rearrange("p t (c i) -> p c t i", i=PACK), 1.0, 0.0, ALU.mult, ALU.add
-        )
+            nc.vector.tensor_copy(as_words(k_woven[c][:]), k_pairs_row[:, c * 2 * N : (c + 1) * 2 * N].bitcast(F32).rearrange("p (u n) -> p n u", u=PACK // PAIR))
 
         quantize(k_codes[:, 0:HALF], k_scales[0], k_woven[0][:])
-        quantize(q_codes[:], q_scales[:], q_woven[:])
         quantize(k_codes[:, HALF:N], k_scales[1], k_woven[1][:])
         for a in range(QT):
             rows = slice(a * P, (a + 1) * P)
@@ -143,13 +138,13 @@ def tile_attend_x_append128_gate_topk_kernel(tc, qT, kT, vT, new_kT, new_vT, vs,
         nc.vector.tensor_copy(v_tile[0][:].indirect(slots_t[:]), new_v[:, 0, :])
         nc.scalar.activation(v_tile[1][:].indirect(slots_t[:]), new_v[:, 1, :], ACT.Copy)
 
-        def gather_values_half(c):
-            nc.scalar.activation(v_picked[1][:, c * HALF : (c + 1) * HALF], v_tile[1][:].indirect(offs_half[c]), ACT.Copy)
-
         def weigh(a):
             nc.vector.tensor_tensor(w_woven[a][:], p_ps[a][:].rearrange("s t q -> s q t"), vs_col.unsqueeze(1).to_broadcast([P, P, PACK]), ALU.mult)
 
-        gather_values_half(0)
+        nc.scalar.activation(v_picked[1][:], v_tile[1][:].indirect(offs_t[:]), ACT.Copy)
+        v_ps = [psum.tile([P, PACK // PAIR, P], F32, name="v_ps0", tag="score_ps1"), psum.tile([P, PACK // PAIR, P], F32, name="v_ps1")]
+        for u in range(PACK // PAIR):
+            nc.tensor.transpose(v_ps[1][:, u, :], v_picked[1][:].bitcast(F32).rearrange("p (s u) -> p u s", u=PAIR)[:, u, :], identity[:])
         for a in range(QT):
             nc.vector.tensor_reduce(neg_max[a], score_ps[a][:], axis=AXX, op=ALU.max, negate=True)
             nc.scalar.activation(
@@ -157,37 +152,32 @@ def tile_attend_x_append128_gate_topk_kernel(tc, qT, kT, vT, new_kT, new_vT, vs,
             )
             for t in range(PACK):
                 nc.tensor.transpose(p_ps[a][:, t, :], p_t[a][:, t, :], identity[:])
-        nc.vector.tensor_copy(v_picked[0][:], v_tile[0][:].indirect(offs_t[:]))
-        gather_values_half(1)
-        v_ps = [psum.tile([P, PACK // PAIR, P], F32, name=f"v_ps{h}", tag=f"score_ps{1 - h}") for h in range(ET)]
-        for h in range(ET):
-            for u in range(PACK // PAIR):
-                nc.tensor.transpose(v_ps[h][:, u, :], v_picked[h][:].bitcast(F32).rearrange("p (s u) -> p u s", u=PAIR)[:, u, :], identity[:])
+        nc.vector.tensor_copy(v_picked[0][:].rearrange("p (u s j) -> p s u j", u=PACK // PAIR, j=PAIR), v_tile[0][:].indirect(offs_t[:]))
+        for u in range(PACK // PAIR):
+            nc.tensor.transpose(v_ps[0][:, u, :], v_picked[0][:].bitcast(F32)[:, u * P : (u + 1) * P], identity[:])
 
+        nc.scalar.copy(as_words(v_woven[1][:]), v_ps[1][:].rearrange("s u e -> s e u"))
         nc.scalar.activation(tanh_t[:], og_t[:], ACT.Tanh, scale=0.5)
-        for h in range(ET):
-            nc.scalar.copy(as_words(v_woven[h][:]), v_ps[h][:].rearrange("s u e -> s e u"))
-        for h in range(ET):
-            cols = slice(h * P, (h + 1) * P)
-            nc.scalar.activation(gate[:, :, cols], tanh_t[:, :, cols], ACT.Copy, scale=0.5, bias=0.5)
+        nc.scalar.activation(gate[:], tanh_t[:], ACT.Copy, scale=0.5, bias=0.5)
+        nc.scalar.copy(as_words(v_woven[0][:]), v_ps[0][:].rearrange("s u e -> s e u"))
 
         weigh(0)
+        quantize(v_codes[:, P:DV], v_scales[:, P:DV], v_woven[1][:])
         weigh(1)
         for a in range(QT):
             quantize(w_codes[a][:], w_scales[a][:], w_woven[a][:])
         quantize(v_codes[:, 0:P], v_scales[:, 0:P], v_woven[0][:])
-        quantize(v_codes[:, P:DV], v_scales[:, P:DV], v_woven[1][:])
         nc.vector.reciprocal(inv_sum[:], row_sum)
 
         y_ps = [
             [psum.tile([P, P], F32, name="y_ps00"), psum.tile([P, P], F32, name="y_ps01", tag="vs_ps")],
-            [psum.tile([P, P], F32, name="y_ps10"), psum.tile([P, P], F32, name="y_ps11")],
+            [psum.tile([P, P], F32, name="y_ps10"), psum.tile([P, P], F32, name="y_ps11", tag="score_ps0")],
         ]
-        for h in range(ET):
+        for h in (1, 0):
             cols = slice(h * P, (h + 1) * P)
             for a in range(QT):
                 product(y_ps[a][h][:], w_codes[a][:], w_scales[a][:], v_codes[:, cols], v_scales[:, cols])
-        for h in range(ET):
+        for h in (1, 0):
             cols = slice(h * P, (h + 1) * P)
             for a in range(QT):
                 nc.vector.scalar_tensor_tensor(result[h][:, a, :], y_ps[a][h][:], inv_sum[:, a : a + 1], gate[:, a, cols], ALU.mult, ALU.mult)

@@ -59,14 +59,14 @@ def tile_attend_x_append128_gate_topk_kernel(tc, qT, kT, vT, new_kT, new_vT, vs,
         k_pairs_row = keep.tile([P, N * PACK], BF16, name="k_pairs_row")
         k_pairs = k_pairs_row[:].rearrange("p (c u i j) -> p c u i j", c=2, u=PACK // PAIR, j=PAIR)
         k_woven = [
-            overlap.tile([P, HALF, PACK], BF16, name="k_woven0", align_bytes=MX_ALIGN, offset=0),
-            overlap.tile([P, HALF, PACK], BF16, name="k_woven1", align_bytes=MX_ALIGN, offset=2048),
+            keep.tile([P, HALF, PACK], BF16, name="k_woven0", align_bytes=MX_ALIGN),
+            keep.tile([P, HALF, PACK], BF16, name="k_woven1", align_bytes=MX_ALIGN),
         ]
         q_woven = keep.tile([P, NQ, PACK], BF16, name="q_woven", align_bytes=MX_ALIGN)
         q_codes = keep.tile([P, NQ], U32, name="q_codes", tag="q_codes", align_bytes=MX_ALIGN)
         q_scales = keep.tile([P, NQ], U8, name="q_scales", align_bytes=MX_ALIGN)
         k_codes = keep.tile([P, N], U32, name="k_codes", align_bytes=MX_ALIGN)
-        k_scales = [keep.tile([P, HALF], U8, name=f"k_scales{c}", align_bytes=MX_ALIGN)[:] for c in range(2)]
+        k_scales = [overlap.tile([P, HALF], U8, name=f"k_scales{c}", align_bytes=MX_ALIGN, offset=c * HALF)[:] for c in range(2)]
         vs_row = keep.tile([P, N], F32, name="vs_row")
         v_picked1 = keep.tile([P, N], BF16, name="v_picked1")
         v_woven = [keep.tile([P, P, PACK], BF16, name=f"v_woven{h}", align_bytes=MX_ALIGN) for h in range(ET)]
@@ -76,7 +76,7 @@ def tile_attend_x_append128_gate_topk_kernel(tc, qT, kT, vT, new_kT, new_vT, vs,
         gate = keep.tile([P, QT, DV], F32, name="gate")
         neg_max = [as_words(v_woven[1][:])[:, 0, 0:1], gate[:, 0, 0:1]]
         row_sum = new_v[:, 1, 0:QT]
-        vs_col = new_k_rest[:, PACK - 2, 0:PACK]
+        vs_col = new_v[:, 1, 8 : 8 + PACK]
         inv_sum = keep.tile([P, QT], F32, name="inv_sum")
         p_t = [keep.tile([P, PACK, P], F32, name=f"p_t{a}") for a in range(QT)]
         w_woven = [keep.tile([P, P, PACK], BF16, name=f"w_woven{a}", align_bytes=MX_ALIGN) for a in range(QT)]
@@ -92,6 +92,7 @@ def tile_attend_x_append128_gate_topk_kernel(tc, qT, kT, vT, new_kT, new_vT, vs,
         new_k_rows = new_kT.rearrange("(p t) n -> p t n", t=PACK)
         v_rows = vT.rearrange("(h p) n -> p h n", p=P)
         out_rows = out[0].rearrange("(a p) (h e) -> h p a e", p=P, e=P)
+        offs_half = [offs_t[:, c * HALF // LIST_ROWS : (c + 1) * HALF // LIST_ROWS] for c in range(2)]
 
         nc.sync.dma_start(offs_t[:], offs)
         nc.scalar.dma_start(vs_t[P - 1 : P, :], vs[0:1, :])
@@ -102,8 +103,8 @@ def tile_attend_x_append128_gate_topk_kernel(tc, qT, kT, vT, new_kT, new_vT, vs,
         nc.vector.memset(vs_t[0 : P - 1, :], 0.0)
         for t in range(1, PACK):
             nc.sync.dma_start(k_plane[t][:], k_rows[:, t, :])
-        nc.sync.dma_start(q_planes[:], qT[0].rearrange("(p t) n -> p t n", t=PACK))
         nc.sync.dma_start(new_v[:], new_vT.rearrange("(h p) n -> p h n", p=P))
+        nc.sync.dma_start(q_planes[:], qT[0].rearrange("(p t) n -> p t n", t=PACK))
         for h in (1, 0):
             nc.sync.dma_start(v_tile[h][:], v_rows[:, h, :])
         nc.sync.dma_start(og_t[:], og[0].rearrange("(a p) e -> p a e", p=P))
@@ -119,8 +120,11 @@ def tile_attend_x_append128_gate_topk_kernel(tc, qT, kT, vT, new_kT, new_vT, vs,
             source = new_k_first[:] if t == 0 else new_k_rest[:, t - 1, :]
             nc.scalar.activation(k_plane[t][:].indirect(slots_t[:]), source, ACT.Copy)
             u, j = divmod(t, PAIR)
-            nc.vector.tensor_copy(k_pairs[:, :, u, :, j], k_plane[t][:].indirect(offs_t[:]))
-        nc.scalar.copy(vs_col, vs_ps[:, :, P - 1])
+            if t < PACK - 1:
+                nc.vector.tensor_copy(k_pairs[:, :, u, :, j], k_plane[t][:].indirect(offs_t[:]))
+            else:
+                for c in range(2):
+                    nc.vector.tensor_copy(k_pairs[:, c, u, :, j], k_plane[t][:].indirect(offs_half[c]))
         nc.scalar.activation(q_woven[:], q_planes[:].rearrange("p t n -> p n t"), ACT.Copy)
         quantize(q_codes[:], q_scales[:], q_woven[:])
         for c in range(2):
@@ -137,6 +141,7 @@ def tile_attend_x_append128_gate_topk_kernel(tc, qT, kT, vT, new_kT, new_vT, vs,
         v_picked = [keep.tile([P, N], BF16, name="v_picked0", tag="q_codes", align_bytes=MX_ALIGN), v_picked1]
         nc.vector.tensor_copy(v_tile[0][:].indirect(slots_t[:]), new_v[:, 0, :])
         nc.scalar.activation(v_tile[1][:].indirect(slots_t[:]), new_v[:, 1, :], ACT.Copy)
+        nc.scalar.copy(vs_col, vs_ps[:, :, P - 1])
 
         def weigh(a):
             nc.vector.tensor_tensor(w_woven[a][:], p_ps[a][:].rearrange("s t q -> s q t"), vs_col.unsqueeze(1).to_broadcast([P, P, PACK]), ALU.mult)

@@ -94,10 +94,10 @@ def tile_attend_x_append128_gate_topk_kernel(tc, qT, kT, vT, new_kT, new_vT, vs,
         out_rows = out[0].rearrange("(a p) (h e) -> h p a e", p=P, e=P)
         offs_half = [offs_t[:, c * HALF // LIST_ROWS : (c + 1) * HALF // LIST_ROWS] for c in range(2)]
 
-        nc.sync.dma_start(offs_t[:], offs)
-        nc.scalar.dma_start(vs_t[P - 1 : P, :], vs[0:1, :])
-        nc.scalar.dma_start(new_k_loaded[:], new_k_rows[:, 0, :])
         nc.sync.dma_start(k_plane[0][:], k_rows[:, 0, :])
+        nc.scalar.dma_start(new_k_loaded[:], new_k_rows[:, 0, :])
+        nc.scalar.dma_start(vs_t[P - 1 : P, :], vs[0:1, :])
+        nc.sync.dma_start(offs_t[:], offs)
         nc.sync.dma_start(slots_t[:], slots)
         nc.sync.dma_start(new_k_rest[:], new_k_rows[:, 1:PACK, :])
         nc.vector.memset(vs_t[0 : P - 1, :], 0.0)

@@ -21,6 +21,8 @@ LIST_ROWS = 16
 QT = NQ // P
 ET = DV // P
 HALF = N // 2
+SCALAR_SLOTS = 192
+LINE = 4
 MX_ALIGN = 64
 
 FLOPS = 2 * NQ * N * (D + DV)
@@ -103,8 +105,8 @@ def tile_attend_x_append128_gate_topk_kernel(tc, qT, kT, vT, new_kT, new_vT, vs,
         nc.vector.memset(vs_t[0 : P - 1, :], 0.0)
         for t in range(1, PACK):
             nc.sync.dma_start(k_plane[t][:], k_rows[:, t, :])
-        nc.sync.dma_start(new_v[:], new_vT.rearrange("(h p) n -> p h n", p=P))
         nc.sync.dma_start(q_planes[:], qT[0].rearrange("(p t) n -> p t n", t=PACK))
+        nc.sync.dma_start(new_v[:], new_vT.rearrange("(h p) n -> p h n", p=P))
         for h in (1, 0):
             nc.sync.dma_start(v_tile[h][:], v_rows[:, h, :])
         nc.sync.dma_start(og_t[:], og[0].rearrange("(a p) e -> p a e", p=P))
@@ -125,7 +127,7 @@ def tile_attend_x_append128_gate_topk_kernel(tc, qT, kT, vT, new_kT, new_vT, vs,
             else:
                 for c in range(2):
                     nc.vector.tensor_copy(k_pairs[:, c, u, :, j], k_plane[t][:].indirect(offs_half[c]))
-        nc.scalar.activation(q_woven[:], q_planes[:].rearrange("p t n -> p n t"), ACT.Copy)
+        nc.scalar.activation(q_woven[:].rearrange("p (c i) t -> p c t i", i=LINE), q_planes[:].rearrange("p t (c i) -> p c t i", i=LINE), ACT.Copy)
         quantize(q_codes[:], q_scales[:], q_woven[:])
         for c in range(2):
             nc.vector.tensor_copy(as_words(k_woven[c][:]), k_pairs_row[:, c * 2 * N : (c + 1) * 2 * N].bitcast(F32).rearrange("p (u n) -> p n u", u=PACK // PAIR))
@@ -139,14 +141,15 @@ def tile_attend_x_append128_gate_topk_kernel(tc, qT, kT, vT, new_kT, new_vT, vs,
                 product(score_ps[a][:, cols], q_codes[:, rows], q_scales[:, rows], k_codes[:, cols], k_scales[c])
 
         v_picked = [keep.tile([P, N], BF16, name="v_picked0", tag="q_codes", align_bytes=MX_ALIGN), v_picked1]
-        nc.vector.tensor_copy(v_tile[0][:].indirect(slots_t[:]), new_v[:, 0, :])
         nc.scalar.activation(v_tile[1][:].indirect(slots_t[:]), new_v[:, 1, :], ACT.Copy)
         nc.scalar.copy(vs_col, vs_ps[:, :, P - 1])
 
         def weigh(a):
             nc.vector.tensor_tensor(w_woven[a][:], p_ps[a][:].rearrange("s t q -> s q t"), vs_col.unsqueeze(1).to_broadcast([P, P, PACK]), ALU.mult)
 
-        nc.scalar.activation(v_picked[1][:], v_tile[1][:].indirect(offs_t[:]), ACT.Copy)
+        nc.scalar.activation(v_picked[1][:, 0:SCALAR_SLOTS], v_tile[1][:].indirect(offs_t[:, 0 : SCALAR_SLOTS // LIST_ROWS]), ACT.Copy)
+        nc.vector.tensor_copy(v_picked[1][:, SCALAR_SLOTS:N], v_tile[1][:].indirect(offs_t[:, SCALAR_SLOTS // LIST_ROWS : N // LIST_ROWS]))
+        nc.scalar.activation(v_tile[0][:].indirect(slots_t[:]), new_v[:, 0, :], ACT.Copy)
         v_ps = [psum.tile([P, PACK // PAIR, P], F32, name="v_ps0", tag="score_ps1"), psum.tile([P, PACK // PAIR, P], F32, name="v_ps1")]
         for u in range(PACK // PAIR):
             nc.tensor.transpose(v_ps[1][:, u, :], v_picked[1][:].bitcast(F32).rearrange("p (s u) -> p u s", u=PAIR)[:, u, :], identity[:])
@@ -161,8 +164,8 @@ def tile_attend_x_append128_gate_topk_kernel(tc, qT, kT, vT, new_kT, new_vT, vs,
         for u in range(PACK // PAIR):
             nc.tensor.transpose(v_ps[0][:, u, :], v_picked[0][:].bitcast(F32)[:, u * P : (u + 1) * P], identity[:])
 
-        nc.scalar.copy(as_words(v_woven[1][:]), v_ps[1][:].rearrange("s u e -> s e u"))
         nc.scalar.activation(tanh_t[:], og_t[:], ACT.Tanh, scale=0.5)
+        nc.scalar.copy(as_words(v_woven[1][:]), v_ps[1][:].rearrange("s u e -> s e u"))
         nc.scalar.activation(gate[:], tanh_t[:], ACT.Copy, scale=0.5, bias=0.5)
         nc.scalar.copy(as_words(v_woven[0][:]), v_ps[0][:].rearrange("s u e -> s e u"))
 

@@ -21,7 +21,7 @@ LIST_ROWS = 16
 QT = NQ // P
 ET = DV // P
 HALF = N // 2
-SCALAR_SLOTS = 192
+SCALAR_SLOTS = 256
 LINE = 4
 MX_ALIGN = 64
 
@@ -73,12 +73,15 @@ def tile_attend_x_append128_gate_topk_kernel(tc, qT, kT, vT, new_kT, new_vT, vs,
         v_picked1 = keep.tile([P, N], BF16, name="v_picked1")
         v_woven = [keep.tile([P, P, PACK], BF16, name=f"v_woven{h}", align_bytes=MX_ALIGN) for h in range(ET)]
         v_codes = keep.tile([P, DV], U32, name="v_codes", align_bytes=MX_ALIGN)
-        v_scales = keep.tile([P, DV], U8, name="v_scales", align_bytes=MX_ALIGN)
+        vs_col = overlap.tile([P, PACK], F32, name="vs_col", align_bytes=MX_ALIGN, offset=N)[:]
+        v_scales = [
+            overlap.tile([P, P], U8, name="v_scales0", align_bytes=MX_ALIGN, offset=N),
+            keep.tile([P, P], U8, name="v_scales1", align_bytes=MX_ALIGN),
+        ]
         tanh_t = keep.tile([P, QT, DV], F32, name="tanh_t")
         gate = keep.tile([P, QT, DV], F32, name="gate")
         neg_max = [as_words(v_woven[1][:])[:, 0, 0:1], gate[:, 0, 0:1]]
         row_sum = new_v[:, 1, 0:QT]
-        vs_col = new_v[:, 1, 8 : 8 + PACK]
         inv_sum = keep.tile([P, QT], F32, name="inv_sum")
         p_t = [keep.tile([P, PACK, P], F32, name=f"p_t{a}") for a in range(QT)]
         w_woven = [keep.tile([P, P, PACK], BF16, name=f"w_woven{a}", align_bytes=MX_ALIGN) for a in range(QT)]
@@ -128,12 +131,13 @@ def tile_attend_x_append128_gate_topk_kernel(tc, qT, kT, vT, new_kT, new_vT, vs,
                 for c in range(2):
                     nc.vector.tensor_copy(k_pairs[:, c, u, :, j], k_plane[t][:].indirect(offs_half[c]))
         nc.scalar.activation(q_woven[:].rearrange("p (c i) t -> p c t i", i=LINE), q_planes[:].rearrange("p t (c i) -> p c t i", i=LINE), ACT.Copy)
-        quantize(q_codes[:], q_scales[:], q_woven[:])
+        quantize(q_codes[:, 0:P], q_scales[:, 0:P], q_woven[:, 0:P, :])
         for c in range(2):
             nc.vector.tensor_copy(as_words(k_woven[c][:]), k_pairs_row[:, c * 2 * N : (c + 1) * 2 * N].bitcast(F32).rearrange("p (u n) -> p n u", u=PACK // PAIR))
 
         quantize(k_codes[:, 0:HALF], k_scales[0], k_woven[0][:])
         quantize(k_codes[:, HALF:N], k_scales[1], k_woven[1][:])
+        quantize(q_codes[:, P:NQ], q_scales[:, P:NQ], q_woven[:, P:NQ, :])
         for a in range(QT):
             rows = slice(a * P, (a + 1) * P)
             for c in range(2):
@@ -164,17 +168,17 @@ def tile_attend_x_append128_gate_topk_kernel(tc, qT, kT, vT, new_kT, new_vT, vs,
         for u in range(PACK // PAIR):
             nc.tensor.transpose(v_ps[0][:, u, :], v_picked[0][:].bitcast(F32)[:, u * P : (u + 1) * P], identity[:])
 
-        nc.scalar.activation(tanh_t[:], og_t[:], ACT.Tanh, scale=0.5)
         nc.scalar.copy(as_words(v_woven[1][:]), v_ps[1][:].rearrange("s u e -> s e u"))
-        nc.scalar.activation(gate[:], tanh_t[:], ACT.Copy, scale=0.5, bias=0.5)
+        nc.scalar.activation(tanh_t[:], og_t[:], ACT.Tanh, scale=0.5)
         nc.scalar.copy(as_words(v_woven[0][:]), v_ps[0][:].rearrange("s u e -> s e u"))
+        nc.scalar.activation(gate[:], tanh_t[:], ACT.Copy, scale=0.5, bias=0.5)
 
         weigh(0)
-        quantize(v_codes[:, P:DV], v_scales[:, P:DV], v_woven[1][:])
+        quantize(v_codes[:, P:DV], v_scales[1][:], v_woven[1][:])
         weigh(1)
         for a in range(QT):
             quantize(w_codes[a][:], w_scales[a][:], w_woven[a][:])
-        quantize(v_codes[:, 0:P], v_scales[:, 0:P], v_woven[0][:])
+        quantize(v_codes[:, 0:P], v_scales[0][:], v_woven[0][:])
         nc.vector.reciprocal(inv_sum[:], row_sum)
 
         y_ps = [
@@ -184,7 +188,7 @@ def tile_attend_x_append128_gate_topk_kernel(tc, qT, kT, vT, new_kT, new_vT, vs,
         for h in (1, 0):
             cols = slice(h * P, (h + 1) * P)
             for a in range(QT):
-                product(y_ps[a][h][:], w_codes[a][:], w_scales[a][:], v_codes[:, cols], v_scales[:, cols])
+                product(y_ps[a][h][:], w_codes[a][:], w_scales[a][:], v_codes[:, cols], v_scales[h][:])
         for h in (1, 0):
             cols = slice(h * P, (h + 1) * P)
             for a in range(QT):

@@ -149,7 +149,12 @@ def tile_attend_x_append128_gate_topk_kernel(tc, qT, kT, vT, new_kT, new_vT, vs,
         nc.scalar.copy(vs_col, vs_ps[:, :, P - 1])
 
         def weigh(a):
-            nc.vector.tensor_tensor(w_woven[a][:], p_ps[a][:].rearrange("s t q -> s q t"), vs_col.unsqueeze(1).to_broadcast([P, P, PACK]), ALU.mult)
+            nc.vector.tensor_tensor(
+                w_woven[a][:].rearrange("s (c i) t -> s c t i", i=PAIR),
+                p_ps[a][:].rearrange("s t (c i) -> s c t i", i=PAIR),
+                vs_col.unsqueeze(1).unsqueeze(3).to_broadcast([P, P // PAIR, PACK, PAIR]),
+                ALU.mult,
+            )
 
         nc.scalar.activation(v_picked[1][:, 0:SCALAR_SLOTS], v_tile[1][:].indirect(offs_t[:, 0 : SCALAR_SLOTS // LIST_ROWS]), ACT.Copy)
         nc.vector.tensor_copy(v_picked[1][:, SCALAR_SLOTS:N], v_tile[1][:].indirect(offs_t[:, SCALAR_SLOTS // LIST_ROWS : N // LIST_ROWS]))

from contextlib import ExitStack

import concourse.mybir as mybir
from concourse.masks import make_identity

F32 = mybir.dt.float32
BF16 = mybir.dt.bfloat16
U32 = mybir.dt.uint32
U16 = mybir.dt.uint16
U8 = mybir.dt.uint8
FP8X4 = mybir.dt.float8_e4m3fn_x4
ACT = mybir.ActivationFunctionType
ALU = mybir.AluOpType
AXX = mybir.AxisListType.X

D, DV, T, N, NQ, NEW = 512, 256, 1024, 512, 256, 128
P = 128
PACK = 4
PAIR = 2
LIST_ROWS = 16
QT = NQ // P
ET = DV // P
HALF = N // 2
SCALAR_SLOTS = 256
LINE = 4
MX_ALIGN = 64

FLOPS = 2 * NQ * N * (D + DV)


def tile_attend_x_append128_gate_topk_kernel(tc, qT, kT, vT, new_kT, new_vT, vs, og, offs, slots, out):
    nc = tc.nc

    def quantize(codes, scales, woven):
        nc.vector.quantize_mx(out=codes.bitcast(FP8X4), scales=scales, in_=woven.rearrange("p n t -> p (n t)"))

    def product(acc, lhs_codes, lhs_scales, rhs_codes, rhs_scales):
        nc.tensor.matmul_mx(
            acc, lhsT=lhs_codes.bitcast(FP8X4), lhsT_scale=lhs_scales, rhs=rhs_codes.bitcast(FP8X4), rhs_scale=rhs_scales, start=True, stop=True
        )

    def as_words(woven):
        return woven.rearrange("p n t -> p (n t)").bitcast(F32).rearrange("p (n u) -> p n u", u=PACK // PAIR)

    with ExitStack() as ctx:
        keep = ctx.enter_context(tc.tile_pool(name="keep", bufs=1))
        overlap = ctx.enter_context(tc.tile_pool(name="overlap", bufs=1))
        psum = ctx.enter_context(tc.psum_pool(name="psum", bufs=1))

        slots_t = keep.tile([P, NEW // LIST_ROWS], U16, name="slots_t")
        offs_t = keep.tile([P, N // LIST_ROWS], U16, name="offs_t")
        k_plane = [keep.tile([P, T], F32, name=f"k_plane{t}") for t in range(PACK)]
        v_tile = [keep.tile([P, T], F32, name=f"v_tile{h}") for h in range(ET)]
        new_k_loaded = keep.tile([P, NEW], F32, name="new_k_loaded")
        new_k_first = keep.tile([P, NEW], F32, name="new_k_first")
        new_k_rest = keep.tile([P, PACK - 1, NEW], F32, name="new_k_rest")
        new_v = keep.tile([P, ET, NEW], F32, name="new_v")
        q_planes = overlap.tile([P, PACK, NQ], F32, name="q_planes", align_bytes=MX_ALIGN, offset=0)
        vs_t = keep.tile([P, T], F32, name="vs_t")
        og_t = keep.tile([P, QT, DV], F32, name="og_t")
        k_pairs_row = keep.tile([P, N * PACK], BF16, name="k_pairs_row")
        k_pairs = k_pairs_row[:].rearrange("p (c u i j) -> p c u i j", c=2, u=PACK // PAIR, j=PAIR)
        k_woven = [
            keep.tile([P, HALF, PACK], BF16, name="k_woven0", align_bytes=MX_ALIGN),
            keep.tile([P, HALF, PACK], BF16, name="k_woven1", align_bytes=MX_ALIGN),
        ]
        q_woven = keep.tile([P, NQ, PACK], BF16, name="q_woven", align_bytes=MX_ALIGN)
        q_codes = keep.tile([P, NQ], U32, name="q_codes", tag="q_codes", align_bytes=MX_ALIGN)
        q_scales = keep.tile([P, NQ], U8, name="q_scales", align_bytes=MX_ALIGN)
        k_codes = keep.tile([P, N], U32, name="k_codes", align_bytes=MX_ALIGN)
        k_scales = [overlap.tile([P, HALF], U8, name=f"k_scales{c}", align_bytes=MX_ALIGN, offset=c * HALF)[:] for c in range(2)]
        vs_row = keep.tile([P, N], F32, name="vs_row")
        v_picked1 = keep.tile([P, N], BF16, name="v_picked1")
        v_woven = [keep.tile([P, P, PACK], BF16, name=f"v_woven{h}", align_bytes=MX_ALIGN) for h in range(ET)]
        v_codes = keep.tile([P, DV], U32, name="v_codes", align_bytes=MX_ALIGN)
        vs_col = overlap.tile([P, PACK], F32, name="vs_col", align_bytes=MX_ALIGN, offset=N)[:]
        v_scales = [
            overlap.tile([P, P], U8, name="v_scales0", align_bytes=MX_ALIGN, offset=N),
            keep.tile([P, P], U8, name="v_scales1", align_bytes=MX_ALIGN),
        ]
        tanh_t = keep.tile([P, QT, DV], F32, name="tanh_t")
        gate = keep.tile([P, QT, DV], F32, name="gate")
        neg_max = [as_words(v_woven[1][:])[:, 0, 0:1], gate[:, 0, 0:1]]
        row_sum = new_v[:, 1, 0:QT]
        inv_sum = keep.tile([P, QT], F32, name="inv_sum")
        p_t = [keep.tile([P, PACK, P], F32, name=f"p_t{a}") for a in range(QT)]
        w_woven = [keep.tile([P, P, PACK], BF16, name=f"w_woven{a}", align_bytes=MX_ALIGN) for a in range(QT)]
        w_codes = [keep.tile([P, P], U32, name=f"w_codes{a}", align_bytes=MX_ALIGN) for a in range(QT)]
        w_scales = [keep.tile([P, P], U8, name=f"w_scales{a}", align_bytes=MX_ALIGN) for a in range(QT)]
        result = [keep.tile([P, QT, P], F32, name=f"result{h}") for h in range(ET)]
        identity = keep.tile([P, P], F32, name="identity")
        score_ps = [psum.tile([P, N], F32, name=f"score_ps{a}", tag=f"score_ps{a}") for a in range(QT)]
        p_ps = [psum.tile([P, PACK, P], F32, name=f"p_ps{a}", tag=f"p_ps{a}") for a in range(QT)]
        vs_ps = psum.tile([P, PACK, P], F32, name="vs_ps", tag="vs_ps")

        k_rows = kT.rearrange("(p t) n -> p t n", t=PACK)
        new_k_rows = new_kT.rearrange("(p t) n -> p t n", t=PACK)
        v_rows = vT.rearrange("(h p) n -> p h n", p=P)
        out_rows = out[0].rearrange("(a p) (h e) -> h p a e", p=P, e=P)
        offs_half = [offs_t[:, c * HALF // LIST_ROWS : (c + 1) * HALF // LIST_ROWS] for c in range(2)]

        nc.sync.dma_start(k_plane[0][:], k_rows[:, 0, :])
        nc.scalar.dma_start(new_k_loaded[:], new_k_rows[:, 0, :])
        nc.scalar.dma_start(vs_t[P - 1 : P, :], vs[0:1, :])
        nc.sync.dma_start(offs_t[:], offs)
        nc.sync.dma_start(slots_t[:], slots)
        nc.sync.dma_start(new_k_rest[:], new_k_rows[:, 1:PACK, :])
        nc.vector.memset(vs_t[0 : P - 1, :], 0.0)
        for t in range(1, PACK):
            nc.sync.dma_start(k_plane[t][:], k_rows[:, t, :])
        nc.sync.dma_start(q_planes[:], qT[0].rearrange("(p t) n -> p t n", t=PACK))
        nc.sync.dma_start(new_v[:], new_vT.rearrange("(h p) n -> p h n", p=P))
        for h in (1, 0):
            nc.sync.dma_start(v_tile[h][:], v_rows[:, h, :])
        nc.sync.dma_start(og_t[:], og[0].rearrange("(a p) e -> p a e", p=P))

        make_identity(nc, identity[:])
        nc.scalar.activation(new_k_first[:], new_k_loaded[:], ACT.Copy)

        nc.vector.tensor_copy(vs_row[:], vs_t[:].indirect(offs_t[:]))
        for t in range(PACK):
            nc.tensor.transpose(vs_ps[:, t, :], vs_row[:].rearrange("p (s t) -> p t s", t=PACK)[:, t, :], identity[:])

        for t in range(PACK):
            source = new_k_first[:] if t == 0 else new_k_rest[:, t - 1, :]
            nc.scalar.activation(k_plane[t][:].indirect(slots_t[:]), source, ACT.Copy)
            u, j = divmod(t, PAIR)
            if t < PACK - 1:
                nc.vector.tensor_copy(k_pairs[:, :, u, :, j], k_plane[t][:].indirect(offs_t[:]))
            else:
                for c in range(2):
                    nc.vector.tensor_copy(k_pairs[:, c, u, :, j], k_plane[t][:].indirect(offs_half[c]))
        nc.scalar.activation(q_woven[:].rearrange("p (c i) t -> p c t i", i=LINE), q_planes[:].rearrange("p t (c i) -> p c t i", i=LINE), ACT.Copy)
        quantize(q_codes[:, 0:P], q_scales[:, 0:P], q_woven[:, 0:P, :])
        for c in range(2):
            nc.vector.tensor_copy(as_words(k_woven[c][:]), k_pairs_row[:, c * 2 * N : (c + 1) * 2 * N].bitcast(F32).rearrange("p (u n) -> p n u", u=PACK // PAIR))

        quantize(k_codes[:, 0:HALF], k_scales[0], k_woven[0][:])
        quantize(k_codes[:, HALF:N], k_scales[1], k_woven[1][:])
        quantize(q_codes[:, P:NQ], q_scales[:, P:NQ], q_woven[:, P:NQ, :])
        for a in range(QT):
            rows = slice(a * P, (a + 1) * P)
            for c in range(2):
                cols = slice(c * HALF, (c + 1) * HALF)
                product(score_ps[a][:, cols], q_codes[:, rows], q_scales[:, rows], k_codes[:, cols], k_scales[c])

        v_picked = [keep.tile([P, N], BF16, name="v_picked0", tag="q_codes", align_bytes=MX_ALIGN), v_picked1]
        nc.scalar.activation(v_tile[1][:].indirect(slots_t[:]), new_v[:, 1, :], ACT.Copy)
        nc.scalar.copy(vs_col, vs_ps[:, :, P - 1])

        def weigh(a):
            nc.vector.tensor_tensor(
                w_woven[a][:].rearrange("s (c i) t -> s c t i", i=PAIR),
                p_ps[a][:].rearrange("s t (c i) -> s c t i", i=PAIR),
                vs_col.unsqueeze(1).unsqueeze(3).to_broadcast([P, P // PAIR, PACK, PAIR]),
                ALU.mult,
            )

        nc.scalar.activation(v_picked[1][:, 0:SCALAR_SLOTS], v_tile[1][:].indirect(offs_t[:, 0 : SCALAR_SLOTS // LIST_ROWS]), ACT.Copy)
        nc.vector.tensor_copy(v_picked[1][:, SCALAR_SLOTS:N], v_tile[1][:].indirect(offs_t[:, SCALAR_SLOTS // LIST_ROWS : N // LIST_ROWS]))
        nc.scalar.activation(v_tile[0][:].indirect(slots_t[:]), new_v[:, 0, :], ACT.Copy)
        v_ps = [psum.tile([P, PACK // PAIR, P], F32, name="v_ps0", tag="score_ps1"), psum.tile([P, PACK // PAIR, P], F32, name="v_ps1")]
        for u in range(PACK // PAIR):
            nc.tensor.transpose(v_ps[1][:, u, :], v_picked[1][:].bitcast(F32).rearrange("p (s u) -> p u s", u=PAIR)[:, u, :], identity[:])
        for a in range(QT):
            nc.vector.tensor_reduce(neg_max[a], score_ps[a][:], axis=AXX, op=ALU.max, negate=True)
            nc.scalar.activation(
                p_t[a][:], score_ps[a][:].rearrange("q (s t) -> q t s", t=PACK), ACT.Exp, bias=neg_max[a], scale=1.0, accum_out=row_sum[:, a : a + 1]
            )
            for t in range(PACK):
                nc.tensor.transpose(p_ps[a][:, t, :], p_t[a][:, t, :], identity[:])
        nc.vector.tensor_copy(v_picked[0][:].rearrange("p (u s j) -> p s u j", u=PACK // PAIR, j=PAIR), v_tile[0][:].indirect(offs_t[:]))
        for u in range(PACK // PAIR):
            nc.tensor.transpose(v_ps[0][:, u, :], v_picked[0][:].bitcast(F32)[:, u * P : (u + 1) * P], identity[:])

        nc.scalar.copy(as_words(v_woven[1][:]), v_ps[1][:].rearrange("s u e -> s e u"))
        nc.scalar.activation(tanh_t[:], og_t[:], ACT.Tanh, scale=0.5)
        nc.scalar.copy(as_words(v_woven[0][:]), v_ps[0][:].rearrange("s u e -> s e u"))
        nc.scalar.activation(gate[:], tanh_t[:], ACT.Copy, scale=0.5, bias=0.5)

        weigh(0)
        quantize(v_codes[:, P:DV], v_scales[1][:], v_woven[1][:])
        weigh(1)
        for a in range(QT):
            quantize(w_codes[a][:], w_scales[a][:], w_woven[a][:])
        quantize(v_codes[:, 0:P], v_scales[0][:], v_woven[0][:])
        nc.vector.reciprocal(inv_sum[:], row_sum)

        y_ps = [
            [psum.tile([P, P], F32, name="y_ps00"), psum.tile([P, P], F32, name="y_ps01", tag="vs_ps")],
            [psum.tile([P, P], F32, name="y_ps10"), psum.tile([P, P], F32, name="y_ps11", tag="score_ps0")],
        ]
        for h in (1, 0):
            cols = slice(h * P, (h + 1) * P)
            for a in range(QT):
                product(y_ps[a][h][:], w_codes[a][:], w_scales[a][:], v_codes[:, cols], v_scales[h][:])
        for h in (1, 0):
            cols = slice(h * P, (h + 1) * P)
            for a in range(QT):
                nc.vector.scalar_tensor_tensor(result[h][:, a, :], y_ps[a][h][:], inv_sum[:, a : a + 1], gate[:, a, cols], ALU.mult, ALU.mult)
            nc.sync.dma_start(out_rows[h], result[h][:])
